import numpy as np
import ml_dtypes


def mxq(x, axis, fmt="e4m3"):
    dtype, down = {"e4m3": (ml_dtypes.float8_e4m3fn, 7), "e5m2": (ml_dtypes.float8_e5m2, 14)}[fmt]
    v = np.moveaxis(np.asarray(x, np.float32).astype(ml_dtypes.bfloat16).astype(np.float64), axis, -1)
    blocks = v.reshape(v.shape[:-1] + (-1, 32))
    amax = np.abs(blocks).max(-1, keepdims=True)
    byte = np.maximum(np.where(amax > 0, np.frexp(amax)[1] - 1 + 127, 0) - down, 1)
    scale = np.exp2(byte - 127.0)
    codes = (blocks / scale).astype(np.float32).astype(dtype).astype(np.float64)
    return np.moveaxis((codes * scale).reshape(v.shape), -1, axis)


WIDE = False


def mx_kscale(k):
    if not WIDE:
        return np.ones(k)
    levels = np.array([10, -10, 5, -5, 0])
    if k % 512:
        return np.exp2(np.random.permutation(np.resize(levels, k // 32))).repeat(32)
    a = np.empty((k // 512, 16))
    for p in range(k // 512):
        a[p, :8] = np.random.permutation(np.resize(levels, 8))
        for g in range(8):
            far = levels[np.abs(levels - a[p, g]) >= 10]
            a[p, g + 8] = far[np.random.randint(len(far))]
    return np.exp2(a.ravel()).repeat(32)


def f64(x):
    return np.asarray(x).astype(np.float64)


def striped(idx):
    return np.tile(idx.reshape(-1, 16).T, (8, 1)).astype(np.uint16)


def unstriped(offs):
    return offs[:16].T.reshape(-1).astype(np.int64)


E2M1 = np.array([0.0, 0.5, 1.0, 1.5, 2.0, 3.0, 4.0, 6.0, -0.0, -0.5, -1.0, -1.5, -2.0, -3.0, -4.0, -6.0])


def pack_weight(w, fmt):
    k, n = w.shape
    w = f64(np.asarray(w, np.float32).astype(ml_dtypes.bfloat16)).reshape(k // 32, 32, n)
    amax = np.abs(w).max(1)
    if fmt == "e4m3":
        byte = np.frexp(amax)[1] - 1 + 127 - 7
    else:
        mant, ex = np.frexp(amax / 6.0)
        byte = np.where(mant > 0.5, ex, ex - 1) + 127
    byte = np.clip(np.where(amax > 0, byte, 1), 1, 254)
    scaled = (w * np.exp2(127.0 - byte)[:, None, :]).reshape(k, n).astype(np.float32)
    by_word = np.ascontiguousarray(scaled.reshape(k // 512, 128, 4, n).transpose(0, 1, 3, 2))
    if fmt == "e4m3":
        words = by_word.astype(ml_dtypes.float8_e4m3fn).view(np.uint8)
    else:
        c = by_word.astype(ml_dtypes.float4_e2m1fn).view(np.uint8) & 0xF
        words = (c[..., 0::2] | (c[..., 1::2] << 4)).reshape(k // 512, 128, 2 * n)
    return np.ascontiguousarray(words), np.ascontiguousarray(byte.astype(np.uint8).reshape(k // 512, 16, n))


def unpack_weight(words, scales, fmt):
    g, _, n = scales.shape
    words = np.ascontiguousarray(words).reshape(g, 128, n, -1)
    if fmt == "e4m3":
        vals = words.view(ml_dtypes.float8_e4m3fn).astype(np.float64)
    else:
        nib = np.empty((g, 128, n, 4), np.uint8)
        nib[..., 0::2] = words & 0xF
        nib[..., 1::2] = words >> 4
        vals = E2M1[nib]
    vals = vals * np.repeat(np.exp2(scales.astype(np.float64) - 127.0), 8, axis=1)[..., None]
    return vals.transpose(0, 1, 3, 2).reshape(g * 512, n)


def gelu(v):
    return 0.5 * v * (1.0 + np.tanh(np.sqrt(2.0 / np.pi) * (v + 0.044715 * v**3)))


def bf(x):
    return np.asarray(x, np.float32).astype(ml_dtypes.bfloat16)

def planes(Y):
    n, m = Y.shape
    b = f64(bf(Y)).reshape(n // 32, 32, m)
    amax = np.abs(b).max(1)
    byte = np.clip(np.where(amax > 0, np.frexp(amax)[1] - 1 + 127 - 7, 1), 1, 254)
    codes = (b * np.exp2(127.0 - byte)[:, None, :]).reshape(n, m).astype(np.float32).astype(ml_dtypes.float8_e4m3fn).view(np.uint8)
    words = codes.reshape(n // 512, 128, 4, m).transpose(0, 1, 3, 2)
    return np.ascontiguousarray(words), np.ascontiguousarray(byte.astype(np.uint8).reshape(n // 512, 16, m))


K, H, N, T, S = 512, 1024, 512, 2048, 1024

def setup_inputs():
    n = np.random.standard_normal
    s = mx_kscale(K)[:, None]
    u = mx_kscale(H)[:, None]
    gain = np.exp(0.8 * n(N))
    tab_words, tab_scales = pack_weight(n((K, T)) * s, "e4m3")
    wl_words, wl_scales = pack_weight(n((K, H)) / np.sqrt(K) / s * u.T, "e2m1")
    wr_words, wr_scales = pack_weight(n((K, H)) / np.sqrt(K) / s, "e4m3")
    wp = n((K, H)) / np.sqrt(K) / s * u.T
    w2 = n((H, N)) / np.sqrt(H) / u * gain[None, :]
    b2 = 0.5 * n(N) * gain
    return {
        "tab_words": tab_words, "tab_scales": tab_scales,
        "offs": striped(np.random.permutation(T)[:S]),
        "offs2": striped(np.random.permutation(T)[:S]),
        "offs3": striped(np.random.permutation(T)[:S]),
        "wp": wp.astype(np.float32),
        "wl_words": wl_words, "wl_scales": wl_scales,
        "wr_words": wr_words, "wr_scales": wr_scales,
        "w2": w2.astype(np.float32), "b2": b2.astype(np.float32),
    }

def reference(tab_words, tab_scales, offs, offs2, offs3, wp, wl_words, wl_scales, wr_words, wr_scales, w2, b2):
    vp = unpack_weight(tab_words, tab_scales, "e4m3")[:, unstriped(offs)]
    vl = unpack_weight(tab_words, tab_scales, "e4m3")[:, unstriped(offs2)]
    vr = unpack_weight(tab_words, tab_scales, "e4m3")[:, unstriped(offs3)]
    wl = unpack_weight(wl_words, wl_scales, "e2m1")
    wr = unpack_weight(wr_words, wr_scales, "e4m3")
    p = mxq(f64(wp), 0, "e4m3").T @ vp
    a = wl.T @ vl
    b = wr.T @ vr
    h = np.maximum(a, 0.0) * np.maximum(b, 0.0) + p
    y = (mxq(f64(w2), 0, "e4m3").T @ mxq(h, 0, "e4m3")) + f64(b2)[:, None]
    words, scales = planes(y)
    return y, words, scales

@@ -1,0 +1,224 @@
+from contextlib import ExitStack
+
+import concourse.mybir as mybir
+
+K, H, N, T, S = 512, 1024, 512, 2048, 1024
+FLOPS = 2 * S * (3 * K * H + H * N)
+
+F32 = mybir.dt.float32
+BF16 = mybir.dt.bfloat16
+I32 = mybir.dt.int32
+U32 = mybir.dt.uint32
+U16 = mybir.dt.uint16
+U8 = mybir.dt.uint8
+E4M3 = mybir.dt.float8_e4m3fn_x4
+E2M1 = mybir.dt.float4_e2m1fn_x4
+ALU = mybir.AluOpType
+ACT = mybir.ActivationFunctionType
+
+P = 128
+G = H // 512
+JT = 128
+CH = 256
+
+
+def tile_list_syntax_node_latency_kernel(tc, tab_words, tab_scales, offs, offs2, offs3, wp, wl_words, wl_scales,
+                                                   wr_words, wr_scales, w2, b2, out_0, out_1, out_2):
+    nc = tc.nc
+    with ExitStack() as ctx:
+        keep = ctx.enter_context(tc.tile_pool(name="keep", bufs=1))
+        ring = ctx.enter_context(tc.tile_pool(name="ring", bufs=3))
+        psum = ctx.enter_context(tc.psum_pool(name="psum", bufs=2))
+
+        shared = ctx.enter_context(tc.tile_pool(name="shared", bufs=1))
+        tab_sc = keep.tile([P, T], U8, name="tab_sc", align_bytes=64)
+        w_raw = shared.tile([P, 2304], I32, name="w_raw", align_bytes=64, offset=0)
+        wr_raw = w_raw[:, 0:H]
+        wl_raw = w_raw[:, H:H + H // 2]
+        w_sc_raw = w_raw[:, H + H // 2:2 * H]
+        wl_sc_raw = w_sc_raw[:, 0:H // 4]
+        wr_sc_raw = w_sc_raw[:, H // 4:H // 2]
+        nc.gpsimd.memset(tab_sc[:].bitcast(I32), 0)
+        nc.gpsimd.memset(w_sc_raw, 0)
+
+        list_l = keep.tile([P, S // 16], U16, name="list_l")
+        list_r = keep.tile([P, S // 16], U16, name="list_r")
+        list_p = keep.tile([P, S // 16], U16, name="list_p")
+        nc.sync.dma_start(list_l[:], offs2)
+        nc.sync.dma_start(list_r[:], offs3)
+        nc.sync.dma_start(list_p[:], offs)
+        for q in range(4):
+            nc.sync.dma_start(tab_sc[32 * q:32 * q + 4, :].bitcast(I32), tab_scales[0][4 * q:4 * q + 4, :].bitcast(I32))
+        tab_w = keep.tile([P, T], I32, name="tab_w", align_bytes=64)
+        nc.sync.dma_start(tab_w[:], tab_words[0].rearrange("p n t -> p (n t)").bitcast(I32))
+        nc.sync.dma_start(wl_raw, wl_words[0].bitcast(I32))
+        for q in range(4):
+            nc.sync.dma_start(wl_sc_raw[32 * q:32 * q + 4, :], wl_scales[0][4 * q:4 * q + 4, :].bitcast(I32))
+        nc.sync.dma_start(wr_raw, wr_words[0].rearrange("p n t -> p (n t)").bitcast(I32))
+        wp_raw = []
+        wp_rows = wp.rearrange("(p i) r -> p i r", i=4)
+        for g in range(G):
+            raw = keep.tile([P, 4, 512], F32, name="wp_raw%d" % g)
+            nc.sync.dma_start(raw[:], wp_rows[:, :, 512 * g:512 * g + 512])
+            wp_raw.append(raw)
+            if g == 0:
+                for q in range(4):
+                    nc.sync.dma_start(wr_sc_raw[32 * q:32 * q + 4, :], wr_scales[0][4 * q:4 * q + 4, :].bitcast(I32))
+        bias = keep.tile([P, 4], F32, name="bias")
+        nc.sync.dma_start(bias[:], b2.rearrange("(p t) -> p t", t=4))
+        w2_raw = []
+        w2_rows = w2.rearrange("(g m t e) n -> g e m t n", g=G, t=4, e=4)
+        for g in range(G):
+            raw = keep.tile([P, 4, N], F32, name="w2_raw%d" % g)
+            for e in range(4):
+                nc.sync.dma_start(raw[e:P:4, :, :], w2_rows[g, e])
+            w2_raw.append(raw)
+
+        def gather_scales(got, lst):
+            nc.vector.tensor_copy(got[:], tab_sc[:].indirect(lst[:]))
+
+        def gather_words(got, lst):
+            nc.vector.tensor_copy(got[:], tab_w[:].bitcast(U32).indirect(lst[:]))
+
+        vl_sc = keep.tile([P, S], U8, name="vl_sc", align_bytes=64)
+        vr_sc = keep.tile([P, S], U8, name="vr_sc", align_bytes=64)
+        vl_w = keep.tile([P, S], U32, name="vl_w", align_bytes=64)
+        gather_scales(vl_sc, list_l)
+        gather_words(vl_w, list_l)
+        gather_scales(vr_sc, list_r)
+
+        wl_w = keep.tile([P, H // 2], I32, name="wl_w", align_bytes=64)
+        wr_w = keep.tile([P, H], I32, name="wr_w", align_bytes=64)
+        wl_sc = keep.tile([P, H], U8, name="wl_sc", align_bytes=64)
+        wr_sc = keep.tile([P, H], U8, name="wr_sc", align_bytes=64)
+        nc.vector.tensor_copy(wl_sc[:].bitcast(I32).rearrange("p (g t m) -> p g t m", g=G, t=4),
+                              wl_sc_raw.rearrange("p (g m t) -> p g t m", g=G, t=4))
+        nc.vector.tensor_copy(wl_w[:].rearrange("p (g t m e) -> p g t m e", g=G, t=4, e=2),
+                              wl_raw.rearrange("p (g m t e) -> p g t m e", g=G, t=4, e=2))
+        nc.vector.tensor_copy(wr_w[:].rearrange("p (g t m e) -> p g t m e", g=G, t=4, e=4),
+                              wr_raw.rearrange("p (g m t e) -> p g t m e", g=G, t=4, e=4))
+        nc.vector.tensor_copy(wr_sc[:].bitcast(I32).rearrange("p (g t m) -> p g t m", g=G, t=4),
+                              wr_sc_raw.rearrange("p (g m t) -> p g t m", g=G, t=4))
+
+        vr_w = shared.tile([P, S], U32, name="vr_w", align_bytes=64, offset=0)
+        vp_w = shared.tile([P, S], U32, name="vp_w", align_bytes=64, offset=4096)
+        vp_sc = shared.tile([P, S], U8, name="vp_sc", align_bytes=64, offset=8192)
+        gather_words(vr_w, list_r)
+        units = [(jt, g) for jt in range(S // JT) for g in range(G)]
+
+        wp_bf = []
+        for g in range(G):
+            grouped = keep.tile([P, 2048], BF16, name="wp_bf%d" % g, align_bytes=64)
+            nc.scalar.copy(grouped[:].rearrange("p (t m e i) -> p t m i e", t=4, e=4, i=4),
+                           wp_raw[g][:].rearrange("p i (m t e) -> p t m i e", t=4, e=4))
+            wp_bf.append(grouped)
+
+        relu_a = []
+        for n, (jt, g) in enumerate(units):
+            js = slice(jt * JT, (jt + 1) * JT)
+            bank = psum.tile([P, 4, JT], F32, name="bank", bufs=6)
+            for t in range(4):
+                c0 = 512 * g + P * t
+                nc.tensor.matmul_mx(out=bank[:, t, :], lhsT=wl_w[:].bitcast(U8)[:, 2 * c0:2 * c0 + 2 * P].bitcast(E2M1),
+                                    lhsT_scale=wl_sc[:, c0:c0 + P], rhs=vl_w[:, js].bitcast(E4M3), rhs_scale=vl_sc[:, js],
+                                    start=True, stop=True)
+            act = keep.tile([P, JT, 4], F32, name="relu_a%d" % n)
+            nc.scalar.activation(act[:], bank[:].rearrange("p t j -> p j t"), ACT.Relu)
+            relu_a.append(act)
+
+        gather_scales(vp_sc, list_p)
+        gather_words(vp_w, list_p)
+
+        prods = []
+        for n, (jt, g) in enumerate(units):
+            js = slice(jt * JT, (jt + 1) * JT)
+            bank = psum.tile([P, 4, JT], F32, name="bank", bufs=6)
+            for t in range(4):
+                c0 = 512 * g + P * t
+                nc.tensor.matmul_mx(out=bank[:, t, :], lhsT=wr_w[:, c0:c0 + P].bitcast(E4M3),
+                                    lhsT_scale=wr_sc[:, c0:c0 + P], rhs=vr_w[:, js].bitcast(E4M3), rhs_scale=vr_sc[:, js],
+                                    start=True, stop=True)
+            prod = keep.tile([P, JT, 4], F32, name="prod%d" % n)
+            nc.vector.scalar_tensor_tensor(prod[:], bank[:].rearrange("p t j -> p j t"), 0.0, relu_a[n][:], ALU.max, ALU.mult)
+            prods.append(prod)
+
+        wp_w, wp_sc, w2_w, w2_sc = [], [], [], []
+        for g in range(G):
+            codes = keep.tile([P, 512], U32, name="wp_w%d" % g, align_bytes=64)
+            plane = keep.tile([P, 512], U8, name="wp_sc%d" % g, align_bytes=64)
+            nc.vector.quantize_mx(out=codes[:].bitcast(E4M3), scales=plane[:], in_=wp_bf[g][:])
+            wp_w.append(codes)
+            wp_sc.append(plane)
+
+        for g in range(G):
+            w2_bf = keep.tile([P, 2048], BF16, name="w2_bf%d" % g, align_bytes=64)
+            nc.scalar.copy(w2_bf[:].rearrange("p (u c t) -> p c u t", u=4, t=4),
+                           w2_raw[g][:].rearrange("p t (c u) -> p c u t", u=4))
+            codes = keep.tile([P, N], U32, name="w2_w%d" % g, align_bytes=64)
+            plane = keep.tile([P, N], U8, name="w2_sc%d" % g, align_bytes=64)
+            nc.vector.quantize_mx(out=codes[:].bitcast(E4M3), scales=plane[:], in_=w2_bf[:])
+            w2_w.append(codes)
+            w2_sc.append(plane)
+
+        y_sc = keep.tile([P, S], U8, name="y_sc", align_bytes=64)
+        y_rows = out_0.rearrange("(p t) j -> p t j", t=4)
+        y_words = out_1[0].rearrange("p m t -> p (m t)").bitcast(I32)
+
+        h_bf = {}
+
+        def add_parent(n):
+            jt, g = units[n]
+            js = slice(jt * JT, (jt + 1) * JT)
+            bank = psum.tile([P, 4, JT], F32, name="bank", bufs=6)
+            for t in range(4):
+                nc.tensor.matmul_mx(out=bank[:, t, :], lhsT=wp_w[g][:, P * t:P * t + P].bitcast(E4M3),
+                                    lhsT_scale=wp_sc[g][:, P * t:P * t + P], rhs=vp_w[:, js].bitcast(E4M3),
+                                    rhs_scale=vp_sc[:, js], start=True, stop=True)
+            c, half = divmod(jt, CH // JT)
+            if c not in h_bf:
+                h_bf[c] = ring.tile([P, G, CH, 4], BF16, name="h_bf", align_bytes=64)
+            nc.vector.tensor_tensor(h_bf[c][:, g, half * JT:(half + 1) * JT, :], bank[:].rearrange("p t j -> p j t"), prods[n][:], ALU.add)
+
+        def second_product(c):
+            h_w = ring.tile([P, G, CH], U32, name="h_w", align_bytes=64)
+            h_sc = ring.tile([P, G, CH], U8, name="h_sc", align_bytes=64)
+            nc.vector.quantize_mx(out=h_w[:].rearrange("p g j -> p (g j)").bitcast(E4M3), scales=h_sc[:].rearrange("p g j -> p (g j)"),
+                                  in_=h_bf[c][:].rearrange("p g j t -> p (g j t)"))
+            y = ring.tile([P, 4, CH], F32, name="y")
+            for pair in range(2):
+                bank_y = psum.tile([P, 2, CH], F32, name="bank_y")
+                for u in range(2):
+                    t = 2 * pair + u
+                    for g in range(G):
+                        nc.tensor.matmul_mx(out=bank_y[:, u, :], lhsT=w2_w[g][:, P * t:P * t + P].bitcast(E4M3),
+                                            lhsT_scale=w2_sc[g][:, P * t:P * t + P], rhs=h_w[:, g, :].bitcast(E4M3),
+                                            rhs_scale=h_sc[:, g, :], start=(g == 0), stop=(g == G - 1))
+                for u in range(2):
+                    t = 2 * pair + u
+                    nc.scalar.activation(y[:, t, :], bank_y[:, u, :], ACT.Identity, bias=bias[:, t:t + 1])
+            nc.sync.dma_start(y_rows[:, :, c * CH:(c + 1) * CH], y[:])
+            y_bf = ring.tile([P, CH * 4], BF16, name="y_bf", align_bytes=64)
+            nc.scalar.copy(y_bf[:].rearrange("p (c i t) -> p c t i", i=4, t=4), y[:].rearrange("p t (c i) -> p c t i", i=4))
+            return y_bf
+
+        def planes(c, y_bf):
+            y_w = ring.tile([P, CH], U32, name="y_w", align_bytes=64)
+            nc.vector.quantize_mx(out=y_w[:].bitcast(E4M3), scales=y_sc[:, c * CH:(c + 1) * CH], in_=y_bf[:])
+            nc.sync.dma_start(y_words[:, c * CH:(c + 1) * CH], y_w[:].bitcast(I32))
+
+        per_chunk = G * CH // JT
+        y_ready = {}
+        for n in range(len(units)):
+            add_parent(n)
+            if n % per_chunk == 0 and n >= per_chunk:
+                c = n // per_chunk - 1
+                y_ready[c] = second_product(c)
+            if n % per_chunk == 1 and n > 2 * per_chunk:
+                c = n // per_chunk - 2
+                planes(c, y_ready[c])
+        last = S // CH - 1
+        y_ready[last] = second_product(last)
+        planes(last - 1, y_ready[last - 1])
+        planes(last, y_ready[last])
+        for q in range(4):
+            nc.sync.dma_start(out_2[0][4 * q:4 * q + 4, :].bitcast(I32), y_sc[32 * q:32 * q + 4, :].bitcast(I32))

@@ -19,7 +19,13 @@ ACT = mybir.ActivationFunctionType
 P = 128
 G = H // 512
 JT = 128
-CH = 256
+CHUNKS = [256, 256, 256, 128, 128]
+ON_GPSIMD = [2, 2, 2, 1, 0]
+RELUS_AHEAD = 6
+
+RAW_AT = 0
+LEFT_AT = 8192
+W2_AT = LEFT_AT + 8192
 
 
 def tile_list_syntax_node_latency_kernel(tc, tab_words, tab_scales, offs, offs2, offs3, wp, wl_words, wl_scales,
@@ -27,52 +33,50 @@ def tile_list_syntax_node_latency_kernel(tc, tab_words, tab_scales, offs, offs2,
     nc = tc.nc
     with ExitStack() as ctx:
         keep = ctx.enter_context(tc.tile_pool(name="keep", bufs=1))
+        shared = ctx.enter_context(tc.tile_pool(name="shared", bufs=1))
         ring = ctx.enter_context(tc.tile_pool(name="ring", bufs=3))
         psum = ctx.enter_context(tc.psum_pool(name="psum", bufs=2))
 
-        shared = ctx.enter_context(tc.tile_pool(name="shared", bufs=1))
         tab_sc = keep.tile([P, T], U8, name="tab_sc", align_bytes=64)
-        w_raw = shared.tile([P, 2304], I32, name="w_raw", align_bytes=64, offset=0)
-        wr_raw = w_raw[:, 0:H]
-        wl_raw = w_raw[:, H:H + H // 2]
-        w_sc_raw = w_raw[:, H + H // 2:2 * H]
-        wl_sc_raw = w_sc_raw[:, 0:H // 4]
-        wr_sc_raw = w_sc_raw[:, H // 4:H // 2]
+        left_raw = shared.tile([P, 2048], I32, name="left_raw", align_bytes=64, offset=RAW_AT)
+        wl_raw = left_raw[:, 0:H // 2]
+        wl_sc_raw = left_raw[:, H // 2:H // 2 + H // 4]
+        wr_raw = keep.tile([P, H], I32, name="wr_raw")[:]
+        wr_sc_raw = keep.tile([P, H // 4], I32, name="wr_sc_raw")[:]
         nc.gpsimd.memset(tab_sc[:].bitcast(I32), 0)
-        nc.gpsimd.memset(w_sc_raw, 0)
+        nc.vector.memset(wl_sc_raw, 0)
+        nc.vector.memset(wr_sc_raw, 0)
+
+        def load_scale_rows(plane, rows):
+            for q in range(4):
+                nc.sync.dma_start(plane[32 * q:32 * q + 4, :], rows[4 * q:4 * q + 4, :].bitcast(I32))
 
         list_l = keep.tile([P, S // 16], U16, name="list_l")
         list_r = keep.tile([P, S // 16], U16, name="list_r")
         list_p = keep.tile([P, S // 16], U16, name="list_p")
+        tab_w = keep.tile([P, T], I32, name="tab_w", align_bytes=64)
+        wp_raw = [keep.tile([P, 4, 512], F32, name="wp_raw0"),
+                  shared.tile([P, 4, 512], F32, name="wp_raw1", align_bytes=64, offset=LEFT_AT)]
+        w2_raw = [shared.tile([P, 4, N], F32, name="w2_raw%d" % g, align_bytes=64, offset=W2_AT + 8192 * (1 - g)) for g in range(G)]
+        bias = keep.tile([P, 4], F32, name="bias")
+        wp_rows = wp.rearrange("(p i) (g r) -> g p i r", i=4, g=G)
+        w2_rows = w2.rearrange("(g m t e) n -> g e m t n", g=G, t=4, e=4)
+
         nc.sync.dma_start(list_l[:], offs2)
         nc.sync.dma_start(list_r[:], offs3)
         nc.sync.dma_start(list_p[:], offs)
-        for q in range(4):
-            nc.sync.dma_start(tab_sc[32 * q:32 * q + 4, :].bitcast(I32), tab_scales[0][4 * q:4 * q + 4, :].bitcast(I32))
-        tab_w = keep.tile([P, T], I32, name="tab_w", align_bytes=64)
+        load_scale_rows(tab_sc[:].bitcast(I32), tab_scales[0])
+        nc.sync.dma_start(wp_raw[0][:], wp_rows[0])
+        load_scale_rows(wl_sc_raw, wl_scales[0])
+        nc.sync.dma_start(wp_raw[1][:], wp_rows[1])
         nc.sync.dma_start(tab_w[:], tab_words[0].rearrange("p n t -> p (n t)").bitcast(I32))
         nc.sync.dma_start(wl_raw, wl_words[0].bitcast(I32))
-        for q in range(4):
-            nc.sync.dma_start(wl_sc_raw[32 * q:32 * q + 4, :], wl_scales[0][4 * q:4 * q + 4, :].bitcast(I32))
-        nc.sync.dma_start(wr_raw, wr_words[0].rearrange("p n t -> p (n t)").bitcast(I32))
-        wp_raw = []
-        wp_rows = wp.rearrange("(p i) r -> p i r", i=4)
         for g in range(G):
-            raw = keep.tile([P, 4, 512], F32, name="wp_raw%d" % g)
-            nc.sync.dma_start(raw[:], wp_rows[:, :, 512 * g:512 * g + 512])
-            wp_raw.append(raw)
-            if g == 0:
-                for q in range(4):
-                    nc.sync.dma_start(wr_sc_raw[32 * q:32 * q + 4, :], wr_scales[0][4 * q:4 * q + 4, :].bitcast(I32))
-        bias = keep.tile([P, 4], F32, name="bias")
-        nc.sync.dma_start(bias[:], b2.rearrange("(p t) -> p t", t=4))
-        w2_raw = []
-        w2_rows = w2.rearrange("(g m t e) n -> g e m t n", g=G, t=4, e=4)
-        for g in range(G):
-            raw = keep.tile([P, 4, N], F32, name="w2_raw%d" % g)
             for e in range(4):
-                nc.sync.dma_start(raw[e:P:4, :, :], w2_rows[g, e])
-            w2_raw.append(raw)
+                nc.sync.dma_start(w2_raw[g][e:P:4, :, :], w2_rows[g, e])
+        nc.sync.dma_start(wr_raw, wr_words[0].rearrange("p n t -> p (n t)").bitcast(I32))
+        load_scale_rows(wr_sc_raw, wr_scales[0])
+        nc.sync.dma_start(bias[:], b2.rearrange("(p t) -> p t", t=4))
 
         def gather_scales(got, lst):
             nc.vector.tensor_copy(got[:], tab_sc[:].indirect(lst[:]))
@@ -80,145 +84,175 @@ def tile_list_syntax_node_latency_kernel(tc, tab_words, tab_scales, offs, offs2,
         def gather_words(got, lst):
             nc.vector.tensor_copy(got[:], tab_w[:].bitcast(U32).indirect(lst[:]))
 
+        vl_w = keep.tile([P, S], U32, name="vl_w", align_bytes=64)
         vl_sc = keep.tile([P, S], U8, name="vl_sc", align_bytes=64)
         vr_sc = keep.tile([P, S], U8, name="vr_sc", align_bytes=64)
-        vl_w = keep.tile([P, S], U32, name="vl_w", align_bytes=64)
         gather_scales(vl_sc, list_l)
-        gather_words(vl_w, list_l)
         gather_scales(vr_sc, list_r)
+        vp_sc = keep.tile([P, S], U8, name="vp_sc", align_bytes=64)
+        gather_scales(vp_sc, list_p)
+        gather_words(vl_w, list_l)
 
         wl_w = keep.tile([P, H // 2], I32, name="wl_w", align_bytes=64)
-        wr_w = keep.tile([P, H], I32, name="wr_w", align_bytes=64)
-        wl_sc = keep.tile([P, H], U8, name="wl_sc", align_bytes=64)
         wr_sc = keep.tile([P, H], U8, name="wr_sc", align_bytes=64)
-        nc.vector.tensor_copy(wl_sc[:].bitcast(I32).rearrange("p (g t m) -> p g t m", g=G, t=4),
-                              wl_sc_raw.rearrange("p (g m t) -> p g t m", g=G, t=4))
-        nc.vector.tensor_copy(wl_w[:].rearrange("p (g t m e) -> p g t m e", g=G, t=4, e=2),
-                              wl_raw.rearrange("p (g m t e) -> p g t m e", g=G, t=4, e=2))
-        nc.vector.tensor_copy(wr_w[:].rearrange("p (g t m e) -> p g t m e", g=G, t=4, e=4),
-                              wr_raw.rearrange("p (g m t e) -> p g t m e", g=G, t=4, e=4))
-        nc.vector.tensor_copy(wr_sc[:].bitcast(I32).rearrange("p (g t m) -> p g t m", g=G, t=4),
-                              wr_sc_raw.rearrange("p (g m t) -> p g t m", g=G, t=4))
+        wl_sc = keep.tile([P, H], U8, name="wl_sc", align_bytes=64)
 
-        vr_w = shared.tile([P, S], U32, name="vr_w", align_bytes=64, offset=0)
-        vp_w = shared.tile([P, S], U32, name="vp_w", align_bytes=64, offset=4096)
-        vp_sc = shared.tile([P, S], U8, name="vp_sc", align_bytes=64, offset=8192)
+        def deal(dealt, raw, run):
+            nc.vector.tensor_copy(dealt.rearrange("p (g t m e) -> p g t m e", g=G, t=4, e=run),
+                                  raw.rearrange("p (g m t e) -> p g t m e", g=G, t=4, e=run))
+
+        deal(wl_sc[:].bitcast(I32), wl_sc_raw, 1)
+        deal(wl_w[:], wl_raw, 2)
+
+        vr_w = shared.tile([P, S], U32, name="vr_w", align_bytes=64, offset=RAW_AT)
+        vp_w = shared.tile([P, S], U32, name="vp_w", align_bytes=64, offset=RAW_AT + 4 * S)
         gather_words(vr_w, list_r)
-        units = [(jt, g) for jt in range(S // JT) for g in range(G)]
+        gather_words(vp_w, list_p)
+        wr_w = keep.tile([P, H], I32, name="wr_w", align_bytes=64)
+        deal(wr_w[:], wr_raw, 4)
+        deal(wr_sc[:].bitcast(I32), wr_sc_raw, 1)
 
-        wp_bf = []
+        def quantize(grouped, name):
+            codes = keep.tile([P, 512], U32, name=name + "_w", align_bytes=64)
+            plane = keep.tile([P, 512], U8, name=name + "_sc", align_bytes=64)
+            nc.vector.quantize_mx(out=codes[:].bitcast(E4M3), scales=plane[:], in_=grouped[:])
+            return codes, plane
+
+        wp_q = []
         for g in range(G):
             grouped = keep.tile([P, 2048], BF16, name="wp_bf%d" % g, align_bytes=64)
             nc.scalar.copy(grouped[:].rearrange("p (t m e i) -> p t m i e", t=4, e=4, i=4),
                            wp_raw[g][:].rearrange("p i (m t e) -> p t m i e", t=4, e=4))
-            wp_bf.append(grouped)
+            wp_q.append(quantize(grouped, "wp%d" % g))
+
+        units = [(jt, g) for jt in range(S // JT) for g in range(G)]
+
+        banks = [psum.tile([P, 4, JT], F32, name="bank%d" % b, bufs=1) for b in range(6)]
+        turns = []
+
+        def first_product(unit, weights, words, plane):
+            jt, g = unit
+            js = slice(jt * JT, (jt + 1) * JT)
+            bank = banks[len(turns) % len(banks)]
+            turns.append(unit)
+            for t in range(4):
+                w_codes, w_plane = weights(g, t)
+                nc.tensor.matmul_mx(out=bank[:, t, :], lhsT=w_codes, lhsT_scale=w_plane, rhs=words[:, js].bitcast(E4M3),
+                                    rhs_scale=plane[:, js], start=True, stop=True)
+            return bank[:].rearrange("p t j -> p j t")
+
+        def left(g, t):
+            c = 512 * g + P * t
+            return wl_w[:, c // 2:(c + P) // 2].bitcast(U8).bitcast(E2M1), wl_sc[:, c:c + P]
+
+        def right(g, t):
+            c = 512 * g + P * t
+            return wr_w[:, c:c + P].bitcast(E4M3), wr_sc[:, c:c + P]
+
+        def parent(g, t):
+            codes, plane = wp_q[g]
+            return codes[:, P * t:P * t + P].bitcast(E4M3), plane[:, P * t:P * t + P]
 
         relu_a = []
-        for n, (jt, g) in enumerate(units):
-            js = slice(jt * JT, (jt + 1) * JT)
-            bank = psum.tile([P, 4, JT], F32, name="bank", bufs=6)
-            for t in range(4):
-                c0 = 512 * g + P * t
-                nc.tensor.matmul_mx(out=bank[:, t, :], lhsT=wl_w[:].bitcast(U8)[:, 2 * c0:2 * c0 + 2 * P].bitcast(E2M1),
-                                    lhsT_scale=wl_sc[:, c0:c0 + P], rhs=vl_w[:, js].bitcast(E4M3), rhs_scale=vl_sc[:, js],
-                                    start=True, stop=True)
-            act = keep.tile([P, JT, 4], F32, name="relu_a%d" % n)
-            nc.scalar.activation(act[:], bank[:].rearrange("p t j -> p j t"), ACT.Relu)
+
+        def rectified_left():
+            n = len(relu_a)
+            slot = n % 8
+            act = shared.tile([P, JT, 4], F32, name="relu_a%d" % n, align_bytes=64, offset=W2_AT + 2048 * slot)
+            nc.scalar.activation(act[:], first_product(units[n], left, vl_w, vl_sc), ACT.Relu)
             relu_a.append(act)
 
-        gather_scales(vp_sc, list_p)
-        gather_words(vp_w, list_p)
-
-        prods = []
-        for n, (jt, g) in enumerate(units):
-            js = slice(jt * JT, (jt + 1) * JT)
-            bank = psum.tile([P, 4, JT], F32, name="bank", bufs=6)
-            for t in range(4):
-                c0 = 512 * g + P * t
-                nc.tensor.matmul_mx(out=bank[:, t, :], lhsT=wr_w[:, c0:c0 + P].bitcast(E4M3),
-                                    lhsT_scale=wr_sc[:, c0:c0 + P], rhs=vr_w[:, js].bitcast(E4M3), rhs_scale=vr_sc[:, js],
-                                    start=True, stop=True)
-            prod = keep.tile([P, JT, 4], F32, name="prod%d" % n)
-            nc.vector.scalar_tensor_tensor(prod[:], bank[:].rearrange("p t j -> p j t"), 0.0, relu_a[n][:], ALU.max, ALU.mult)
-            prods.append(prod)
-
-        wp_w, wp_sc, w2_w, w2_sc = [], [], [], []
+        w2_q = []
         for g in range(G):
-            codes = keep.tile([P, 512], U32, name="wp_w%d" % g, align_bytes=64)
-            plane = keep.tile([P, 512], U8, name="wp_sc%d" % g, align_bytes=64)
-            nc.vector.quantize_mx(out=codes[:].bitcast(E4M3), scales=plane[:], in_=wp_bf[g][:])
-            wp_w.append(codes)
-            wp_sc.append(plane)
-
-        for g in range(G):
-            w2_bf = keep.tile([P, 2048], BF16, name="w2_bf%d" % g, align_bytes=64)
-            nc.scalar.copy(w2_bf[:].rearrange("p (u c t) -> p c u t", u=4, t=4),
+            grouped = shared.tile([P, 2048], BF16, name="w2_bf%d" % g, align_bytes=64, offset=LEFT_AT + 4096 * g)
+            nc.scalar.copy(grouped[:].rearrange("p (u c t) -> p c u t", u=4, t=4),
                            w2_raw[g][:].rearrange("p t (c u) -> p c u t", u=4))
-            codes = keep.tile([P, N], U32, name="w2_w%d" % g, align_bytes=64)
-            plane = keep.tile([P, N], U8, name="w2_sc%d" % g, align_bytes=64)
-            nc.vector.quantize_mx(out=codes[:].bitcast(E4M3), scales=plane[:], in_=w2_bf[:])
-            w2_w.append(codes)
-            w2_sc.append(plane)
+            w2_q.append(quantize(grouped, "w2%d" % g))
+        for n in range(RELUS_AHEAD):
+            rectified_left()
 
         y_sc = keep.tile([P, S], U8, name="y_sc", align_bytes=64)
         y_rows = out_0.rearrange("(p t) j -> p t j", t=4)
         y_words = out_1[0].rearrange("p m t -> p (m t)").bitcast(I32)
 
-        h_bf = {}
+        def product(n):
+            prod = ring.tile([P, JT, 4], F32, name="prod", bufs=5)
+            nc.vector.scalar_tensor_tensor(prod[:], first_product(units[n], right, vr_w, vr_sc), 0.0, relu_a[n][:], ALU.max, ALU.mult)
+            return prod
 
-        def add_parent(n):
-            jt, g = units[n]
-            js = slice(jt * JT, (jt + 1) * JT)
-            bank = psum.tile([P, 4, JT], F32, name="bank", bufs=6)
-            for t in range(4):
-                nc.tensor.matmul_mx(out=bank[:, t, :], lhsT=wp_w[g][:, P * t:P * t + P].bitcast(E4M3),
-                                    lhsT_scale=wp_sc[g][:, P * t:P * t + P], rhs=vp_w[:, js].bitcast(E4M3),
-                                    rhs_scale=vp_sc[:, js], start=True, stop=True)
-            c, half = divmod(jt, CH // JT)
-            if c not in h_bf:
-                h_bf[c] = ring.tile([P, G, CH, 4], BF16, name="h_bf", align_bytes=64)
-            nc.vector.tensor_tensor(h_bf[c][:, g, half * JT:(half + 1) * JT, :], bank[:].rearrange("p t j -> p j t"), prods[n][:], ALU.add)
+        def add_parent(n, prod, h_part, on_gpsimd):
+            p_bank = first_product(units[n], parent, vp_w, vp_sc)
+            if on_gpsimd:
+                p_sb = ring.tile([P, JT, 4], F32, name="p_sb")
+                nc.scalar.copy(p_sb[:], p_bank)
+                nc.gpsimd.tensor_tensor(h_part, p_sb[:], prod[:], ALU.add)
+            else:
+                nc.vector.tensor_tensor(h_part, p_bank, prod[:], ALU.add)
 
-        def second_product(c):
-            h_w = ring.tile([P, G, CH], U32, name="h_w", align_bytes=64)
-            h_sc = ring.tile([P, G, CH], U8, name="h_sc", align_bytes=64)
+        def second_product(j0, width, h_bf, at_end):
+            h_w = ring.tile([P, G, width], U32, name="h_w", align_bytes=64)
+            h_sc = ring.tile([P, G, width], U8, name="h_sc", align_bytes=64)
             nc.vector.quantize_mx(out=h_w[:].rearrange("p g j -> p (g j)").bitcast(E4M3), scales=h_sc[:].rearrange("p g j -> p (g j)"),
-                                  in_=h_bf[c][:].rearrange("p g j t -> p (g j t)"))
-            y = ring.tile([P, 4, CH], F32, name="y")
+                                  in_=h_bf[:].rearrange("p g j t -> p (g j t)"))
+            y = ring.tile([P, 4, width], F32, name="y")
             for pair in range(2):
-                bank_y = psum.tile([P, 2, CH], F32, name="bank_y")
+                bank_y = psum.tile([P, 2, width], F32, name="bank_y")
                 for u in range(2):
                     t = 2 * pair + u
                     for g in range(G):
-                        nc.tensor.matmul_mx(out=bank_y[:, u, :], lhsT=w2_w[g][:, P * t:P * t + P].bitcast(E4M3),
-                                            lhsT_scale=w2_sc[g][:, P * t:P * t + P], rhs=h_w[:, g, :].bitcast(E4M3),
+                        codes, plane = w2_q[g]
+                        nc.tensor.matmul_mx(out=bank_y[:, u, :], lhsT=codes[:, P * t:P * t + P].bitcast(E4M3),
+                                            lhsT_scale=plane[:, P * t:P * t + P], rhs=h_w[:, g, :].bitcast(E4M3),
                                             rhs_scale=h_sc[:, g, :], start=(g == 0), stop=(g == G - 1))
                 for u in range(2):
                     t = 2 * pair + u
-                    nc.scalar.activation(y[:, t, :], bank_y[:, u, :], ACT.Identity, bias=bias[:, t:t + 1])
-            nc.sync.dma_start(y_rows[:, :, c * CH:(c + 1) * CH], y[:])
-            y_bf = ring.tile([P, CH * 4], BF16, name="y_bf", align_bytes=64)
-            nc.scalar.copy(y_bf[:].rearrange("p (c i t) -> p c t i", i=4, t=4), y[:].rearrange("p t (c i) -> p c t i", i=4))
+                    if at_end and pair == 1:
+                        nc.vector.tensor_scalar(y[:, t, :], bank_y[:, u, :], bias[:, t:t + 1], None, ALU.add)
+                    else:
+                        nc.scalar.activation(y[:, t, :], bank_y[:, u, :], ACT.Identity, bias=bias[:, t:t + 1])
+            nc.sync.dma_start(y_rows[:, :, j0:j0 + width], y[:])
+            y_bf = ring.tile([P, width * 4], BF16, name="y_bf", align_bytes=64)
+            grouped = y_bf[:].rearrange("p (c i t) -> p c t i", i=4, t=4)
+            rows = y[:].rearrange("p t (c i) -> p c t i", i=4)
+            if at_end:
+                nc.vector.tensor_copy(grouped, rows)
+            else:
+                nc.scalar.copy(grouped, rows)
             return y_bf
 
-        def planes(c, y_bf):
-            y_w = ring.tile([P, CH], U32, name="y_w", align_bytes=64)
-            nc.vector.quantize_mx(out=y_w[:].bitcast(E4M3), scales=y_sc[:, c * CH:(c + 1) * CH], in_=y_bf[:])
-            nc.sync.dma_start(y_words[:, c * CH:(c + 1) * CH], y_w[:].bitcast(I32))
+        def planes(j0, width, y_bf):
+            y_w = ring.tile([P, width], U32, name="y_w", align_bytes=64)
+            nc.vector.quantize_mx(out=y_w[:].bitcast(E4M3), scales=y_sc[:, j0:j0 + width], in_=y_bf[:])
+            nc.sync.dma_start(y_words[:, j0:j0 + width], y_w[:].bitcast(I32))
 
-        per_chunk = G * CH // JT
-        y_ready = {}
-        for n in range(len(units)):
-            add_parent(n)
-            if n % per_chunk == 0 and n >= per_chunk:
-                c = n // per_chunk - 1
-                y_ready[c] = second_product(c)
-            if n % per_chunk == 1 and n > 2 * per_chunk:
-                c = n // per_chunk - 2
-                planes(c, y_ready[c])
-        last = S // CH - 1
-        y_ready[last] = second_product(last)
-        planes(last - 1, y_ready[last - 1])
-        planes(last, y_ready[last])
+        later = []
+        n = 0
+        j0 = 0
+        prod = product(0)
+        for c, width in enumerate(CHUNKS):
+            h_bf = ring.tile([P, G, width, 4], BF16, name="h_bf", align_bytes=64)
+            steps, later = later, []
+            for k in range(G * width // JT):
+                half, g = divmod(k, G)
+                following = product(n + 1) if n + 1 < len(units) else None
+                add_parent(n, prod, h_bf[:, g, half * JT:(half + 1) * JT, :], k < ON_GPSIMD[c])
+                if len(relu_a) < len(units):
+                    rectified_left()
+                prod = following
+                n = n + 1
+                if k == 0:
+                    for kind, args in steps:
+                        if kind == "second":
+                            later.append(("planes", args[:2] + (second_product(*args),)))
+                if k == 1:
+                    for kind, args in steps:
+                        if kind == "planes":
+                            planes(*args)
+            later.append(("second", (j0, width, h_bf, c == len(CHUNKS) - 1)))
+            j0 = j0 + width
+        ready, last = later[0][1], later[1][1]
+        y_last = second_product(*last)
+        planes(*ready)
+        planes(last[0], last[1], y_last)
         for q in range(4):
             nc.sync.dma_start(out_2[0][4 * q:4 * q + 4, :].bitcast(I32), y_sc[32 * q:32 * q + 4, :].bitcast(I32))

@@ -21,11 +21,13 @@ G = H // 512
 JT = 128
 CHUNKS = [256, 256, 256, 128, 128]
 ON_GPSIMD = [2, 2, 2, 1, 0]
-RELUS_AHEAD = 6
-
-RAW_AT = 0
-LEFT_AT = 8192
-W2_AT = LEFT_AT + 8192
+RELUS_FIRST = 9
+RELUS_BY_CHUNK = [11, 14, 16, 16, 16, 16]
+W2_AT = 25088
+P_SB_AT = [12288, 14336, 0, 2048]
+PROD_AT = [4096, 6144, 0, 2048, 41472, 43520]
+FIRST = 256
+LAST = 640
 
 
 def tile_list_syntax_node_latency_kernel(tc, tab_words, tab_scales, offs, offs2, offs3, wp, wl_words, wl_scales,
@@ -38,14 +40,14 @@ def tile_list_syntax_node_latency_kernel(tc, tab_words, tab_scales, offs, offs2,
         psum = ctx.enter_context(tc.psum_pool(name="psum", bufs=2))
 
         tab_sc = keep.tile([P, T], U8, name="tab_sc", align_bytes=64)
-        left_raw = shared.tile([P, 2048], I32, name="left_raw", align_bytes=64, offset=RAW_AT)
+        left_raw = shared.tile([P, 6272], I32, name="left_raw", align_bytes=64, offset=0)
         wl_raw = left_raw[:, 0:H // 2]
         wl_sc_raw = left_raw[:, H // 2:H // 2 + H // 4]
         wr_raw = keep.tile([P, H], I32, name="wr_raw")[:]
         wr_sc_raw = keep.tile([P, H // 4], I32, name="wr_sc_raw")[:]
         nc.gpsimd.memset(tab_sc[:].bitcast(I32), 0)
-        nc.vector.memset(wl_sc_raw, 0)
-        nc.vector.memset(wr_sc_raw, 0)
+        nc.gpsimd.memset(wl_sc_raw, 0)
+        nc.gpsimd.memset(wr_sc_raw, 0)
 
         def load_scale_rows(plane, rows):
             for q in range(4):
@@ -55,9 +57,8 @@ def tile_list_syntax_node_latency_kernel(tc, tab_words, tab_scales, offs, offs2,
         list_r = keep.tile([P, S // 16], U16, name="list_r")
         list_p = keep.tile([P, S // 16], U16, name="list_p")
         tab_w = keep.tile([P, T], I32, name="tab_w", align_bytes=64)
-        wp_raw = [keep.tile([P, 4, 512], F32, name="wp_raw0"),
-                  shared.tile([P, 4, 512], F32, name="wp_raw1", align_bytes=64, offset=LEFT_AT)]
-        w2_raw = [shared.tile([P, 4, N], F32, name="w2_raw%d" % g, align_bytes=64, offset=W2_AT + 8192 * (1 - g)) for g in range(G)]
+        wp_raw = [keep.tile([P, 4, 512], F32, name="wp_raw%d" % g) for g in range(G)]
+        w2_raw = [shared.tile([P, 4, N], F32, name="w2_raw%d" % g, align_bytes=64, offset=W2_AT + 8192 * g) for g in range(G)]
         bias = keep.tile([P, 4], F32, name="bias")
         wp_rows = wp.rearrange("(p i) (g r) -> g p i r", i=4, g=G)
         w2_rows = w2.rearrange("(g m t e) n -> g e m t n", g=G, t=4, e=4)
@@ -66,51 +67,49 @@ def tile_list_syntax_node_latency_kernel(tc, tab_words, tab_scales, offs, offs2,
         nc.sync.dma_start(list_r[:], offs3)
         nc.sync.dma_start(list_p[:], offs)
         load_scale_rows(tab_sc[:].bitcast(I32), tab_scales[0])
-        nc.sync.dma_start(wp_raw[0][:], wp_rows[0])
-        load_scale_rows(wl_sc_raw, wl_scales[0])
-        nc.sync.dma_start(wp_raw[1][:], wp_rows[1])
         nc.sync.dma_start(tab_w[:], tab_words[0].rearrange("p n t -> p (n t)").bitcast(I32))
         nc.sync.dma_start(wl_raw, wl_words[0].bitcast(I32))
+        load_scale_rows(wl_sc_raw, wl_scales[0])
+        nc.sync.dma_start(wr_raw, wr_words[0].rearrange("p n t -> p (n t)").bitcast(I32))
+        load_scale_rows(wr_sc_raw, wr_scales[0])
+        nc.sync.dma_start(wp_raw[0][:], wp_rows[0])
+        nc.sync.dma_start(wp_raw[1][:], wp_rows[1])
         for g in range(G):
             for e in range(4):
                 nc.sync.dma_start(w2_raw[g][e:P:4, :, :], w2_rows[g, e])
-        nc.sync.dma_start(wr_raw, wr_words[0].rearrange("p n t -> p (n t)").bitcast(I32))
-        load_scale_rows(wr_sc_raw, wr_scales[0])
         nc.sync.dma_start(bias[:], b2.rearrange("(p t) -> p t", t=4))
 
         def gather_scales(got, lst):
-            nc.vector.tensor_copy(got[:], tab_sc[:].indirect(lst[:]))
+            nc.vector.tensor_copy(got[:], tab_sc[:].indirect(lst))
 
         def gather_words(got, lst):
-            nc.vector.tensor_copy(got[:], tab_w[:].bitcast(U32).indirect(lst[:]))
-
-        vl_w = keep.tile([P, S], U32, name="vl_w", align_bytes=64)
-        vl_sc = keep.tile([P, S], U8, name="vl_sc", align_bytes=64)
-        vr_sc = keep.tile([P, S], U8, name="vr_sc", align_bytes=64)
-        gather_scales(vl_sc, list_l)
-        gather_scales(vr_sc, list_r)
-        vp_sc = keep.tile([P, S], U8, name="vp_sc", align_bytes=64)
-        gather_scales(vp_sc, list_p)
-        gather_words(vl_w, list_l)
-
-        wl_w = keep.tile([P, H // 2], I32, name="wl_w", align_bytes=64)
-        wr_sc = keep.tile([P, H], U8, name="wr_sc", align_bytes=64)
-        wl_sc = keep.tile([P, H], U8, name="wl_sc", align_bytes=64)
+            nc.vector.tensor_copy(got[:], tab_w[:].bitcast(U32).indirect(lst))
 
         def deal(dealt, raw, run):
             nc.vector.tensor_copy(dealt.rearrange("p (g t m e) -> p g t m e", g=G, t=4, e=run),
                                   raw.rearrange("p (g m t e) -> p g t m e", g=G, t=4, e=run))
 
-        deal(wl_sc[:].bitcast(I32), wl_sc_raw, 1)
+        vl_sc = keep.tile([P, S], U8, name="vl_sc", align_bytes=64)
+        vl_first = keep.tile([P, FIRST], U32, name="vl_first", align_bytes=64)
+        wl_w = keep.tile([P, H // 2], I32, name="wl_w", align_bytes=64)
+        wl_sc = keep.tile([P, H], U8, name="wl_sc", align_bytes=64)
+        gather_scales(vl_sc, list_l[:])
+        gather_words(vl_first, list_l[:, 0:FIRST // 16])
         deal(wl_w[:], wl_raw, 2)
+        deal(wl_sc[:].bitcast(I32), wl_sc_raw, 1)
 
-        vr_w = shared.tile([P, S], U32, name="vr_w", align_bytes=64, offset=RAW_AT)
-        vp_w = shared.tile([P, S], U32, name="vp_w", align_bytes=64, offset=RAW_AT + 4 * S)
-        gather_words(vr_w, list_r)
-        gather_words(vp_w, list_p)
-        wr_w = keep.tile([P, H], I32, name="wr_w", align_bytes=64)
-        deal(wr_w[:], wr_raw, 4)
-        deal(wr_sc[:].bitcast(I32), wr_sc_raw, 1)
+        vl_mid = shared.tile([P, LAST - FIRST], U32, name="vl_mid", align_bytes=64, offset=3584)
+        vl_last = shared.tile([P, S - LAST], U32, name="vl_last", align_bytes=64, offset=8192)
+        vr_sc = shared.tile([P, S], U8, name="vr_sc", align_bytes=64, offset=9728)
+        vp_sc = shared.tile([P, S], U8, name="vp_sc", align_bytes=64, offset=10752)
+        vr_w = shared.tile([P, S], U32, name="vr_w", align_bytes=64, offset=11776)
+        vp_w = shared.tile([P, S], U32, name="vp_w", align_bytes=64, offset=15872)
+        gather_words(vl_mid, list_l[:, FIRST // 16:LAST // 16])
+        gather_words(vl_last, list_l[:, LAST // 16:S // 16])
+        gather_scales(vr_sc, list_r[:])
+        gather_words(vr_w, list_r[:])
+        gather_scales(vp_sc, list_p[:])
+        gather_words(vp_w, list_p[:])
 
         def quantize(grouped, name):
             codes = keep.tile([P, 512], U32, name=name + "_w", align_bytes=64)
@@ -121,24 +120,30 @@ def tile_list_syntax_node_latency_kernel(tc, tab_words, tab_scales, offs, offs2,
         wp_q = []
         for g in range(G):
             grouped = keep.tile([P, 2048], BF16, name="wp_bf%d" % g, align_bytes=64)
-            nc.scalar.copy(grouped[:].rearrange("p (t m e i) -> p t m i e", t=4, e=4, i=4),
-                           wp_raw[g][:].rearrange("p i (m t e) -> p t m i e", t=4, e=4))
+            for t in range(4):
+                nc.gpsimd.tensor_scalar(grouped[:].rearrange("p (t m e i) -> p t m e i", t=4, e=4, i=4)[:, t],
+                                        wp_raw[g][:].rearrange("p i (m t e) -> p t m e i", t=4, e=4)[:, t],
+                                        1.0, 0.0, ALU.mult, ALU.add)
             wp_q.append(quantize(grouped, "wp%d" % g))
 
-        units = [(jt, g) for jt in range(S // JT) for g in range(G)]
+        wr_w = shared.tile([P, H], I32, name="wr_w", align_bytes=64, offset=19968)
+        wr_sc = shared.tile([P, H], U8, name="wr_sc", align_bytes=64, offset=24064)
+        deal(wr_w[:], wr_raw, 4)
+        deal(wr_sc[:].bitcast(I32), wr_sc_raw, 1)
 
+        units = [(jt, g) for jt in range(S // JT) for g in range(G)]
         banks = [psum.tile([P, 4, JT], F32, name="bank%d" % b, bufs=1) for b in range(6)]
         turns = []
 
-        def first_product(unit, weights, words, plane):
-            jt, g = unit
-            js = slice(jt * JT, (jt + 1) * JT)
+        def first_product(n, weights, moving):
+            jt, g = units[n]
+            words, plane = moving(jt * JT)
             bank = banks[len(turns) % len(banks)]
-            turns.append(unit)
+            turns.append(n)
             for t in range(4):
                 w_codes, w_plane = weights(g, t)
-                nc.tensor.matmul_mx(out=bank[:, t, :], lhsT=w_codes, lhsT_scale=w_plane, rhs=words[:, js].bitcast(E4M3),
-                                    rhs_scale=plane[:, js], start=True, stop=True)
+                nc.tensor.matmul_mx(out=bank[:, t, :], lhsT=w_codes, lhsT_scale=w_plane, rhs=words.bitcast(E4M3),
+                                    rhs_scale=plane, start=True, stop=True)
             return bank[:].rearrange("p t j -> p j t")
 
         def left(g, t):
@@ -153,22 +158,37 @@ def tile_list_syntax_node_latency_kernel(tc, tab_words, tab_scales, offs, offs2,
             codes, plane = wp_q[g]
             return codes[:, P * t:P * t + P].bitcast(E4M3), plane[:, P * t:P * t + P]
 
+        def left_children(j):
+            words, at = (vl_first, 0) if j < FIRST else (vl_mid, FIRST) if j < LAST else (vl_last, LAST)
+            return words[:, j - at:j - at + JT], vl_sc[:, j:j + JT]
+
+        def right_children(j):
+            return vr_w[:, j:j + JT], vr_sc[:, j:j + JT]
+
+        def parents(j):
+            return vp_w[:, j:j + JT], vp_sc[:, j:j + JT]
+
         relu_a = []
 
         def rectified_left():
             n = len(relu_a)
-            slot = n % 8
-            act = shared.tile([P, JT, 4], F32, name="relu_a%d" % n, align_bytes=64, offset=W2_AT + 2048 * slot)
-            nc.scalar.activation(act[:], first_product(units[n], left, vl_w, vl_sc), ACT.Relu)
+            if n < RELUS_FIRST or n >= RELUS_FIRST + 2:
+                act = keep.tile([P, JT, 4], F32, name="relu_a%d" % n)
+            else:
+                act = shared.tile([P, JT, 4], F32, name="relu_a%d" % n, align_bytes=64, offset=W2_AT + 8192 + 2048 * (n - RELUS_FIRST))
+            nc.scalar.activation(act[:], first_product(n, left, left_children), ACT.Relu)
             relu_a.append(act)
+
+        for n in range(RELUS_FIRST):
+            rectified_left()
 
         w2_q = []
         for g in range(G):
-            grouped = shared.tile([P, 2048], BF16, name="w2_bf%d" % g, align_bytes=64, offset=LEFT_AT + 4096 * g)
+            grouped = shared.tile([P, 2048], BF16, name="w2_bf%d" % g, align_bytes=64, offset=4096 * g)
             nc.scalar.copy(grouped[:].rearrange("p (u c t) -> p c u t", u=4, t=4),
                            w2_raw[g][:].rearrange("p t (c u) -> p c u t", u=4))
             w2_q.append(quantize(grouped, "w2%d" % g))
-        for n in range(RELUS_AHEAD):
+        while len(relu_a) < RELUS_BY_CHUNK[0]:
             rectified_left()
 
         y_sc = keep.tile([P, S], U8, name="y_sc", align_bytes=64)
@@ -176,18 +196,9 @@ def tile_list_syntax_node_latency_kernel(tc, tab_words, tab_scales, offs, offs2,
         y_words = out_1[0].rearrange("p m t -> p (m t)").bitcast(I32)
 
         def product(n):
-            prod = ring.tile([P, JT, 4], F32, name="prod", bufs=5)
-            nc.vector.scalar_tensor_tensor(prod[:], first_product(units[n], right, vr_w, vr_sc), 0.0, relu_a[n][:], ALU.max, ALU.mult)
+            prod = shared.tile([P, JT, 4], F32, name="prod%d" % n, align_bytes=64, offset=PROD_AT[n % len(PROD_AT)])
+            nc.vector.scalar_tensor_tensor(prod[:], first_product(n, right, right_children), 0.0, relu_a[n][:], ALU.max, ALU.mult)
             return prod
-
-        def add_parent(n, prod, h_part, on_gpsimd):
-            p_bank = first_product(units[n], parent, vp_w, vp_sc)
-            if on_gpsimd:
-                p_sb = ring.tile([P, JT, 4], F32, name="p_sb")
-                nc.scalar.copy(p_sb[:], p_bank)
-                nc.gpsimd.tensor_tensor(h_part, p_sb[:], prod[:], ALU.add)
-            else:
-                nc.vector.tensor_tensor(h_part, p_bank, prod[:], ALU.add)
 
         def second_product(j0, width, h_bf, at_end):
             h_w = ring.tile([P, G, width], U32, name="h_w", align_bytes=64)
@@ -225,34 +236,31 @@ def tile_list_syntax_node_latency_kernel(tc, tab_words, tab_scales, offs, offs2,
             nc.vector.quantize_mx(out=y_w[:].bitcast(E4M3), scales=y_sc[:, j0:j0 + width], in_=y_bf[:])
             nc.sync.dma_start(y_words[:, j0:j0 + width], y_w[:].bitcast(I32))
 
-        later = []
-        n = 0
+        waiting = []
+        copied = []
+        n0 = 0
         j0 = 0
-        prod = product(0)
         for c, width in enumerate(CHUNKS):
             h_bf = ring.tile([P, G, width, 4], BF16, name="h_bf", align_bytes=64)
-            steps, later = later, []
-            for k in range(G * width // JT):
-                half, g = divmod(k, G)
-                following = product(n + 1) if n + 1 < len(units) else None
-                add_parent(n, prod, h_bf[:, g, half * JT:(half + 1) * JT, :], k < ON_GPSIMD[c])
-                if len(relu_a) < len(units):
-                    rectified_left()
-                prod = following
-                n = n + 1
-                if k == 0:
-                    for kind, args in steps:
-                        if kind == "second":
-                            later.append(("planes", args[:2] + (second_product(*args),)))
-                if k == 1:
-                    for kind, args in steps:
-                        if kind == "planes":
-                            planes(*args)
-            later.append(("second", (j0, width, h_bf, c == len(CHUNKS) - 1)))
+            count = G * width // JT
+            h_part = [h_bf[:, k % G, (k // G) * JT:(k // G + 1) * JT, :] for k in range(count)]
+            for k in range(ON_GPSIMD[c]):
+                prod = product(n0 + k)
+                p_sb = shared.tile([P, JT, 4], F32, name="p_sb%d" % (n0 + k), align_bytes=64, offset=W2_AT + P_SB_AT[len(copied) % len(P_SB_AT)])
+                copied.append(n0 + k)
+                nc.scalar.copy(p_sb[:], first_product(n0 + k, parent, parents))
+                nc.gpsimd.tensor_tensor(h_part[k], p_sb[:], prod[:], ALU.add)
+            while len(relu_a) < RELUS_BY_CHUNK[c + 1]:
+                rectified_left()
+            prods = {k: product(n0 + k) for k in range(ON_GPSIMD[c], count)}
+            for k in range(ON_GPSIMD[c], count):
+                nc.vector.tensor_tensor(h_part[k], first_product(n0 + k, parent, parents), prods[k][:], ALU.add)
+            if len(waiting) == 2:
+                planes(*waiting.pop(0))
+            waiting.append((j0, width, second_product(j0, width, h_bf, c == len(CHUNKS) - 1)))
+            n0 = n0 + count
             j0 = j0 + width
-        ready, last = later[0][1], later[1][1]
-        y_last = second_product(*last)
-        planes(*ready)
-        planes(last[0], last[1], y_last)
+        for args in waiting:
+            planes(*args)
         for q in range(4):
             nc.sync.dma_start(out_2[0][4 * q:4 * q + 4, :].bitcast(I32), y_sc[32 * q:32 * q + 4, :].bitcast(I32))

@@ -20,7 +20,7 @@ P = 128
 G = H // 512
 JT = 128
 CHUNKS = [256, 256, 256, 128, 128]
-ON_GPSIMD = [2, 2, 2, 1, 0]
+ON_GPSIMD = [2, 2, 2, 1, 1]
 RELUS_FIRST = 9
 RELUS_BY_CHUNK = [11, 14, 16, 16, 16, 16]
 W2_AT = 25088
@@ -61,7 +61,7 @@ def tile_list_syntax_node_latency_kernel(tc, tab_words, tab_scales, offs, offs2,
         w2_raw = [shared.tile([P, 4, N], F32, name="w2_raw%d" % g, align_bytes=64, offset=W2_AT + 8192 * g) for g in range(G)]
         bias = keep.tile([P, 4], F32, name="bias")
         wp_rows = wp.rearrange("(p i) (g r) -> g p i r", i=4, g=G)
-        w2_rows = w2.rearrange("(g m t e) n -> g e m t n", g=G, t=4, e=4)
+        w2_rows = w2.rearrange("(g m t e) n -> g t m (e n)", g=G, t=4, e=4)
 
         nc.sync.dma_start(list_l[:], offs2)
         nc.sync.dma_start(list_r[:], offs3)
@@ -70,13 +70,13 @@ def tile_list_syntax_node_latency_kernel(tc, tab_words, tab_scales, offs, offs2,
         nc.sync.dma_start(tab_w[:], tab_words[0].rearrange("p n t -> p (n t)").bitcast(I32))
         nc.sync.dma_start(wl_raw, wl_words[0].bitcast(I32))
         load_scale_rows(wl_sc_raw, wl_scales[0])
-        nc.sync.dma_start(wr_raw, wr_words[0].rearrange("p n t -> p (n t)").bitcast(I32))
-        load_scale_rows(wr_sc_raw, wr_scales[0])
         nc.sync.dma_start(wp_raw[0][:], wp_rows[0])
         nc.sync.dma_start(wp_raw[1][:], wp_rows[1])
+        nc.sync.dma_start(wr_raw, wr_words[0].rearrange("p n t -> p (n t)").bitcast(I32))
+        load_scale_rows(wr_sc_raw, wr_scales[0])
         for g in range(G):
-            for e in range(4):
-                nc.sync.dma_start(w2_raw[g][e:P:4, :, :], w2_rows[g, e])
+            for t in range(4):
+                nc.sync.dma_start(w2_raw[g][:, t, :], w2_rows[g, t])
         nc.sync.dma_start(bias[:], b2.rearrange("(p t) -> p t", t=4))
 
         def gather_scales(got, lst):
@@ -89,6 +89,10 @@ def tile_list_syntax_node_latency_kernel(tc, tab_words, tab_scales, offs, offs2,
             nc.vector.tensor_copy(dealt.rearrange("p (g t m e) -> p g t m e", g=G, t=4, e=run),
                                   raw.rearrange("p (g m t e) -> p g t m e", g=G, t=4, e=run))
 
+        def deal_scales(dealt, raw):
+            nc.vector.tensor_copy(dealt.rearrange("p (g t c i) -> p g c t i", g=G, t=4, i=4),
+                                  raw.rearrange("p (g c i t) -> p g c t i", g=G, t=4, i=4))
+
         vl_sc = keep.tile([P, S], U8, name="vl_sc", align_bytes=64)
         vl_first = keep.tile([P, FIRST], U32, name="vl_first", align_bytes=64)
         wl_w = keep.tile([P, H // 2], I32, name="wl_w", align_bytes=64)
@@ -96,7 +100,7 @@ def tile_list_syntax_node_latency_kernel(tc, tab_words, tab_scales, offs, offs2,
         gather_scales(vl_sc, list_l[:])
         gather_words(vl_first, list_l[:, 0:FIRST // 16])
         deal(wl_w[:], wl_raw, 2)
-        deal(wl_sc[:].bitcast(I32), wl_sc_raw, 1)
+        deal_scales(wl_sc[:].bitcast(I32), wl_sc_raw)
 
         vl_mid = shared.tile([P, LAST - FIRST], U32, name="vl_mid", align_bytes=64, offset=3584)
         vl_last = shared.tile([P, S - LAST], U32, name="vl_last", align_bytes=64, offset=8192)
@@ -110,6 +114,11 @@ def tile_list_syntax_node_latency_kernel(tc, tab_words, tab_scales, offs, offs2,
         gather_words(vr_w, list_r[:])
         gather_scales(vp_sc, list_p[:])
         gather_words(vp_w, list_p[:])
+
+        wr_w = shared.tile([P, H], I32, name="wr_w", align_bytes=64, offset=19968)
+        wr_sc = shared.tile([P, H], U8, name="wr_sc", align_bytes=64, offset=24064)
+        deal(wr_w[:], wr_raw, 4)
+        deal_scales(wr_sc[:].bitcast(I32), wr_sc_raw)
 
         def quantize(grouped, name):
             codes = keep.tile([P, 512], U32, name=name + "_w", align_bytes=64)
@@ -125,11 +134,6 @@ def tile_list_syntax_node_latency_kernel(tc, tab_words, tab_scales, offs, offs2,
                                         wp_raw[g][:].rearrange("p i (m t e) -> p t m e i", t=4, e=4)[:, t],
                                         1.0, 0.0, ALU.mult, ALU.add)
             wp_q.append(quantize(grouped, "wp%d" % g))
-
-        wr_w = shared.tile([P, H], I32, name="wr_w", align_bytes=64, offset=19968)
-        wr_sc = shared.tile([P, H], U8, name="wr_sc", align_bytes=64, offset=24064)
-        deal(wr_w[:], wr_raw, 4)
-        deal(wr_sc[:].bitcast(I32), wr_sc_raw, 1)
 
         units = [(jt, g) for jt in range(S // JT) for g in range(G)]
         banks = [psum.tile([P, 4, JT], F32, name="bank%d" % b, bufs=1) for b in range(6)]
@@ -206,29 +210,29 @@ def tile_list_syntax_node_latency_kernel(tc, tab_words, tab_scales, offs, offs2,
             nc.vector.quantize_mx(out=h_w[:].rearrange("p g j -> p (g j)").bitcast(E4M3), scales=h_sc[:].rearrange("p g j -> p (g j)"),
                                   in_=h_bf[:].rearrange("p g j t -> p (g j t)"))
             y = ring.tile([P, 4, width], F32, name="y")
-            for pair in range(2):
-                bank_y = psum.tile([P, 2, width], F32, name="bank_y")
-                for u in range(2):
-                    t = 2 * pair + u
-                    for g in range(G):
-                        codes, plane = w2_q[g]
-                        nc.tensor.matmul_mx(out=bank_y[:, u, :], lhsT=codes[:, P * t:P * t + P].bitcast(E4M3),
-                                            lhsT_scale=plane[:, P * t:P * t + P], rhs=h_w[:, g, :].bitcast(E4M3),
-                                            rhs_scale=h_sc[:, g, :], start=(g == 0), stop=(g == G - 1))
-                for u in range(2):
-                    t = 2 * pair + u
-                    if at_end and pair == 1:
-                        nc.vector.tensor_scalar(y[:, t, :], bank_y[:, u, :], bias[:, t:t + 1], None, ALU.add)
-                    else:
-                        nc.scalar.activation(y[:, t, :], bank_y[:, u, :], ACT.Identity, bias=bias[:, t:t + 1])
-            nc.sync.dma_start(y_rows[:, :, j0:j0 + width], y[:])
-            y_bf = ring.tile([P, width * 4], BF16, name="y_bf", align_bytes=64)
-            grouped = y_bf[:].rearrange("p (c i t) -> p c t i", i=4, t=4)
-            rows = y[:].rearrange("p t (c i) -> p c t i", i=4)
             if at_end:
-                nc.vector.tensor_copy(grouped, rows)
+                pairs = [banks[(len(turns) + pair) % len(banks)] for pair in range(2)]
             else:
-                nc.scalar.copy(grouped, rows)
+                pairs = [psum.tile([P, 2, width], F32, name="bank_y") for pair in range(2)]
+            for t in range(4):
+                for g in range(G):
+                    codes, plane = w2_q[g]
+                    nc.tensor.matmul_mx(out=pairs[t // 2][:, t % 2, :], lhsT=codes[:, P * t:P * t + P].bitcast(E4M3),
+                                        lhsT_scale=plane[:, P * t:P * t + P], rhs=h_w[:, g, :].bitcast(E4M3),
+                                        rhs_scale=h_sc[:, g, :], start=(g == 0), stop=(g == G - 1))
+            return y, pairs
+
+        def add_bias(j0, width, y, pairs, on_vector):
+            for t in range(4):
+                if t in on_vector:
+                    nc.vector.tensor_scalar(y[:, t, :], pairs[t // 2][:, t % 2, :], bias[:, t:t + 1], None, ALU.add)
+                else:
+                    nc.scalar.activation(y[:, t, :], pairs[t // 2][:, t % 2, :], ACT.Identity, bias=bias[:, t:t + 1])
+            nc.sync.dma_start(y_rows[:, :, j0:j0 + width], y[:])
+
+        def cast_y(width, y, copy):
+            y_bf = ring.tile([P, width * 4], BF16, name="y_bf", align_bytes=64)
+            copy(y_bf[:].rearrange("p (c i t) -> p c t i", i=4, t=4), y[:].rearrange("p t (c i) -> p c t i", i=4))
             return y_bf
 
         def planes(j0, width, y_bf):
@@ -255,12 +259,22 @@ def tile_list_syntax_node_latency_kernel(tc, tab_words, tab_scales, offs, offs2,
             prods = {k: product(n0 + k) for k in range(ON_GPSIMD[c], count)}
             for k in range(ON_GPSIMD[c], count):
                 nc.vector.tensor_tensor(h_part[k], first_product(n0 + k, parent, parents), prods[k][:], ALU.add)
-            if len(waiting) == 2:
+            last = c == len(CHUNKS) - 1
+            if c >= 2 and not last:
                 planes(*waiting.pop(0))
-            waiting.append((j0, width, second_product(j0, width, h_bf, c == len(CHUNKS) - 1)))
+            y, pairs = second_product(j0, width, h_bf, last)
+            if c < len(CHUNKS) - 2:
+                add_bias(j0, width, y, pairs, ())
+                waiting.append((j0, width, cast_y(width, y, nc.scalar.copy)))
+            elif not last:
+                add_bias(j0, width, y, pairs, ())
+                before = (j0, width, y)
             n0 = n0 + count
             j0 = j0 + width
-        for args in waiting:
-            planes(*args)
+        planes(*waiting.pop(0))
+        before_bf = cast_y(before[1], before[2], nc.vector.tensor_copy)
+        add_bias(S - width, width, y, pairs, (2, 3))
+        planes(before[0], before[1], before_bf)
+        planes(S - width, width, cast_y(width, y, nc.vector.tensor_copy))
         for q in range(4):
             nc.sync.dma_start(out_2[0][4 * q:4 * q + 4, :].bitcast(I32), y_sc[32 * q:32 * q + 4, :].bitcast(I32))

@@ -20,14 +20,15 @@ P = 128
 G = H // 512
 JT = 128
 CHUNKS = [256, 256, 256, 128, 128]
-ON_GPSIMD = [2, 2, 2, 1, 1]
-RELUS_FIRST = 9
-RELUS_BY_CHUNK = [11, 14, 16, 16, 16, 16]
+ON_GPSIMD = [2, 2, 2, 1, 0]
+RELUS_FIRST = 12
+RELUS_BY_CHUNK = [15, 16, 16, 16, 16]
 W2_AT = 25088
 P_SB_AT = [12288, 14336, 0, 2048]
-PROD_AT = [4096, 6144, 0, 2048, 41472, 43520]
+PROD_AT = [4096, 6144, W2_AT + 8192, W2_AT + 10240, 0, 2048]
+WR_AT = W2_AT + 16384
 FIRST = 256
-LAST = 640
+LAST = 768
 
 
 def tile_list_syntax_node_latency_kernel(tc, tab_words, tab_scales, offs, offs2, offs3, wp, wl_words, wl_scales,
@@ -43,8 +44,9 @@ def tile_list_syntax_node_latency_kernel(tc, tab_words, tab_scales, offs, offs2,
         left_raw = shared.tile([P, 6272], I32, name="left_raw", align_bytes=64, offset=0)
         wl_raw = left_raw[:, 0:H // 2]
         wl_sc_raw = left_raw[:, H // 2:H // 2 + H // 4]
-        wr_raw = keep.tile([P, H], I32, name="wr_raw")[:]
-        wr_sc_raw = keep.tile([P, H // 4], I32, name="wr_sc_raw")[:]
+        right_raw = shared.tile([P, H + H // 4], I32, name="right_raw", align_bytes=64, offset=WR_AT)
+        wr_raw = right_raw[:, 0:H]
+        wr_sc_raw = right_raw[:, H:H + H // 4]
         nc.gpsimd.memset(tab_sc[:].bitcast(I32), 0)
         nc.gpsimd.memset(wl_sc_raw, 0)
         nc.gpsimd.memset(wr_sc_raw, 0)
@@ -64,9 +66,9 @@ def tile_list_syntax_node_latency_kernel(tc, tab_words, tab_scales, offs, offs2,
         w2_rows = w2.rearrange("(g m t e) n -> g t m (e n)", g=G, t=4, e=4)
 
         nc.sync.dma_start(list_l[:], offs2)
+        load_scale_rows(tab_sc[:].bitcast(I32), tab_scales[0])
         nc.sync.dma_start(list_r[:], offs3)
         nc.sync.dma_start(list_p[:], offs)
-        load_scale_rows(tab_sc[:].bitcast(I32), tab_scales[0])
         nc.sync.dma_start(tab_w[:], tab_words[0].rearrange("p n t -> p (n t)").bitcast(I32))
         nc.sync.dma_start(wl_raw, wl_words[0].bitcast(I32))
         load_scale_rows(wl_sc_raw, wl_scales[0])
@@ -102,38 +104,40 @@ def tile_list_syntax_node_latency_kernel(tc, tab_words, tab_scales, offs, offs2,
         deal(wl_w[:], wl_raw, 2)
         deal_scales(wl_sc[:].bitcast(I32), wl_sc_raw)
 
-        vl_mid = shared.tile([P, LAST - FIRST], U32, name="vl_mid", align_bytes=64, offset=3584)
+        vl_mid = shared.tile([P, LAST - FIRST], U32, name="vl_mid", align_bytes=64, offset=3072)
         vl_last = shared.tile([P, S - LAST], U32, name="vl_last", align_bytes=64, offset=8192)
         vr_sc = shared.tile([P, S], U8, name="vr_sc", align_bytes=64, offset=9728)
         vp_sc = shared.tile([P, S], U8, name="vp_sc", align_bytes=64, offset=10752)
         vr_w = shared.tile([P, S], U32, name="vr_w", align_bytes=64, offset=11776)
-        vp_w = shared.tile([P, S], U32, name="vp_w", align_bytes=64, offset=15872)
+        vp_w = shared.tile([P, S], U32, name="vp_w", align_bytes=64, offset=WR_AT)
         gather_words(vl_mid, list_l[:, FIRST // 16:LAST // 16])
         gather_words(vl_last, list_l[:, LAST // 16:S // 16])
         gather_scales(vr_sc, list_r[:])
         gather_words(vr_w, list_r[:])
         gather_scales(vp_sc, list_p[:])
-        gather_words(vp_w, list_p[:])
-
         wr_w = shared.tile([P, H], I32, name="wr_w", align_bytes=64, offset=19968)
         wr_sc = shared.tile([P, H], U8, name="wr_sc", align_bytes=64, offset=24064)
         deal(wr_w[:], wr_raw, 4)
         deal_scales(wr_sc[:].bitcast(I32), wr_sc_raw)
+        gather_words(vp_w, list_p[:])
 
-        def quantize(grouped, name):
-            codes = keep.tile([P, 512], U32, name=name + "_w", align_bytes=64)
-            plane = keep.tile([P, 512], U8, name=name + "_sc", align_bytes=64)
+
+        def quantize(grouped, name, passes, plane_at=None):
+            codes = keep.tile([P, passes * 512], U32, name=name + "_w", align_bytes=64)
+            if plane_at is None:
+                plane = keep.tile([P, passes * 512], U8, name=name + "_sc", align_bytes=64)
+            else:
+                plane = shared.tile([P, passes * 512], U8, name=name + "_sc", align_bytes=64, offset=plane_at)
             nc.vector.quantize_mx(out=codes[:].bitcast(E4M3), scales=plane[:], in_=grouped[:])
-            return codes, plane
+            return [(codes[:, 512 * g:512 * g + 512], plane[:, 512 * g:512 * g + 512]) for g in range(passes)]
 
-        wp_q = []
+        wp_bf = keep.tile([P, G * 2048], BF16, name="wp_bf", align_bytes=64)
         for g in range(G):
-            grouped = keep.tile([P, 2048], BF16, name="wp_bf%d" % g, align_bytes=64)
             for t in range(4):
-                nc.gpsimd.tensor_scalar(grouped[:].rearrange("p (t m e i) -> p t m e i", t=4, e=4, i=4)[:, t],
+                nc.gpsimd.tensor_scalar(wp_bf[:].rearrange("p (g t m e i) -> p g t m e i", g=G, t=4, e=4, i=4)[:, g, t],
                                         wp_raw[g][:].rearrange("p i (m t e) -> p t m e i", t=4, e=4)[:, t],
                                         1.0, 0.0, ALU.mult, ALU.add)
-            wp_q.append(quantize(grouped, "wp%d" % g))
+        wp_q = quantize(wp_bf, "wp", G, WR_AT + 4 * S)
 
         units = [(jt, g) for jt in range(S // JT) for g in range(G)]
         banks = [psum.tile([P, 4, JT], F32, name="bank%d" % b, bufs=1) for b in range(6)]
@@ -176,10 +180,7 @@ def tile_list_syntax_node_latency_kernel(tc, tab_words, tab_scales, offs, offs2,
 
         def rectified_left():
             n = len(relu_a)
-            if n < RELUS_FIRST or n >= RELUS_FIRST + 2:
-                act = keep.tile([P, JT, 4], F32, name="relu_a%d" % n)
-            else:
-                act = shared.tile([P, JT, 4], F32, name="relu_a%d" % n, align_bytes=64, offset=W2_AT + 8192 + 2048 * (n - RELUS_FIRST))
+            act = keep.tile([P, JT, 4], F32, name="relu_a%d" % n)
             nc.scalar.activation(act[:], first_product(n, left, left_children), ACT.Relu)
             relu_a.append(act)
 
@@ -188,12 +189,9 @@ def tile_list_syntax_node_latency_kernel(tc, tab_words, tab_scales, offs, offs2,
 
         w2_q = []
         for g in range(G):
-            grouped = shared.tile([P, 2048], BF16, name="w2_bf%d" % g, align_bytes=64, offset=4096 * g)
-            nc.scalar.copy(grouped[:].rearrange("p (u c t) -> p c u t", u=4, t=4),
-                           w2_raw[g][:].rearrange("p t (c u) -> p c u t", u=4))
-            w2_q.append(quantize(grouped, "w2%d" % g))
-        while len(relu_a) < RELUS_BY_CHUNK[0]:
-            rectified_left()
+            w2_bf = shared.tile([P, 2048], BF16, name="w2_bf%d" % g, align_bytes=64, offset=4096 * g)
+            nc.scalar.copy(w2_bf[:].rearrange("p (u c t) -> p c u t", u=4, t=4), w2_raw[g][:].rearrange("p t (c u) -> p c u t", u=4))
+            w2_q.extend(quantize(w2_bf, "w2%d" % g, 1))
 
         y_sc = keep.tile([P, S], U8, name="y_sc", align_bytes=64)
         y_rows = out_0.rearrange("(p t) j -> p t j", t=4)
@@ -240,28 +238,39 @@ def tile_list_syntax_node_latency_kernel(tc, tab_words, tab_scales, offs, offs2,
             nc.vector.quantize_mx(out=y_w[:].bitcast(E4M3), scales=y_sc[:, j0:j0 + width], in_=y_bf[:])
             nc.sync.dma_start(y_words[:, j0:j0 + width], y_w[:].bitcast(I32))
 
+        copied = {}
+        prods = {}
+
+        def copy_parents(n0, count):
+            for n in range(n0, n0 + count):
+                p_sb = shared.tile([P, JT, 4], F32, name="p_sb%d" % n, align_bytes=64, offset=W2_AT + P_SB_AT[len(copied) % len(P_SB_AT)])
+                nc.scalar.copy(p_sb[:], first_product(n, parent, parents))
+                copied[n] = p_sb
+
+        copy_parents(0, ON_GPSIMD[0])
         waiting = []
-        copied = []
         n0 = 0
         j0 = 0
         for c, width in enumerate(CHUNKS):
             h_bf = ring.tile([P, G, width, 4], BF16, name="h_bf", align_bytes=64)
             count = G * width // JT
             h_part = [h_bf[:, k % G, (k // G) * JT:(k // G + 1) * JT, :] for k in range(count)]
-            for k in range(ON_GPSIMD[c]):
-                prod = product(n0 + k)
-                p_sb = shared.tile([P, JT, 4], F32, name="p_sb%d" % (n0 + k), align_bytes=64, offset=W2_AT + P_SB_AT[len(copied) % len(P_SB_AT)])
-                copied.append(n0 + k)
-                nc.scalar.copy(p_sb[:], first_product(n0 + k, parent, parents))
-                nc.gpsimd.tensor_tensor(h_part[k], p_sb[:], prod[:], ALU.add)
-            while len(relu_a) < RELUS_BY_CHUNK[c + 1]:
-                rectified_left()
-            prods = {k: product(n0 + k) for k in range(ON_GPSIMD[c], count)}
-            for k in range(ON_GPSIMD[c], count):
-                nc.vector.tensor_tensor(h_part[k], first_product(n0 + k, parent, parents), prods[k][:], ALU.add)
+            for n in range(n0, n0 + count):
+                if n not in prods:
+                    prods[n] = product(n)
+            for k in range(count):
+                if k < ON_GPSIMD[c]:
+                    nc.gpsimd.tensor_tensor(h_part[k], copied[n0 + k][:], prods[n0 + k][:], ALU.add)
+                else:
+                    nc.vector.tensor_tensor(h_part[k], first_product(n0 + k, parent, parents), prods[n0 + k][:], ALU.add)
             last = c == len(CHUNKS) - 1
             if c >= 2 and not last:
                 planes(*waiting.pop(0))
+            if not last:
+                copy_parents(n0 + count, ON_GPSIMD[c + 1])
+                prods[n0 + count] = product(n0 + count)
+            while len(relu_a) < RELUS_BY_CHUNK[c]:
+                rectified_left()
             y, pairs = second_product(j0, width, h_bf, last)
             if c < len(CHUNKS) - 2:
                 add_bias(j0, width, y, pairs, ())
@@ -277,4 +286,5 @@ def tile_list_syntax_node_latency_kernel(tc, tab_words, tab_scales, offs, offs2,
         planes(before[0], before[1], before_bf)
         planes(S - width, width, cast_y(width, y, nc.vector.tensor_copy))
         for q in range(4):
-            nc.sync.dma_start(out_2[0][4 * q:4 * q + 4, :].bitcast(I32), y_sc[32 * q:32 * q + 4, :].bitcast(I32))
+            queue = nc.sync if q < 2 else nc.scalar
+            queue.dma_start(out_2[0][4 * q:4 * q + 4, :].bitcast(I32), y_sc[32 * q:32 * q + 4, :].bitcast(I32))

@@ -66,9 +66,9 @@ def tile_list_syntax_node_latency_kernel(tc, tab_words, tab_scales, offs, offs2,
         w2_rows = w2.rearrange("(g m t e) n -> g t m (e n)", g=G, t=4, e=4)
 
         nc.sync.dma_start(list_l[:], offs2)
-        load_scale_rows(tab_sc[:].bitcast(I32), tab_scales[0])
         nc.sync.dma_start(list_r[:], offs3)
         nc.sync.dma_start(list_p[:], offs)
+        load_scale_rows(tab_sc[:].bitcast(I32), tab_scales[0])
         nc.sync.dma_start(tab_w[:], tab_words[0].rearrange("p n t -> p (n t)").bitcast(I32))
         nc.sync.dma_start(wl_raw, wl_words[0].bitcast(I32))
         load_scale_rows(wl_sc_raw, wl_scales[0])
@@ -109,17 +109,17 @@ def tile_list_syntax_node_latency_kernel(tc, tab_words, tab_scales, offs, offs2,
         vr_sc = shared.tile([P, S], U8, name="vr_sc", align_bytes=64, offset=9728)
         vp_sc = shared.tile([P, S], U8, name="vp_sc", align_bytes=64, offset=10752)
         vr_w = shared.tile([P, S], U32, name="vr_w", align_bytes=64, offset=11776)
-        vp_w = shared.tile([P, S], U32, name="vp_w", align_bytes=64, offset=WR_AT)
+        vp_w = shared.tile([P, S], U32, name="vp_w", align_bytes=64, offset=15872)
         gather_words(vl_mid, list_l[:, FIRST // 16:LAST // 16])
         gather_words(vl_last, list_l[:, LAST // 16:S // 16])
         gather_scales(vr_sc, list_r[:])
         gather_words(vr_w, list_r[:])
         gather_scales(vp_sc, list_p[:])
+        gather_words(vp_w, list_p[:])
         wr_w = shared.tile([P, H], I32, name="wr_w", align_bytes=64, offset=19968)
         wr_sc = shared.tile([P, H], U8, name="wr_sc", align_bytes=64, offset=24064)
         deal(wr_w[:], wr_raw, 4)
         deal_scales(wr_sc[:].bitcast(I32), wr_sc_raw)
-        gather_words(vp_w, list_p[:])
 
 
         def quantize(grouped, name, passes, plane_at=None):
@@ -252,7 +252,8 @@ def tile_list_syntax_node_latency_kernel(tc, tab_words, tab_scales, offs, offs2,
         n0 = 0
         j0 = 0
         for c, width in enumerate(CHUNKS):
-            h_bf = ring.tile([P, G, width, 4], BF16, name="h_bf", align_bytes=64)
+            h_bf = shared.tile([P, G, width, 4], BF16, name="h_bf%d" % c, align_bytes=64,
+                               offset=WR_AT + 5120 + (2048 if c == len(CHUNKS) - 1 else 0))
             count = G * width // JT
             h_part = [h_bf[:, k % G, (k // G) * JT:(k // G + 1) * JT, :] for k in range(count)]
             for n in range(n0, n0 + count):
@@ -264,14 +265,14 @@ def tile_list_syntax_node_latency_kernel(tc, tab_words, tab_scales, offs, offs2,
                 else:
                     nc.vector.tensor_tensor(h_part[k], first_product(n0 + k, parent, parents), prods[n0 + k][:], ALU.add)
             last = c == len(CHUNKS) - 1
-            if c >= 2 and not last:
-                planes(*waiting.pop(0))
             if not last:
                 copy_parents(n0 + count, ON_GPSIMD[c + 1])
                 prods[n0 + count] = product(n0 + count)
             while len(relu_a) < RELUS_BY_CHUNK[c]:
                 rectified_left()
             y, pairs = second_product(j0, width, h_bf, last)
+            if c >= 2 and not last:
+                planes(*waiting.pop(0))
             if c < len(CHUNKS) - 2:
                 add_bias(j0, width, y, pairs, ())
                 waiting.append((j0, width, cast_y(width, y, nc.scalar.copy)))
@@ -286,5 +287,4 @@ def tile_list_syntax_node_latency_kernel(tc, tab_words, tab_scales, offs, offs2,
         planes(before[0], before[1], before_bf)
         planes(S - width, width, cast_y(width, y, nc.vector.tensor_copy))
         for q in range(4):
-            queue = nc.sync if q < 2 else nc.scalar
-            queue.dma_start(out_2[0][4 * q:4 * q + 4, :].bitcast(I32), y_sc[32 * q:32 * q + 4, :].bitcast(I32))
+            nc.sync.dma_start(out_2[0][4 * q:4 * q + 4, :].bitcast(I32), y_sc[32 * q:32 * q + 4, :].bitcast(I32))

@@ -19,16 +19,21 @@ ACT = mybir.ActivationFunctionType
 P = 128
 G = H // 512
 JT = 128
-CHUNKS = [256, 256, 256, 128, 128]
-ON_GPSIMD = [2, 2, 2, 1, 0]
-RELUS_FIRST = 12
-RELUS_BY_CHUNK = [15, 16, 16, 16, 16]
-W2_AT = 25088
-P_SB_AT = [12288, 14336, 0, 2048]
-PROD_AT = [4096, 6144, W2_AT + 8192, W2_AT + 10240, 0, 2048]
-WR_AT = W2_AT + 16384
-FIRST = 256
-LAST = 768
+KB = 1024
+EARLY_RELUS = 10
+LEFT_AT = 0
+WP_AT = [6 * KB, 24 * KB]
+WP_BF_AT = [14 * KB, 16 * KB]
+RIGHT_AT = 18 * KB
+H_AT = 16 * KB
+W2_AT = [64 * KB, 72 * KB]
+PROD_AT = {3: (30 * KB, 8), 7: (88 * KB, 2), 8: (90 * KB, 2), 9: (110 * KB, 3), 10: (92 * KB, 2),
+           11: (104 * KB, 2), 12: (40 * KB, 3), 14: (120 * KB, 2), 15: (122 * KB, 2)}
+P_SB_AT = {0: 64 * KB, 2: 66 * KB, 1: 68 * KB, 3: 72 * KB, 4: 74 * KB, 6: 76 * KB, 5: 78 * KB}
+Y_W_AT = {0: 112 * KB + 512, 256: 42 * KB + 512}
+Y_BF_AT = {0: (116 * KB, 8)}
+RELU_AT = {4: (48 * KB, 2), 8: (46 * KB, 2), 10: (80 * KB, 2), 12: (113 * KB, 3), 14: (43 * KB, 2)}
+H_W_AT = {256: 46 * KB, 512: 113 * KB + 512, 768: 43 * KB + 512}
 
 
 def tile_list_syntax_node_latency_kernel(tc, tab_words, tab_scales, offs, offs2, offs3, wp, wl_words, wl_scales,
@@ -40,11 +45,16 @@ def tile_list_syntax_node_latency_kernel(tc, tab_words, tab_scales, offs, offs2,
         ring = ctx.enter_context(tc.tile_pool(name="ring", bufs=3))
         psum = ctx.enter_context(tc.psum_pool(name="psum", bufs=2))
 
+        def placed(shape, dtype, name, at):
+            if at is None:
+                return keep.tile(shape, dtype, name=name, align_bytes=64)
+            return shared.tile(shape, dtype, name=name, align_bytes=64, offset=at)
+
         tab_sc = keep.tile([P, T], U8, name="tab_sc", align_bytes=64)
-        left_raw = shared.tile([P, 6272], I32, name="left_raw", align_bytes=64, offset=0)
+        left_raw = placed([P, 1536], I32, "left_raw", LEFT_AT)
         wl_raw = left_raw[:, 0:H // 2]
         wl_sc_raw = left_raw[:, H // 2:H // 2 + H // 4]
-        right_raw = shared.tile([P, H + H // 4], I32, name="right_raw", align_bytes=64, offset=WR_AT)
+        right_raw = placed([P, H + H // 4], I32, "right_raw", RIGHT_AT)
         wr_raw = right_raw[:, 0:H]
         wr_sc_raw = right_raw[:, H:H + H // 4]
         nc.gpsimd.memset(tab_sc[:].bitcast(I32), 0)
@@ -59,8 +69,8 @@ def tile_list_syntax_node_latency_kernel(tc, tab_words, tab_scales, offs, offs2,
         list_r = keep.tile([P, S // 16], U16, name="list_r")
         list_p = keep.tile([P, S // 16], U16, name="list_p")
         tab_w = keep.tile([P, T], I32, name="tab_w", align_bytes=64)
-        wp_raw = [keep.tile([P, 4, 512], F32, name="wp_raw%d" % g) for g in range(G)]
-        w2_raw = [shared.tile([P, 4, N], F32, name="w2_raw%d" % g, align_bytes=64, offset=W2_AT + 8192 * g) for g in range(G)]
+        wp_raw = [placed([P, 4, 512], F32, "wp_raw%d" % g, WP_AT[g]) for g in range(G)]
+        w2_raw = [placed([P, 4 + g, N], F32, "w2_raw%d" % g, W2_AT[g]) for g in range(G)]
         bias = keep.tile([P, 4], F32, name="bias")
         wp_rows = wp.rearrange("(p i) (g r) -> g p i r", i=4, g=G)
         w2_rows = w2.rearrange("(g m t e) n -> g t m (e n)", g=G, t=4, e=4)
@@ -73,19 +83,32 @@ def tile_list_syntax_node_latency_kernel(tc, tab_words, tab_scales, offs, offs2,
         nc.sync.dma_start(wl_raw, wl_words[0].bitcast(I32))
         load_scale_rows(wl_sc_raw, wl_scales[0])
         nc.sync.dma_start(wp_raw[0][:], wp_rows[0])
-        nc.sync.dma_start(wp_raw[1][:], wp_rows[1])
         nc.sync.dma_start(wr_raw, wr_words[0].rearrange("p n t -> p (n t)").bitcast(I32))
         load_scale_rows(wr_sc_raw, wr_scales[0])
+        nc.sync.dma_start(wp_raw[1][:], wp_rows[1])
         for g in range(G):
             for t in range(4):
                 nc.sync.dma_start(w2_raw[g][:, t, :], w2_rows[g, t])
         nc.sync.dma_start(bias[:], b2.rearrange("(p t) -> p t", t=4))
 
-        def gather_scales(got, lst):
-            nc.vector.tensor_copy(got[:], tab_sc[:].indirect(lst))
+        lists = {"l": list_l, "r": list_r, "p": list_p}
+        got_words = {"l": [], "r": [], "p": []}
+        got_scales = {"l": [], "r": [], "p": []}
 
-        def gather_words(got, lst):
-            nc.vector.tensor_copy(got[:], tab_w[:].bitcast(U32).indirect(lst))
+        def gather(store, window, dtype, side, j0, width, at):
+            got = placed([P, width], dtype, "got_%s%d_%d" % (side, j0, len(store[side]) + (8 if dtype == U8 else 0)), at)
+            nc.vector.tensor_copy(got[:], window.indirect(lists[side][:, j0 // 16:(j0 + width) // 16]))
+            store[side].append((j0, width, got))
+
+        def gather_scales(side, j0, width, at=None):
+            gather(got_scales, tab_sc[:], U8, side, j0, width, at)
+
+        def gather_words(side, j0, width, at=None):
+            gather(got_words, tab_w[:].bitcast(U32), U32, side, j0, width, at)
+
+        def picked(store, side, j):
+            j0, width, got = [piece for piece in store[side] if piece[0] <= j < piece[0] + piece[1]][0]
+            return got[:, j - j0:j - j0 + JT]
 
         def deal(dealt, raw, run):
             nc.vector.tensor_copy(dealt.rearrange("p (g t m e) -> p g t m e", g=G, t=4, e=run),
@@ -95,64 +118,54 @@ def tile_list_syntax_node_latency_kernel(tc, tab_words, tab_scales, offs, offs2,
             nc.vector.tensor_copy(dealt.rearrange("p (g t c i) -> p g c t i", g=G, t=4, i=4),
                                   raw.rearrange("p (g c i t) -> p g c t i", g=G, t=4, i=4))
 
-        vl_sc = keep.tile([P, S], U8, name="vl_sc", align_bytes=64)
-        vl_first = keep.tile([P, FIRST], U32, name="vl_first", align_bytes=64)
-        wl_w = keep.tile([P, H // 2], I32, name="wl_w", align_bytes=64)
-        wl_sc = keep.tile([P, H], U8, name="wl_sc", align_bytes=64)
-        gather_scales(vl_sc, list_l[:])
-        gather_words(vl_first, list_l[:, 0:FIRST // 16])
-        deal(wl_w[:], wl_raw, 2)
-        deal_scales(wl_sc[:].bitcast(I32), wl_sc_raw)
+        def quantize(grouped, name, codes_at=None, plane_at=None):
+            codes = placed([P, 512], U32, name + "_w", codes_at)
+            plane = placed([P, 512], U8, name + "_sc", plane_at)
+            nc.vector.quantize_mx(out=codes[:].bitcast(E4M3), scales=plane[:], in_=grouped)
+            return codes, plane
 
-        vl_mid = shared.tile([P, LAST - FIRST], U32, name="vl_mid", align_bytes=64, offset=3072)
-        vl_last = shared.tile([P, S - LAST], U32, name="vl_last", align_bytes=64, offset=8192)
-        vr_sc = shared.tile([P, S], U8, name="vr_sc", align_bytes=64, offset=9728)
-        vp_sc = shared.tile([P, S], U8, name="vp_sc", align_bytes=64, offset=10752)
-        vr_w = shared.tile([P, S], U32, name="vr_w", align_bytes=64, offset=11776)
-        vp_w = shared.tile([P, S], U32, name="vp_w", align_bytes=64, offset=15872)
-        gather_words(vl_mid, list_l[:, FIRST // 16:LAST // 16])
-        gather_words(vl_last, list_l[:, LAST // 16:S // 16])
-        gather_scales(vr_sc, list_r[:])
-        gather_words(vr_w, list_r[:])
-        gather_scales(vp_sc, list_p[:])
-        gather_words(vp_w, list_p[:])
-        wr_w = shared.tile([P, H], I32, name="wr_w", align_bytes=64, offset=19968)
-        wr_sc = shared.tile([P, H], U8, name="wr_sc", align_bytes=64, offset=24064)
-        deal(wr_w[:], wr_raw, 4)
-        deal_scales(wr_sc[:].bitcast(I32), wr_sc_raw)
-
-
-        def quantize(grouped, name, passes, plane_at=None):
-            codes = keep.tile([P, passes * 512], U32, name=name + "_w", align_bytes=64)
-            if plane_at is None:
-                plane = keep.tile([P, passes * 512], U8, name=name + "_sc", align_bytes=64)
-            else:
-                plane = shared.tile([P, passes * 512], U8, name=name + "_sc", align_bytes=64, offset=plane_at)
-            nc.vector.quantize_mx(out=codes[:].bitcast(E4M3), scales=plane[:], in_=grouped[:])
-            return [(codes[:, 512 * g:512 * g + 512], plane[:, 512 * g:512 * g + 512]) for g in range(passes)]
-
-        wp_bf = keep.tile([P, G * 2048], BF16, name="wp_bf", align_bytes=64)
-        for g in range(G):
+        def cast_wp(g):
+            wp_bf = placed([P, 2048], BF16, "wp_bf%d" % g, WP_BF_AT[g])
             for t in range(4):
-                nc.gpsimd.tensor_scalar(wp_bf[:].rearrange("p (g t m e i) -> p g t m e i", g=G, t=4, e=4, i=4)[:, g, t],
+                nc.gpsimd.tensor_scalar(wp_bf[:].rearrange("p (t m e i) -> p t m e i", t=4, e=4, i=4)[:, t],
                                         wp_raw[g][:].rearrange("p i (m t e) -> p t m e i", t=4, e=4)[:, t],
                                         1.0, 0.0, ALU.mult, ALU.add)
-        wp_q = quantize(wp_bf, "wp", G, WR_AT + 4 * S)
+            return wp_bf[:]
 
-        units = [(jt, g) for jt in range(S // JT) for g in range(G)]
-        banks = [psum.tile([P, 4, JT], F32, name="bank%d" % b, bufs=1) for b in range(6)]
-        turns = []
+        def cast_w2(g, at, size):
+            w2_bf = placed([P, size * KB // 2], BF16, "w2_bf%d" % g, at)[:, 0:2048]
+            nc.scalar.copy(w2_bf.rearrange("p (u c t) -> p c u t", u=4, t=4), w2_raw[g][:, 0:4, :].rearrange("p t (c u) -> p c u t", u=4))
+            return w2_bf
 
-        def first_product(n, weights, moving):
-            jt, g = units[n]
-            words, plane = moving(jt * JT)
-            bank = banks[len(turns) % len(banks)]
-            turns.append(n)
+        banks = {reader: [psum.tile([P, 4, JT], F32, name="bank_%s%d" % (reader, b), bufs=1) for b in range(count)]
+                 for reader, count in (("vector", 3), ("scalar", 3), ("wide", 2))}
+        turns = {reader: [] for reader in banks}
+
+        def next_bank(reader):
+            turns[reader].append(reader)
+            return banks[reader][len(turns[reader]) % len(banks[reader])]
+
+        def first_product(n, side, weights, reader):
+            jt, g = divmod(n, G)
+            words = picked(got_words, side, jt * JT)
+            plane = picked(got_scales, side, jt * JT)
+            bank = next_bank(reader)
             for t in range(4):
                 w_codes, w_plane = weights(g, t)
                 nc.tensor.matmul_mx(out=bank[:, t, :], lhsT=w_codes, lhsT_scale=w_plane, rhs=words.bitcast(E4M3),
                                     rhs_scale=plane, start=True, stop=True)
             return bank[:].rearrange("p t j -> p j t")
+
+        wl_w = keep.tile([P, H // 2], I32, name="wl_w", align_bytes=64)
+        wl_sc = keep.tile([P, H], U8, name="wl_sc", align_bytes=64)
+        gather_scales("l", 0, S)
+        gather_words("l", 0, 256)
+        deal(wl_w[:], wl_raw, 2)
+        deal_scales(wl_sc[:].bitcast(I32), wl_sc_raw)
+        gather_words("l", 256, 768, LEFT_AT)
+        gather_scales("r", 0, 512, LEFT_AT + 5 * KB)
+        gather_words("r", 0, 256, LEFT_AT + 3 * KB)
+        gather_words("p", 0, 256, LEFT_AT + 4 * KB)
 
         def left(g, t):
             c = 512 * g + P * t
@@ -166,125 +179,188 @@ def tile_list_syntax_node_latency_kernel(tc, tab_words, tab_scales, offs, offs2,
             codes, plane = wp_q[g]
             return codes[:, P * t:P * t + P].bitcast(E4M3), plane[:, P * t:P * t + P]
 
-        def left_children(j):
-            words, at = (vl_first, 0) if j < FIRST else (vl_mid, FIRST) if j < LAST else (vl_last, LAST)
-            return words[:, j - at:j - at + JT], vl_sc[:, j:j + JT]
-
-        def right_children(j):
-            return vr_w[:, j:j + JT], vr_sc[:, j:j + JT]
-
-        def parents(j):
-            return vp_w[:, j:j + JT], vp_sc[:, j:j + JT]
-
         relu_a = []
+        prods = {}
+        copied = {}
+        h_tiles = {}
 
-        def rectified_left():
+        def rectify_left():
             n = len(relu_a)
-            act = keep.tile([P, JT, 4], F32, name="relu_a%d" % n)
-            nc.scalar.activation(act[:], first_product(n, left, left_children), ACT.Relu)
-            relu_a.append(act)
+            at, size = RELU_AT.get(n, (None, 2))
+            room = placed([P, size * KB // 4], F32, "relu_a%d" % n, at)
+            relu_a.append(room[:, 0:4 * JT].rearrange("p (j t) -> p j t", t=4))
+            nc.scalar.activation(relu_a[n], first_product(n, "l", left, "scalar"), ACT.Relu)
 
-        for n in range(RELUS_FIRST):
-            rectified_left()
+        def product(n):
+            at, size = PROD_AT.get(n, (None, 2))
+            room = placed([P, size * KB // 4], F32, "prod%d" % n, at)
+            prods[n] = room[:, 0:4 * JT].rearrange("p (j t) -> p j t", t=4)
+            nc.vector.scalar_tensor_tensor(prods[n], first_product(n, "r", right, "vector"), 0.0, relu_a[n], ALU.max, ALU.mult)
 
-        w2_q = []
-        for g in range(G):
-            w2_bf = shared.tile([P, 2048], BF16, name="w2_bf%d" % g, align_bytes=64, offset=4096 * g)
-            nc.scalar.copy(w2_bf[:].rearrange("p (u c t) -> p c u t", u=4, t=4), w2_raw[g][:].rearrange("p t (c u) -> p c u t", u=4))
-            w2_q.extend(quantize(w2_bf, "w2%d" % g, 1))
+        def copy_parent(n, reader="scalar"):
+            p_sb = placed([P, JT, 4], F32, "p_sb%d" % n, P_SB_AT.get(n))
+            nc.scalar.copy(p_sb[:], first_product(n, "p", parent, reader))
+            copied[n] = p_sb
+
+        def open_h(j0, width, at, size=4):
+            room = placed([P, size * KB // 2], BF16, "h_bf%d" % j0, at)
+            h_tiles[j0] = (width, room[:, 0:G * width * 4].rearrange("p (g j t) -> p g j t", g=G, t=4))
+
+        def h_part(n):
+            jt, g = divmod(n, G)
+            j0 = max(j for j in h_tiles if j <= jt * JT)
+            return h_tiles[j0][1][:, g, jt * JT - j0:jt * JT - j0 + JT, :]
+
+        def add_on_gpsimd(n):
+            nc.gpsimd.tensor_tensor(h_part(n), copied[n][:], prods[n], ALU.add)
+
+        def add_on_vector(n):
+            nc.vector.tensor_tensor(h_part(n), first_product(n, "p", parent, "vector"), prods[n], ALU.add)
 
         y_sc = keep.tile([P, S], U8, name="y_sc", align_bytes=64)
         y_rows = out_0.rearrange("(p t) j -> p t j", t=4)
         y_words = out_1[0].rearrange("p m t -> p (m t)").bitcast(I32)
 
-        def product(n):
-            prod = shared.tile([P, JT, 4], F32, name="prod%d" % n, align_bytes=64, offset=PROD_AT[n % len(PROD_AT)])
-            nc.vector.scalar_tensor_tensor(prod[:], first_product(n, right, right_children), 0.0, relu_a[n][:], ALU.max, ALU.mult)
-            return prod
-
-        def second_product(j0, width, h_bf, at_end):
-            h_w = ring.tile([P, G, width], U32, name="h_w", align_bytes=64)
+        def quantize_h(j0):
+            width, h_bf = h_tiles[j0]
+            h_w = placed([P, G, width], U32, "h_w%d" % j0, H_W_AT.get(j0))
             h_sc = ring.tile([P, G, width], U8, name="h_sc", align_bytes=64)
             nc.vector.quantize_mx(out=h_w[:].rearrange("p g j -> p (g j)").bitcast(E4M3), scales=h_sc[:].rearrange("p g j -> p (g j)"),
-                                  in_=h_bf[:].rearrange("p g j t -> p (g j t)"))
-            y = ring.tile([P, 4, width], F32, name="y")
-            if at_end:
-                pairs = [banks[(len(turns) + pair) % len(banks)] for pair in range(2)]
-            else:
-                pairs = [psum.tile([P, 2, width], F32, name="bank_y") for pair in range(2)]
+                                  in_=h_bf.rearrange("p g j t -> p (g j t)"))
+            return h_w, h_sc
+
+        def second_product(h_q, sums):
+            h_w, h_sc = h_q
             for t in range(4):
                 for g in range(G):
                     codes, plane = w2_q[g]
-                    nc.tensor.matmul_mx(out=pairs[t // 2][:, t % 2, :], lhsT=codes[:, P * t:P * t + P].bitcast(E4M3),
+                    nc.tensor.matmul_mx(out=sums[t], lhsT=codes[:, P * t:P * t + P].bitcast(E4M3),
                                         lhsT_scale=plane[:, P * t:P * t + P], rhs=h_w[:, g, :].bitcast(E4M3),
                                         rhs_scale=h_sc[:, g, :], start=(g == 0), stop=(g == G - 1))
-            return y, pairs
+            return sums
 
-        def add_bias(j0, width, y, pairs, on_vector):
+        def wide_banks():
+            pairs = [next_bank("wide")[:].rearrange("p (a b) j -> p a (b j)", a=2) for pair in range(2)]
+            return [pairs[t // 2][:, t % 2, :] for t in range(4)]
+
+        def add_bias(j0, width, sums, on_vector):
+            y = ring.tile([P, 4, width], F32, name="y")
             for t in range(4):
                 if t in on_vector:
-                    nc.vector.tensor_scalar(y[:, t, :], pairs[t // 2][:, t % 2, :], bias[:, t:t + 1], None, ALU.add)
+                    nc.vector.tensor_scalar(y[:, t, :], sums[t], bias[:, t:t + 1], None, ALU.add)
                 else:
-                    nc.scalar.activation(y[:, t, :], pairs[t // 2][:, t % 2, :], ACT.Identity, bias=bias[:, t:t + 1])
+                    nc.scalar.activation(y[:, t, :], sums[t], ACT.Identity, bias=bias[:, t:t + 1])
             nc.sync.dma_start(y_rows[:, :, j0:j0 + width], y[:])
+            return y
 
-        def cast_y(width, y, copy):
-            y_bf = ring.tile([P, width * 4], BF16, name="y_bf", align_bytes=64)
-            copy(y_bf[:].rearrange("p (c i t) -> p c t i", i=4, t=4), y[:].rearrange("p t (c i) -> p c t i", i=4))
+        def cast_y(j0, width, y, copy):
+            at, size = Y_BF_AT.get(j0, (None, 2))
+            y_bf = placed([P, size * KB // 2], BF16, "y_bf%d" % j0, at)[:, 0:4 * width]
+            copy(y_bf.rearrange("p (c i t) -> p c t i", i=4, t=4), y[:].rearrange("p t (c i) -> p c t i", i=4))
             return y_bf
 
         def planes(j0, width, y_bf):
-            y_w = ring.tile([P, width], U32, name="y_w", align_bytes=64)
-            nc.vector.quantize_mx(out=y_w[:].bitcast(E4M3), scales=y_sc[:, j0:j0 + width], in_=y_bf[:])
+            y_w = placed([P, width], U32, "y_w%d" % j0, Y_W_AT.get(j0))
+            nc.vector.quantize_mx(out=y_w[:].bitcast(E4M3), scales=y_sc[:, j0:j0 + width], in_=y_bf)
             nc.sync.dma_start(y_words[:, j0:j0 + width], y_w[:].bitcast(I32))
 
-        copied = {}
-        prods = {}
+        for n in range(EARLY_RELUS):
+            rectify_left()
 
-        def copy_parents(n0, count):
-            for n in range(n0, n0 + count):
-                p_sb = shared.tile([P, JT, 4], F32, name="p_sb%d" % n, align_bytes=64, offset=W2_AT + P_SB_AT[len(copied) % len(P_SB_AT)])
-                nc.scalar.copy(p_sb[:], first_product(n, parent, parents))
-                copied[n] = p_sb
+        wp_bf = cast_wp(0)
+        wr_w = placed([P, H], I32, "wr_w", WP_AT[0])
+        wr_sc = placed([P, H], U8, "wr_sc", WP_AT[0] + 4 * KB)
+        deal(wr_w[:], wr_raw, 4)
+        deal_scales(wr_sc[:].bitcast(I32), wr_sc_raw)
+        wp_q = [quantize(wp_bf, "wp0")]
+        gather_scales("p", 0, 512, RIGHT_AT + 2 * KB)
+        wp_bf = cast_wp(1)
+        for n in range(3):
+            product(n)
+        wp_q.append(quantize(wp_bf, "wp1"))
 
-        copy_parents(0, ON_GPSIMD[0])
-        waiting = []
-        n0 = 0
-        j0 = 0
-        for c, width in enumerate(CHUNKS):
-            h_bf = shared.tile([P, G, width, 4], BF16, name="h_bf%d" % c, align_bytes=64,
-                               offset=WR_AT + 5120 + (2048 if c == len(CHUNKS) - 1 else 0))
-            count = G * width // JT
-            h_part = [h_bf[:, k % G, (k // G) * JT:(k // G + 1) * JT, :] for k in range(count)]
-            for n in range(n0, n0 + count):
-                if n not in prods:
-                    prods[n] = product(n)
-            for k in range(count):
-                if k < ON_GPSIMD[c]:
-                    nc.gpsimd.tensor_tensor(h_part[k], copied[n0 + k][:], prods[n0 + k][:], ALU.add)
-                else:
-                    nc.vector.tensor_tensor(h_part[k], first_product(n0 + k, parent, parents), prods[n0 + k][:], ALU.add)
-            last = c == len(CHUNKS) - 1
-            if not last:
-                copy_parents(n0 + count, ON_GPSIMD[c + 1])
-                prods[n0 + count] = product(n0 + count)
-            while len(relu_a) < RELUS_BY_CHUNK[c]:
-                rectified_left()
-            y, pairs = second_product(j0, width, h_bf, last)
-            if c >= 2 and not last:
-                planes(*waiting.pop(0))
-            if c < len(CHUNKS) - 2:
-                add_bias(j0, width, y, pairs, ())
-                waiting.append((j0, width, cast_y(width, y, nc.scalar.copy)))
-            elif not last:
-                add_bias(j0, width, y, pairs, ())
-                before = (j0, width, y)
-            n0 = n0 + count
-            j0 = j0 + width
-        planes(*waiting.pop(0))
-        before_bf = cast_y(before[1], before[2], nc.vector.tensor_copy)
-        add_bias(S - width, width, y, pairs, (2, 3))
-        planes(before[0], before[1], before_bf)
-        planes(S - width, width, cast_y(width, y, nc.vector.tensor_copy))
+        open_h(0, 256, H_AT)
+        w2_bf = [cast_w2(0, None, 4)]
+        copy_parent(0)
+        product(3)
+        gather_words("r", 256, 256, WP_AT[1])
+        gather_words("p", 256, 256, WP_AT[1] + KB)
+        copy_parent(2)
+        copy_parent(1)
+        w2_bf.append(cast_w2(1, 84 * KB, 14))
+        add_on_gpsimd(0)
+        add_on_gpsimd(2)
+        product(4)
+        add_on_gpsimd(1)
+        copy_parent(3, "wide")
+        product(6)
+        copy_parent(4, "wide")
+        product(5)
+        gather_scales("p", 512, 512, 48 * KB)
+        gather_words("p", 512, 256, 49 * KB)
+        copy_parent(6)
+        copy_parent(5)
+        add_on_gpsimd(3)
+        w2_q = [quantize(w2_bf[0], "w20", 32 * KB, 36 * KB)]
+        h_q = quantize_h(0)
+        w2_q.append(quantize(w2_bf[1], "w21", 34 * KB, 36 * KB + 512))
+        sums = second_product(h_q, wide_banks())
+
+        open_h(256, 256, 96 * KB, 16)
+        rectify_left()
+        rectify_left()
+        rectify_left()
+        product(7)
+        rectify_left()
+        copy_parent(8)
+        gather_scales("r", 512, 512, 94 * KB)
+        gather_words("r", 512, 256, 95 * KB)
+        for n in (4, 6, 5):
+            add_on_gpsimd(n)
+        late = [cast_y(0, 256, add_bias(0, 256, sums, ()), nc.scalar.copy)]
+        add_on_vector(7)
+        product(8)
+        product(10)
+        copy_parent(10)
+        copy_parent(9)
+        sums = second_product(quantize_h(256), wide_banks())
+
+        open_h(512, 256, 100 * KB)
+        rectify_left()
+        product(9)
+        rectify_left()
+        product(11)
+        gather_words("p", 768, 256, 106 * KB)
+        gather_words("r", 768, 256, 107 * KB)
+        for n in (8, 10, 9):
+            add_on_gpsimd(n)
+        late.append(cast_y(256, 256, add_bias(256, 256, sums, ()), nc.scalar.copy))
+        add_on_vector(11)
+        product(12)
+        product(13)
+        copy_parent(12)
+        sums = second_product(quantize_h(512), wide_banks())
+        planes(0, 256, late[0])
+
+        open_h(768, JT, 118 * KB, 2)
+        add_on_gpsimd(12)
+        add_on_vector(13)
+        product(14)
+        product(15)
+        y_bf = cast_y(512, 256, add_bias(512, 256, sums, ()), nc.scalar.copy)
+        h_q = quantize_h(768)
+        planes(256, 256, late[1])
+        open_h(896, JT, None, 2)
+        add_on_vector(14)
+        add_on_vector(15)
+        bank = next_bank("scalar")
+        sums = second_product(h_q, [bank[:, t, :] for t in range(4)])
+        pairs = [next_bank("scalar"), next_bank("scalar")]
+        last_sums = second_product(quantize_h(896), [pairs[t // 2][:, t % 2, :] for t in range(4)])
+        planes(512, 256, y_bf)
+        y_bf = cast_y(768, JT, add_bias(768, JT, sums, ()), nc.vector.tensor_copy)
+        y = add_bias(896, JT, last_sums, (2, 3))
+        planes(768, JT, y_bf)
+        planes(896, JT, cast_y(896, JT, y, nc.vector.tensor_copy))
         for q in range(4):
             nc.sync.dma_start(out_2[0][4 * q:4 * q + 4, :].bitcast(I32), y_sc[32 * q:32 * q + 4, :].bitcast(I32))

@@ -20,20 +20,19 @@ P = 128
 G = H // 512
 JT = 128
 KB = 1024
-EARLY_RELUS = 10
+EARLY_RELUS = 16
 LEFT_AT = 0
-WP_AT = [6 * KB, 24 * KB]
-WP_BF_AT = [14 * KB, 16 * KB]
-RIGHT_AT = 18 * KB
-H_AT = 16 * KB
-W2_AT = [64 * KB, 72 * KB]
-PROD_AT = {3: (30 * KB, 8), 7: (88 * KB, 2), 8: (90 * KB, 2), 9: (110 * KB, 3), 10: (92 * KB, 2),
-           11: (104 * KB, 2), 12: (40 * KB, 3), 14: (120 * KB, 2), 15: (122 * KB, 2)}
-P_SB_AT = {0: 64 * KB, 2: 66 * KB, 1: 68 * KB, 3: 72 * KB, 4: 74 * KB, 6: 76 * KB, 5: 78 * KB}
-Y_W_AT = {0: 112 * KB + 512, 256: 42 * KB + 512}
-Y_BF_AT = {0: (116 * KB, 8)}
-RELU_AT = {4: (48 * KB, 2), 8: (46 * KB, 2), 10: (80 * KB, 2), 12: (113 * KB, 3), 14: (43 * KB, 2)}
-H_W_AT = {256: 46 * KB, 512: 113 * KB + 512, 768: 43 * KB + 512}
+WP_AT = [8 * KB, 32 * KB]
+WP_BF_AT = [16 * KB, 18 * KB]
+RIGHT_AT = 20 * KB
+W2_AT = [52 * KB, 60 * KB]
+PROD_AT = {1: (38 * KB, 4), 2: (32 * KB, 2), 3: (34 * KB, 2), 7: (92 * KB, 2), 8: (94 * KB, 3), 10: (97 * KB, 2),
+           13: (84 * KB, 2), 14: (90 * KB, 6), 15: (86 * KB, 2)}
+P_SB_AT = {1: 52 * KB, 4: 62 * KB, 6: 64 * KB, 5: 66 * KB}
+Y_W_AT = {0: 96 * KB + 512, 256: 79 * KB, 512: 88 * KB}
+Y_BF_AT = {0: (78 * KB, 2)}
+RELU_AT = {6: (42 * KB, 8), 11: (100 * KB, 2)}
+H_W_AT = {0: 48 * KB, 256: 100 * KB, 768: 92 * KB}
 
 
 def tile_list_syntax_node_latency_kernel(tc, tab_words, tab_scales, offs, offs2, offs3, wp, wl_words, wl_scales,
@@ -51,10 +50,10 @@ def tile_list_syntax_node_latency_kernel(tc, tab_words, tab_scales, offs, offs2,
             return shared.tile(shape, dtype, name=name, align_bytes=64, offset=at)
 
         tab_sc = keep.tile([P, T], U8, name="tab_sc", align_bytes=64)
-        left_raw = placed([P, 1536], I32, "left_raw", LEFT_AT)
+        left_raw = placed([P, 2048], I32, "left_raw", LEFT_AT)
         wl_raw = left_raw[:, 0:H // 2]
         wl_sc_raw = left_raw[:, H // 2:H // 2 + H // 4]
-        right_raw = placed([P, H + H // 4], I32, "right_raw", RIGHT_AT)
+        right_raw = placed([P, 2560], I32, "right_raw", RIGHT_AT)
         wr_raw = right_raw[:, 0:H]
         wr_sc_raw = right_raw[:, H:H + H // 4]
         nc.gpsimd.memset(tab_sc[:].bitcast(I32), 0)
@@ -70,7 +69,7 @@ def tile_list_syntax_node_latency_kernel(tc, tab_words, tab_scales, offs, offs2,
         list_p = keep.tile([P, S // 16], U16, name="list_p")
         tab_w = keep.tile([P, T], I32, name="tab_w", align_bytes=64)
         wp_raw = [placed([P, 4, 512], F32, "wp_raw%d" % g, WP_AT[g]) for g in range(G)]
-        w2_raw = [placed([P, 4 + g, N], F32, "w2_raw%d" % g, W2_AT[g]) for g in range(G)]
+        w2_raw = [placed([P, 4, N], F32, "w2_raw%d" % g, W2_AT[g]) for g in range(G)]
         bias = keep.tile([P, 4], F32, name="bias")
         wp_rows = wp.rearrange("(p i) (g r) -> g p i r", i=4, g=G)
         w2_rows = w2.rearrange("(g m t e) n -> g t m (e n)", g=G, t=4, e=4)
@@ -134,7 +133,7 @@ def tile_list_syntax_node_latency_kernel(tc, tab_words, tab_scales, offs, offs2,
 
         def cast_w2(g, at, size):
             w2_bf = placed([P, size * KB // 2], BF16, "w2_bf%d" % g, at)[:, 0:2048]
-            nc.scalar.copy(w2_bf.rearrange("p (u c t) -> p c u t", u=4, t=4), w2_raw[g][:, 0:4, :].rearrange("p t (c u) -> p c u t", u=4))
+            nc.scalar.copy(w2_bf.rearrange("p (u c t) -> p c t u", u=4, t=4), w2_raw[g][:].rearrange("p t (c u) -> p c t u", u=4))
             return w2_bf
 
         banks = {reader: [psum.tile([P, 4, JT], F32, name="bank_%s%d" % (reader, b), bufs=1) for b in range(count)]
@@ -163,9 +162,8 @@ def tile_list_syntax_node_latency_kernel(tc, tab_words, tab_scales, offs, offs2,
         deal(wl_w[:], wl_raw, 2)
         deal_scales(wl_sc[:].bitcast(I32), wl_sc_raw)
         gather_words("l", 256, 768, LEFT_AT)
-        gather_scales("r", 0, 512, LEFT_AT + 5 * KB)
-        gather_words("r", 0, 256, LEFT_AT + 3 * KB)
-        gather_words("p", 0, 256, LEFT_AT + 4 * KB)
+        gather_scales("p", 0, S, LEFT_AT + 3 * KB)
+        gather_words("p", 0, S, LEFT_AT + 4 * KB)
 
         def left(g, t):
             c = 512 * g + P * t
@@ -189,7 +187,7 @@ def tile_list_syntax_node_latency_kernel(tc, tab_words, tab_scales, offs, offs2,
             at, size = RELU_AT.get(n, (None, 2))
             room = placed([P, size * KB // 4], F32, "relu_a%d" % n, at)
             relu_a.append(room[:, 0:4 * JT].rearrange("p (j t) -> p j t", t=4))
-            nc.scalar.activation(relu_a[n], first_product(n, "l", left, "scalar"), ACT.Relu)
+            nc.scalar.activation(relu_a[n], first_product(n, "l", left, "scalar" if n < 13 else "vector"), ACT.Relu)
 
         def product(n):
             at, size = PROD_AT.get(n, (None, 2))
@@ -239,8 +237,8 @@ def tile_list_syntax_node_latency_kernel(tc, tab_words, tab_scales, offs, offs2,
                                         rhs_scale=h_sc[:, g, :], start=(g == 0), stop=(g == G - 1))
             return sums
 
-        def wide_banks():
-            pairs = [next_bank("wide")[:].rearrange("p (a b) j -> p a (b j)", a=2) for pair in range(2)]
+        def wide_banks(reader="wide"):
+            pairs = [next_bank(reader)[:].rearrange("p (a b) j -> p a (b j)", a=2) for pair in range(2)]
             return [pairs[t // 2][:, t % 2, :] for t in range(4)]
 
         def add_bias(j0, width, sums, on_vector):
@@ -273,94 +271,73 @@ def tile_list_syntax_node_latency_kernel(tc, tab_words, tab_scales, offs, offs2,
         deal(wr_w[:], wr_raw, 4)
         deal_scales(wr_sc[:].bitcast(I32), wr_sc_raw)
         wp_q = [quantize(wp_bf, "wp0")]
-        gather_scales("p", 0, 512, RIGHT_AT + 2 * KB)
+        gather_scales("r", 0, S, RIGHT_AT + 2 * KB)
+        gather_words("r", 0, 512, RIGHT_AT + 4 * KB)
+        gather_words("r", 512, 512, RIGHT_AT + 6 * KB)
+        copy_parent(0)
+        copy_parent(2)
         wp_bf = cast_wp(1)
-        for n in range(3):
-            product(n)
+        product(0)
         wp_q.append(quantize(wp_bf, "wp1"))
 
-        open_h(0, 256, H_AT)
+        open_h(0, 256, WP_BF_AT[1])
         w2_bf = [cast_w2(0, None, 4)]
-        copy_parent(0)
-        product(3)
-        gather_words("r", 256, 256, WP_AT[1])
-        gather_words("p", 256, 256, WP_AT[1] + KB)
-        copy_parent(2)
         copy_parent(1)
-        w2_bf.append(cast_w2(1, 84 * KB, 14))
-        add_on_gpsimd(0)
-        add_on_gpsimd(2)
-        product(4)
-        add_on_gpsimd(1)
-        copy_parent(3, "wide")
-        product(6)
-        copy_parent(4, "wide")
-        product(5)
-        gather_scales("p", 512, 512, 48 * KB)
-        gather_words("p", 512, 256, 49 * KB)
-        copy_parent(6)
-        copy_parent(5)
-        add_on_gpsimd(3)
-        w2_q = [quantize(w2_bf[0], "w20", 32 * KB, 36 * KB)]
+        w2_bf.append(cast_w2(1, 84 * KB, 12))
+        for n in (2, 1, 3):
+            product(n)
+        add_on_vector(3)
+        for n in (0, 2, 1):
+            add_on_gpsimd(n)
+        for n in (4, 6, 5):
+            product(n)
+        for n in (4, 6, 5):
+            copy_parent(n)
+        w2_q = [quantize(w2_bf[0], "w20", 44 * KB, 40 * KB)]
         h_q = quantize_h(0)
-        w2_q.append(quantize(w2_bf[1], "w21", 34 * KB, 36 * KB + 512))
+        w2_q.append(quantize(w2_bf[1], "w21", 46 * KB, 40 * KB + 512))
         sums = second_product(h_q, wide_banks())
 
-        open_h(256, 256, 96 * KB, 16)
-        rectify_left()
-        rectify_left()
-        rectify_left()
+        open_h(256, 256, 88 * KB)
+        for n in (8, 12, 14):
+            copy_parent(n)
         product(7)
-        rectify_left()
-        copy_parent(8)
-        gather_scales("r", 512, 512, 94 * KB)
-        gather_words("r", 512, 256, 95 * KB)
+        product(8)
+        add_on_vector(7)
         for n in (4, 6, 5):
             add_on_gpsimd(n)
         late = [cast_y(0, 256, add_bias(0, 256, sums, ()), nc.scalar.copy)]
-        add_on_vector(7)
-        product(8)
-        product(10)
-        copy_parent(10)
-        copy_parent(9)
+        for n in (10, 9, 11, 12):
+            product(n)
         sums = second_product(quantize_h(256), wide_banks())
 
-        open_h(512, 256, 100 * KB)
-        rectify_left()
-        product(9)
-        rectify_left()
-        product(11)
-        gather_words("p", 768, 256, 106 * KB)
-        gather_words("r", 768, 256, 107 * KB)
-        for n in (8, 10, 9):
-            add_on_gpsimd(n)
+        open_h(512, 256, 80 * KB, 12)
+        add_on_gpsimd(8)
+        for n in (9, 10, 11):
+            add_on_vector(n)
         late.append(cast_y(256, 256, add_bias(256, 256, sums, ()), nc.scalar.copy))
-        add_on_vector(11)
-        product(12)
-        product(13)
-        copy_parent(12)
-        sums = second_product(quantize_h(512), wide_banks())
         planes(0, 256, late[0])
+        sums = second_product(quantize_h(512), wide_banks("scalar"))
 
-        open_h(768, JT, 118 * KB, 2)
+        open_h(768, JT, 79 * KB, 2)
+        open_h(896, JT, 88 * KB, 2)
+        for n in (14, 13, 15):
+            product(n)
         add_on_gpsimd(12)
+        add_on_gpsimd(14)
         add_on_vector(13)
-        product(14)
-        product(15)
-        y_bf = cast_y(512, 256, add_bias(512, 256, sums, ()), nc.scalar.copy)
-        h_q = quantize_h(768)
-        planes(256, 256, late[1])
-        open_h(896, JT, None, 2)
-        add_on_vector(14)
         add_on_vector(15)
-        bank = next_bank("scalar")
-        sums = second_product(h_q, [bank[:, t, :] for t in range(4)])
-        pairs = [next_bank("scalar"), next_bank("scalar")]
-        last_sums = second_product(quantize_h(896), [pairs[t // 2][:, t % 2, :] for t in range(4)])
-        planes(512, 256, y_bf)
-        y_bf = cast_y(768, JT, add_bias(768, JT, sums, ()), nc.vector.tensor_copy)
-        y = add_bias(896, JT, last_sums, (2, 3))
-        planes(768, JT, y_bf)
-        planes(896, JT, cast_y(896, JT, y, nc.vector.tensor_copy))
+        late.append(cast_y(512, 256, add_bias(512, 256, sums, ()), nc.scalar.copy))
+        bank = next_bank("wide")
+        sums = second_product(quantize_h(768), [bank[:, t, :] for t in range(4)])
+        bank = next_bank("wide")
+        last_sums = second_product(quantize_h(896), [bank[:, t, :] for t in range(4)])
+        planes(256, 256, late[1])
+        planes(512, 256, late[2])
+        before_bf = cast_y(768, JT, add_bias(768, JT, sums, ()), nc.scalar.copy)
+        last_bf = cast_y(896, JT, add_bias(896, JT, last_sums, (0, 1, 2, 3)), nc.vector.tensor_copy)
+        planes(768, JT, before_bf)
+        planes(896, JT, last_bf)
         for q in range(4):
-            nc.sync.dma_start(out_2[0][4 * q:4 * q + 4, :].bitcast(I32), y_sc[32 * q:32 * q + 4, :].bitcast(I32))
+            queue = nc.sync if q % 2 == 0 else nc.scalar
+            queue.dma_start(out_2[0][4 * q:4 * q + 4, :].bitcast(I32), y_sc[32 * q:32 * q + 4, :].bitcast(I32))

@@ -20,19 +20,19 @@ P = 128
 G = H // 512
 JT = 128
 KB = 1024
-EARLY_RELUS = 16
+EARLY_RELUS = 14
 LEFT_AT = 0
 WP_AT = [8 * KB, 32 * KB]
 WP_BF_AT = [16 * KB, 18 * KB]
 RIGHT_AT = 20 * KB
 W2_AT = [52 * KB, 60 * KB]
-PROD_AT = {1: (38 * KB, 4), 2: (32 * KB, 2), 3: (34 * KB, 2), 7: (92 * KB, 2), 8: (94 * KB, 3), 10: (97 * KB, 2),
-           13: (84 * KB, 2), 14: (90 * KB, 6), 15: (86 * KB, 2)}
-P_SB_AT = {1: 52 * KB, 4: 62 * KB, 6: 64 * KB, 5: 66 * KB}
-Y_W_AT = {0: 96 * KB + 512, 256: 79 * KB, 512: 88 * KB}
+PAIRS = {2: 1, 6: 5}
+PROD_AT = {2: (36 * KB, 6), 3: (34 * KB, 2), 6: (None, 4), 8: (18 * KB, 2), 10: (96 * KB, 2), 15: (86 * KB, 2)}
+P_SB_AT = {2: (52 * KB, 4), 4: (62 * KB, 2), 6: (64 * KB, 4), 8: (94 * KB, 2)}
+Y_W_AT = {0: 95 * KB + 512, 256: 79 * KB, 512: 88 * KB}
 Y_BF_AT = {0: (78 * KB, 2)}
-RELU_AT = {6: (42 * KB, 8), 11: (100 * KB, 2)}
-H_W_AT = {0: 48 * KB, 256: 100 * KB, 768: 92 * KB}
+RELU_AT = {5: (42 * KB, 8), 14: (100 * KB, 2), 15: (102 * KB, 2)}
+H_W_AT = {0: 48 * KB, 256: 100 * KB, 768: 102 * KB}
 
 
 def tile_list_syntax_node_latency_kernel(tc, tab_words, tab_scales, offs, offs2, offs3, wp, wl_words, wl_scales,
@@ -187,33 +187,43 @@ def tile_list_syntax_node_latency_kernel(tc, tab_words, tab_scales, offs, offs2,
             at, size = RELU_AT.get(n, (None, 2))
             room = placed([P, size * KB // 4], F32, "relu_a%d" % n, at)
             relu_a.append(room[:, 0:4 * JT].rearrange("p (j t) -> p j t", t=4))
-            nc.scalar.activation(relu_a[n], first_product(n, "l", left, "scalar" if n < 13 else "vector"), ACT.Relu)
+            nc.scalar.activation(relu_a[n], first_product(n, "l", left, "vector" if EARLY_RELUS - 3 <= n < EARLY_RELUS else "scalar"), ACT.Relu)
+
+        def room_for(store, places, name, n):
+            if n not in store:
+                at, size = places.get(n, (None, 2))
+                room = placed([P, size * KB // 4], F32, "%s%d" % (name, n), at)
+                store[n] = room[:, 0:4 * JT]
+                if n in PAIRS:
+                    store[PAIRS[n]] = room[:, 4 * JT:8 * JT]
+                    store[n, PAIRS[n]] = room[:, 0:8 * JT]
+            return store[n].rearrange("p (j t) -> p j t", t=4)
 
         def product(n):
-            at, size = PROD_AT.get(n, (None, 2))
-            room = placed([P, size * KB // 4], F32, "prod%d" % n, at)
-            prods[n] = room[:, 0:4 * JT].rearrange("p (j t) -> p j t", t=4)
-            nc.vector.scalar_tensor_tensor(prods[n], first_product(n, "r", right, "vector"), 0.0, relu_a[n], ALU.max, ALU.mult)
+            nc.vector.scalar_tensor_tensor(room_for(prods, PROD_AT, "prod", n), first_product(n, "r", right, "vector"), 0.0,
+                                           relu_a[n], ALU.max, ALU.mult)
 
-        def copy_parent(n, reader="scalar"):
-            p_sb = placed([P, JT, 4], F32, "p_sb%d" % n, P_SB_AT.get(n))
-            nc.scalar.copy(p_sb[:], first_product(n, "p", parent, reader))
-            copied[n] = p_sb
+        def copy_parent(n):
+            nc.scalar.copy(room_for(copied, P_SB_AT, "p_sb", n), first_product(n, "p", parent, "scalar"))
 
         def open_h(j0, width, at, size=4):
             room = placed([P, size * KB // 2], BF16, "h_bf%d" % j0, at)
-            h_tiles[j0] = (width, room[:, 0:G * width * 4].rearrange("p (g j t) -> p g j t", g=G, t=4))
+            h_tiles[j0] = (width, room[:, 0:G * width * 4])
 
-        def h_part(n):
+        def h_part(n, units=1):
             jt, g = divmod(n, G)
             j0 = max(j for j in h_tiles if j <= jt * JT)
-            return h_tiles[j0][1][:, g, jt * JT - j0:jt * JT - j0 + JT, :]
+            width, h_bf = h_tiles[j0]
+            at = 4 * (g * width + jt * JT - j0)
+            return h_bf[:, at:at + 4 * JT * units]
 
         def add_on_gpsimd(n):
-            nc.gpsimd.tensor_tensor(h_part(n), copied[n][:], prods[n], ALU.add)
+            key = (n, PAIRS[n]) if n in PAIRS else n
+            nc.gpsimd.tensor_tensor(h_part(n, 2 if n in PAIRS else 1), copied[key], prods[key], ALU.add)
 
         def add_on_vector(n):
-            nc.vector.tensor_tensor(h_part(n), first_product(n, "p", parent, "vector"), prods[n], ALU.add)
+            nc.vector.tensor_tensor(h_part(n).rearrange("p (j t) -> p j t", t=4), first_product(n, "p", parent, "vector"),
+                                    prods[n].rearrange("p (j t) -> p j t", t=4), ALU.add)
 
         y_sc = keep.tile([P, S], U8, name="y_sc", align_bytes=64)
         y_rows = out_0.rearrange("(p t) j -> p t j", t=4)
@@ -224,7 +234,7 @@ def tile_list_syntax_node_latency_kernel(tc, tab_words, tab_scales, offs, offs2,
             h_w = placed([P, G, width], U32, "h_w%d" % j0, H_W_AT.get(j0))
             h_sc = ring.tile([P, G, width], U8, name="h_sc", align_bytes=64)
             nc.vector.quantize_mx(out=h_w[:].rearrange("p g j -> p (g j)").bitcast(E4M3), scales=h_sc[:].rearrange("p g j -> p (g j)"),
-                                  in_=h_bf.rearrange("p g j t -> p (g j t)"))
+                                  in_=h_bf)
             return h_w, h_sc
 
         def second_product(h_q, sums):
@@ -262,6 +272,11 @@ def tile_list_syntax_node_latency_kernel(tc, tab_words, tab_scales, offs, offs2,
             nc.vector.quantize_mx(out=y_w[:].bitcast(E4M3), scales=y_sc[:, j0:j0 + width], in_=y_bf)
             nc.sync.dma_start(y_words[:, j0:j0 + width], y_w[:].bitcast(I32))
 
+        def store_scale_rows(j0, j1):
+            for q in range(4):
+                queue = nc.sync if j1 < S or q % 2 == 0 else nc.scalar
+                queue.dma_start(out_2[0][4 * q:4 * q + 4, j0:j1].bitcast(I32), y_sc[32 * q:32 * q + 4, j0:j1].bitcast(I32))
+
         for n in range(EARLY_RELUS):
             rectify_left()
 
@@ -275,21 +290,21 @@ def tile_list_syntax_node_latency_kernel(tc, tab_words, tab_scales, offs, offs2,
         gather_words("r", 0, 512, RIGHT_AT + 4 * KB)
         gather_words("r", 512, 512, RIGHT_AT + 6 * KB)
         copy_parent(0)
-        copy_parent(2)
         wp_bf = cast_wp(1)
         product(0)
         wp_q.append(quantize(wp_bf, "wp1"))
 
         open_h(0, 256, WP_BF_AT[1])
         w2_bf = [cast_w2(0, None, 4)]
+        copy_parent(2)
         copy_parent(1)
-        w2_bf.append(cast_w2(1, 84 * KB, 12))
+        w2_bf.append(cast_w2(1, 84 * KB, 8))
         for n in (2, 1, 3):
             product(n)
         add_on_vector(3)
-        for n in (0, 2, 1):
+        for n in (0, 2):
             add_on_gpsimd(n)
-        for n in (4, 6, 5):
+        for n in (4, 6, 5, 7):
             product(n)
         for n in (4, 6, 5):
             copy_parent(n)
@@ -299,15 +314,16 @@ def tile_list_syntax_node_latency_kernel(tc, tab_words, tab_scales, offs, offs2,
         sums = second_product(h_q, wide_banks())
 
         open_h(256, 256, 88 * KB)
-        for n in (8, 12, 14):
-            copy_parent(n)
-        product(7)
+        rectify_left()
+        rectify_left()
         product(8)
         add_on_vector(7)
-        for n in (4, 6, 5):
+        for n in (4, 6):
             add_on_gpsimd(n)
         late = [cast_y(0, 256, add_bias(0, 256, sums, ()), nc.scalar.copy)]
-        for n in (10, 9, 11, 12):
+        copy_parent(8)
+        copy_parent(12)
+        for n in (10, 9, 11, 12, 14, 13):
             product(n)
         sums = second_product(quantize_h(256), wide_banks())
 
@@ -321,23 +337,21 @@ def tile_list_syntax_node_latency_kernel(tc, tab_words, tab_scales, offs, offs2,
 
         open_h(768, JT, 79 * KB, 2)
         open_h(896, JT, 88 * KB, 2)
-        for n in (14, 13, 15):
-            product(n)
         add_on_gpsimd(12)
-        add_on_gpsimd(14)
         add_on_vector(13)
-        add_on_vector(15)
+        product(15)
+        add_on_vector(14)
         late.append(cast_y(512, 256, add_bias(512, 256, sums, ()), nc.scalar.copy))
         bank = next_bank("wide")
         sums = second_product(quantize_h(768), [bank[:, t, :] for t in range(4)])
-        bank = next_bank("wide")
-        last_sums = second_product(quantize_h(896), [bank[:, t, :] for t in range(4)])
+        add_on_vector(15)
         planes(256, 256, late[1])
+        pairs = [next_bank("wide"), next_bank("vector")]
+        last_sums = second_product(quantize_h(896), [pairs[t // 2][:, t % 2, :] for t in range(4)])
         planes(512, 256, late[2])
-        before_bf = cast_y(768, JT, add_bias(768, JT, sums, ()), nc.scalar.copy)
-        last_bf = cast_y(896, JT, add_bias(896, JT, last_sums, (0, 1, 2, 3)), nc.vector.tensor_copy)
+        before = add_bias(768, JT, sums, ())
+        y = add_bias(896, JT, last_sums, (2, 3))
+        before_bf = cast_y(768, JT, before, nc.scalar.copy)
+        planes(896, JT, cast_y(896, JT, y, nc.vector.tensor_copy))
         planes(768, JT, before_bf)
-        planes(896, JT, last_bf)
-        for q in range(4):
-            queue = nc.sync if q % 2 == 0 else nc.scalar
-            queue.dma_start(out_2[0][4 * q:4 * q + 4, :].bitcast(I32), y_sc[32 * q:32 * q + 4, :].bitcast(I32))
+        store_scale_rows(0, S)

@@ -20,19 +20,19 @@ P = 128
 G = H // 512
 JT = 128
 KB = 1024
-EARLY_RELUS = 14
+EARLY_RELUS = 16
 LEFT_AT = 0
 WP_AT = [8 * KB, 32 * KB]
 WP_BF_AT = [16 * KB, 18 * KB]
 RIGHT_AT = 20 * KB
 W2_AT = [52 * KB, 60 * KB]
 PAIRS = {2: 1, 6: 5}
-PROD_AT = {2: (36 * KB, 6), 3: (34 * KB, 2), 6: (None, 4), 8: (18 * KB, 2), 10: (96 * KB, 2), 15: (86 * KB, 2)}
-P_SB_AT = {2: (52 * KB, 4), 4: (62 * KB, 2), 6: (64 * KB, 4), 8: (94 * KB, 2)}
-Y_W_AT = {0: 95 * KB + 512, 256: 79 * KB, 512: 88 * KB}
-Y_BF_AT = {0: (78 * KB, 2)}
-RELU_AT = {5: (42 * KB, 8), 14: (100 * KB, 2), 15: (102 * KB, 2)}
-H_W_AT = {0: 48 * KB, 256: 100 * KB, 768: 102 * KB}
+PROD_AT = {2: (36 * KB, 6), 3: (34 * KB, 2), 6: (None, 4), 7: (18 * KB, 2), 8: (92 * KB, 2), 11: (96 * KB, 4),
+           13: (98 * KB, 2), 14: (96 * KB, 2)}
+P_SB_AT = {2: (52 * KB, 4), 4: (62 * KB, 2), 6: (64 * KB, 4)}
+RELU_AT = {6: (42 * KB, 8), 11: (100 * KB, 2)}
+H_W_AT = {0: 48 * KB, 256: 100 * KB}
+H_AT = 88 * KB
 
 
 def tile_list_syntax_node_latency_kernel(tc, tab_words, tab_scales, offs, offs2, offs3, wp, wl_words, wl_scales,
@@ -261,16 +261,14 @@ def tile_list_syntax_node_latency_kernel(tc, tab_words, tab_scales, offs, offs2,
             nc.sync.dma_start(y_rows[:, :, j0:j0 + width], y[:])
             return y
 
-        def cast_y(j0, width, y, copy):
-            at, size = Y_BF_AT.get(j0, (None, 2))
-            y_bf = placed([P, size * KB // 2], BF16, "y_bf%d" % j0, at)[:, 0:4 * width]
-            copy(y_bf.rearrange("p (c i t) -> p c t i", i=4, t=4), y[:].rearrange("p t (c i) -> p c t i", i=4))
-            return y_bf
+        y_bf = keep.tile([P, 4 * S], BF16, name="y_bf", align_bytes=64)
 
-        def planes(j0, width, y_bf):
-            y_w = placed([P, width], U32, "y_w%d" % j0, Y_W_AT.get(j0))
-            nc.vector.quantize_mx(out=y_w[:].bitcast(E4M3), scales=y_sc[:, j0:j0 + width], in_=y_bf)
-            nc.sync.dma_start(y_words[:, j0:j0 + width], y_w[:].bitcast(I32))
+        def cast_y(j0, width, y, copy):
+            copy(y_bf[:, 4 * j0:4 * (j0 + width)].rearrange("p (c i t) -> p c t i", i=4, t=4),
+                 y[:].rearrange("p t (c i) -> p c t i", i=4))
+
+        def planes(y_w, at, j0, j1):
+            nc.vector.quantize_mx(out=y_w[:, j0 - at:j1 - at].bitcast(E4M3), scales=y_sc[:, j0:j1], in_=y_bf[:, 4 * j0:4 * j1])
 
         def store_scale_rows(j0, j1):
             for q in range(4):
@@ -298,13 +296,13 @@ def tile_list_syntax_node_latency_kernel(tc, tab_words, tab_scales, offs, offs2,
         w2_bf = [cast_w2(0, None, 4)]
         copy_parent(2)
         copy_parent(1)
-        w2_bf.append(cast_w2(1, 84 * KB, 8))
-        for n in (2, 1, 3):
+        w2_bf.append(cast_w2(1, 84 * KB, 10))
+        for n in (2, 1, 3, 4):
             product(n)
         add_on_vector(3)
         for n in (0, 2):
             add_on_gpsimd(n)
-        for n in (4, 6, 5, 7):
+        for n in (6, 5):
             product(n)
         for n in (4, 6, 5):
             copy_parent(n)
@@ -313,45 +311,48 @@ def tile_list_syntax_node_latency_kernel(tc, tab_words, tab_scales, offs, offs2,
         w2_q.append(quantize(w2_bf[1], "w21", 46 * KB, 40 * KB + 512))
         sums = second_product(h_q, wide_banks())
 
-        open_h(256, 256, 88 * KB)
-        rectify_left()
-        rectify_left()
+        open_h(256, 256, H_AT)
+        for n in (8, 12, 14):
+            copy_parent(n)
+        product(7)
         product(8)
         add_on_vector(7)
         for n in (4, 6):
             add_on_gpsimd(n)
-        late = [cast_y(0, 256, add_bias(0, 256, sums, ()), nc.scalar.copy)]
-        copy_parent(8)
-        copy_parent(12)
-        for n in (10, 9, 11, 12, 14, 13):
+        cast_y(0, 256, add_bias(0, 256, sums, ()), nc.scalar.copy)
+        for n in (10, 9, 11, 12):
             product(n)
         sums = second_product(quantize_h(256), wide_banks())
 
-        open_h(512, 256, 80 * KB, 12)
+        open_h(512, 256, H_AT)
         add_on_gpsimd(8)
         for n in (9, 10, 11):
             add_on_vector(n)
-        late.append(cast_y(256, 256, add_bias(256, 256, sums, ()), nc.scalar.copy))
-        planes(0, 256, late[0])
+        cast_y(256, 256, add_bias(256, 256, sums, ()), nc.scalar.copy)
         sums = second_product(quantize_h(512), wide_banks("scalar"))
 
-        open_h(768, JT, 79 * KB, 2)
-        open_h(896, JT, 88 * KB, 2)
+        open_h(768, JT, H_AT, 2)
+        open_h(896, JT, H_AT + 2 * KB, 2)
+        for n in (14, 13, 15):
+            product(n)
         add_on_gpsimd(12)
+        add_on_gpsimd(14)
         add_on_vector(13)
-        product(15)
-        add_on_vector(14)
-        late.append(cast_y(512, 256, add_bias(512, 256, sums, ()), nc.scalar.copy))
+        add_on_vector(15)
+        cast_y(512, 256, add_bias(512, 256, sums, ()), nc.scalar.copy)
         bank = next_bank("wide")
         sums = second_product(quantize_h(768), [bank[:, t, :] for t in range(4)])
-        add_on_vector(15)
-        planes(256, 256, late[1])
         pairs = [next_bank("wide"), next_bank("vector")]
         last_sums = second_product(quantize_h(896), [pairs[t // 2][:, t % 2, :] for t in range(4)])
-        planes(512, 256, late[2])
+        y_w = placed([P, 768], U32, "y_w_first", H_AT - KB)
+        planes(y_w, 0, 0, 512)
+        planes(y_w, 0, 512, 768)
+        nc.sync.dma_start(y_words[:, 0:768], y_w[:].bitcast(I32))
         before = add_bias(768, JT, sums, ())
         y = add_bias(896, JT, last_sums, (2, 3))
-        before_bf = cast_y(768, JT, before, nc.scalar.copy)
-        planes(896, JT, cast_y(896, JT, y, nc.vector.tensor_copy))
-        planes(768, JT, before_bf)
+        cast_y(768, JT, before, nc.scalar.copy)
+        cast_y(896, JT, y, nc.vector.tensor_copy)
+        y_w = placed([P, 256], U32, "y_w_last", None)
+        planes(y_w, 768, 768, S)
+        nc.sync.dma_start(y_words[:, 768:S], y_w[:].bitcast(I32))
         store_scale_rows(0, S)

@@ -285,8 +285,8 @@ def tile_list_syntax_node_latency_kernel(tc, tab_words, tab_scales, offs, offs2,
         deal_scales(wr_sc[:].bitcast(I32), wr_sc_raw)
         wp_q = [quantize(wp_bf, "wp0")]
         gather_scales("r", 0, S, RIGHT_AT + 2 * KB)
-        gather_words("r", 0, 512, RIGHT_AT + 4 * KB)
-        gather_words("r", 512, 512, RIGHT_AT + 6 * KB)
+        gather_words("r", 0, 256, RIGHT_AT + 4 * KB)
+        gather_words("r", 256, 768, RIGHT_AT + 5 * KB)
         copy_parent(0)
         wp_bf = cast_wp(1)
         product(0)

@@ -56,7 +56,6 @@ def tile_list_syntax_node_latency_kernel(tc, tab_words, tab_scales, offs, offs2,
         right_raw = placed([P, 2560], I32, "right_raw", RIGHT_AT)
         wr_raw = right_raw[:, 0:H]
         wr_sc_raw = right_raw[:, H:H + H // 4]
-        nc.gpsimd.memset(tab_sc[:].bitcast(I32), 0)
         nc.gpsimd.memset(wl_sc_raw, 0)
         nc.gpsimd.memset(wr_sc_raw, 0)
 
@@ -75,12 +74,14 @@ def tile_list_syntax_node_latency_kernel(tc, tab_words, tab_scales, offs, offs2,
         w2_rows = w2.rearrange("(g m t e) n -> g t m (e n)", g=G, t=4, e=4)
 
         nc.sync.dma_start(list_l[:], offs2)
-        nc.sync.dma_start(list_r[:], offs3)
-        nc.sync.dma_start(list_p[:], offs)
-        load_scale_rows(tab_sc[:].bitcast(I32), tab_scales[0])
+        for q in range(4):
+            nc.sync.dma_start(tab_sc[:].bitcast(I32)[32 * q:32 * q + 32, :],
+                              tab_scales[0][4 * q:4 * q + 4, :].bitcast(I32).unsqueeze(0).to_broadcast([8, 4, T // 4]))
         nc.sync.dma_start(tab_w[:], tab_words[0].rearrange("p n t -> p (n t)").bitcast(I32))
         nc.sync.dma_start(wl_raw, wl_words[0].bitcast(I32))
         load_scale_rows(wl_sc_raw, wl_scales[0])
+        nc.sync.dma_start(list_p[:], offs)
+        nc.sync.dma_start(list_r[:], offs3)
         nc.sync.dma_start(wp_raw[0][:], wp_rows[0])
         nc.sync.dma_start(wr_raw, wr_words[0].rearrange("p n t -> p (n t)").bitcast(I32))
         load_scale_rows(wr_sc_raw, wr_scales[0])

@@ -20,19 +20,17 @@ P = 128
 G = H // 512
 JT = 128
 KB = 1024
-EARLY_RELUS = 16
-LEFT_AT = 0
-WP_AT = [8 * KB, 32 * KB]
-WP_BF_AT = [16 * KB, 18 * KB]
-RIGHT_AT = 20 * KB
-W2_AT = [52 * KB, 60 * KB]
-PAIRS = {2: 1, 6: 5}
-PROD_AT = {2: (36 * KB, 6), 3: (34 * KB, 2), 6: (None, 4), 7: (18 * KB, 2), 8: (92 * KB, 2), 11: (96 * KB, 4),
-           13: (98 * KB, 2), 14: (96 * KB, 2)}
-P_SB_AT = {2: (52 * KB, 4), 4: (62 * KB, 2), 6: (64 * KB, 4)}
-RELU_AT = {6: (42 * KB, 8), 11: (100 * KB, 2)}
-H_W_AT = {0: 48 * KB, 256: 100 * KB}
-H_AT = 88 * KB
+UNITS = G * S // JT
+LEFT_AT = 3 * KB
+WP1_AT = 8 * KB
+WP_BF_AT = [16 * KB, 20 * KB]
+W2_BF_AT = [20 * KB, 24 * KB]
+W21_AT = 38 * KB
+H_AT = 46 * KB
+RELU_AT = {0: 28 * KB, 4: 36 * KB, 9: 54 * KB, 14: 56 * KB}
+PROD_AT = {2: 32 * KB, 5: 24 * KB, 6: 26 * KB, 7: 20 * KB, 14: 58 * KB}
+P_SB_AT = {2: 34 * KB, 5: W21_AT, 6: W21_AT + 2 * KB, 8: W21_AT + 4 * KB}
+H_W_AT = {256: RELU_AT[9], 512: RELU_AT[14], 768: PROD_AT[14]}
 
 
 def tile_list_syntax_node_latency_kernel(tc, tab_words, tab_scales, offs, offs2, offs3, wp, wl_words, wl_scales,
@@ -50,10 +48,10 @@ def tile_list_syntax_node_latency_kernel(tc, tab_words, tab_scales, offs, offs2,
             return shared.tile(shape, dtype, name=name, align_bytes=64, offset=at)
 
         tab_sc = keep.tile([P, T], U8, name="tab_sc", align_bytes=64)
-        left_raw = placed([P, 2048], I32, "left_raw", LEFT_AT)
+        left_raw = placed([P, 768], I32, "left_raw", LEFT_AT)
         wl_raw = left_raw[:, 0:H // 2]
         wl_sc_raw = left_raw[:, H // 2:H // 2 + H // 4]
-        right_raw = placed([P, 2560], I32, "right_raw", RIGHT_AT)
+        right_raw = placed([P, 1280], I32, "right_raw", None)
         wr_raw = right_raw[:, 0:H]
         wr_sc_raw = right_raw[:, H:H + H // 4]
         nc.gpsimd.memset(wl_sc_raw, 0)
@@ -67,8 +65,8 @@ def tile_list_syntax_node_latency_kernel(tc, tab_words, tab_scales, offs, offs2,
         list_r = keep.tile([P, S // 16], U16, name="list_r")
         list_p = keep.tile([P, S // 16], U16, name="list_p")
         tab_w = keep.tile([P, T], I32, name="tab_w", align_bytes=64)
-        wp_raw = [placed([P, 4, 512], F32, "wp_raw%d" % g, WP_AT[g]) for g in range(G)]
-        w2_raw = [placed([P, 4, N], F32, "w2_raw%d" % g, W2_AT[g]) for g in range(G)]
+        wp_raw = [placed([P, 4, 512], F32, "wp_raw%d" % g, [None, WP1_AT][g]) for g in range(G)]
+        w2_raw = [placed([P, 4, N], F32, "w2_raw%d" % g, [H_AT, W21_AT][g]) for g in range(G)]
         bias = keep.tile([P, 4], F32, name="bias")
         wp_rows = wp.rearrange("(p i) (g r) -> g p i r", i=4, g=G)
         w2_rows = w2.rearrange("(g m t e) n -> g t m (e n)", g=G, t=4, e=4)
@@ -81,11 +79,11 @@ def tile_list_syntax_node_latency_kernel(tc, tab_words, tab_scales, offs, offs2,
         nc.sync.dma_start(wl_raw, wl_words[0].bitcast(I32))
         load_scale_rows(wl_sc_raw, wl_scales[0])
         nc.sync.dma_start(list_p[:], offs)
-        nc.sync.dma_start(list_r[:], offs3)
         nc.sync.dma_start(wp_raw[0][:], wp_rows[0])
+        nc.sync.dma_start(list_r[:], offs3)
+        nc.sync.dma_start(wp_raw[1][:], wp_rows[1])
         nc.sync.dma_start(wr_raw, wr_words[0].rearrange("p n t -> p (n t)").bitcast(I32))
         load_scale_rows(wr_sc_raw, wr_scales[0])
-        nc.sync.dma_start(wp_raw[1][:], wp_rows[1])
         for g in range(G):
             for t in range(4):
                 nc.sync.dma_start(w2_raw[g][:, t, :], w2_rows[g, t])
@@ -126,16 +124,20 @@ def tile_list_syntax_node_latency_kernel(tc, tab_words, tab_scales, offs, offs2,
 
         def cast_wp(g):
             wp_bf = placed([P, 2048], BF16, "wp_bf%d" % g, WP_BF_AT[g])
-            for t in range(4):
-                nc.gpsimd.tensor_scalar(wp_bf[:].rearrange("p (t m e i) -> p t m e i", t=4, e=4, i=4)[:, t],
-                                        wp_raw[g][:].rearrange("p i (m t e) -> p t m e i", t=4, e=4)[:, t],
-                                        1.0, 0.0, ALU.mult, ALU.add)
+            nc.gpsimd.tensor_scalar(wp_bf[:].rearrange("p (t m e i) -> p m t e i", t=4, e=4, i=4),
+                                    wp_raw[g][:].rearrange("p i (m t e) -> p m t e i", t=4, e=4), 1.0, 0.0, ALU.mult, ALU.add)
             return wp_bf[:]
 
-        def cast_w2(g, at, size):
-            w2_bf = placed([P, size * KB // 2], BF16, "w2_bf%d" % g, at)[:, 0:2048]
-            nc.scalar.copy(w2_bf.rearrange("p (u c t) -> p c t u", u=4, t=4), w2_raw[g][:].rearrange("p t (c u) -> p c t u", u=4))
-            return w2_bf
+        def cast_w2(g):
+            w2_bf = placed([P, 2048], BF16, "w2_bf%d" % g, W2_BF_AT[g])
+            dealt = w2_bf[:].rearrange("p (u c t) -> p c t u", u=4, t=4)
+            raw = w2_raw[g][:].rearrange("p t (c u) -> p c t u", u=4)
+            if g == 0:
+                nc.gpsimd.tensor_scalar(dealt.rearrange("p c t u -> p c u t"), raw.rearrange("p c t u -> p c u t"),
+                                        1.0, 0.0, ALU.mult, ALU.add)
+            else:
+                nc.scalar.copy(dealt, raw)
+            return w2_bf[:]
 
         banks = {reader: [psum.tile([P, 4, JT], F32, name="bank_%s%d" % (reader, b), bufs=1) for b in range(count)]
                  for reader, count in (("vector", 3), ("scalar", 3), ("wide", 2))}
@@ -162,9 +164,10 @@ def tile_list_syntax_node_latency_kernel(tc, tab_words, tab_scales, offs, offs2,
         gather_words("l", 0, 256)
         deal(wl_w[:], wl_raw, 2)
         deal_scales(wl_sc[:].bitcast(I32), wl_sc_raw)
-        gather_words("l", 256, 768, LEFT_AT)
-        gather_scales("p", 0, S, LEFT_AT + 3 * KB)
-        gather_words("p", 0, S, LEFT_AT + 4 * KB)
+        gather_words("l", 256, 768, 64)
+        gather_scales("p", 0, S, LEFT_AT + 64)
+        gather_scales("r", 0, S, LEFT_AT + KB + 64)
+        gather_words("p", 0, 512, LEFT_AT + 2 * KB + 64)
 
         def left(g, t):
             c = 512 * g + P * t
@@ -178,53 +181,41 @@ def tile_list_syntax_node_latency_kernel(tc, tab_words, tab_scales, offs, offs2,
             codes, plane = wp_q[g]
             return codes[:, P * t:P * t + P].bitcast(E4M3), plane[:, P * t:P * t + P]
 
-        relu_a = []
+        relu_a = {}
         prods = {}
         copied = {}
         h_tiles = {}
 
-        def rectify_left():
-            n = len(relu_a)
-            at, size = RELU_AT.get(n, (None, 2))
-            room = placed([P, size * KB // 4], F32, "relu_a%d" % n, at)
-            relu_a.append(room[:, 0:4 * JT].rearrange("p (j t) -> p j t", t=4))
-            nc.scalar.activation(relu_a[n], first_product(n, "l", left, "vector" if EARLY_RELUS - 3 <= n < EARLY_RELUS else "scalar"), ACT.Relu)
+        def unit_tile(store, places, name, n):
+            store[n] = placed([P, JT, 4], F32, "%s%d" % (name, n), places.get(n))
+            return store[n][:]
 
-        def room_for(store, places, name, n):
-            if n not in store:
-                at, size = places.get(n, (None, 2))
-                room = placed([P, size * KB // 4], F32, "%s%d" % (name, n), at)
-                store[n] = room[:, 0:4 * JT]
-                if n in PAIRS:
-                    store[PAIRS[n]] = room[:, 4 * JT:8 * JT]
-                    store[n, PAIRS[n]] = room[:, 0:8 * JT]
-            return store[n].rearrange("p (j t) -> p j t", t=4)
+        def rectify_left(n):
+            nc.scalar.activation(unit_tile(relu_a, RELU_AT, "relu_a", n),
+                                 first_product(n, "l", left, "vector" if n >= UNITS - 3 else "scalar"), ACT.Relu)
 
         def product(n):
-            nc.vector.scalar_tensor_tensor(room_for(prods, PROD_AT, "prod", n), first_product(n, "r", right, "vector"), 0.0,
-                                           relu_a[n], ALU.max, ALU.mult)
+            nc.vector.scalar_tensor_tensor(unit_tile(prods, PROD_AT, "prod", n), first_product(n, "r", right, "vector"), 0.0,
+                                           relu_a[n][:], ALU.max, ALU.mult)
 
         def copy_parent(n):
-            nc.scalar.copy(room_for(copied, P_SB_AT, "p_sb", n), first_product(n, "p", parent, "scalar"))
+            nc.scalar.copy(unit_tile(copied, P_SB_AT, "p_sb", n), first_product(n, "p", parent, "scalar"))
 
-        def open_h(j0, width, at, size=4):
-            room = placed([P, size * KB // 2], BF16, "h_bf%d" % j0, at)
-            h_tiles[j0] = (width, room[:, 0:G * width * 4])
+        def open_h(j0, width, at):
+            h_tiles[j0] = (width, placed([P, G * width * 4], BF16, "h_bf%d" % j0, at))
 
-        def h_part(n, units=1):
+        def h_part(n):
             jt, g = divmod(n, G)
             j0 = max(j for j in h_tiles if j <= jt * JT)
             width, h_bf = h_tiles[j0]
             at = 4 * (g * width + jt * JT - j0)
-            return h_bf[:, at:at + 4 * JT * units]
+            return h_bf[:, at:at + 4 * JT].rearrange("p (j t) -> p j t", t=4)
 
         def add_on_gpsimd(n):
-            key = (n, PAIRS[n]) if n in PAIRS else n
-            nc.gpsimd.tensor_tensor(h_part(n, 2 if n in PAIRS else 1), copied[key], prods[key], ALU.add)
+            nc.gpsimd.tensor_tensor(h_part(n), copied[n][:], prods[n][:], ALU.add)
 
         def add_on_vector(n):
-            nc.vector.tensor_tensor(h_part(n).rearrange("p (j t) -> p j t", t=4), first_product(n, "p", parent, "vector"),
-                                    prods[n].rearrange("p (j t) -> p j t", t=4), ALU.add)
+            nc.vector.tensor_tensor(h_part(n), first_product(n, "p", parent, "vector"), prods[n][:], ALU.add)
 
         y_sc = keep.tile([P, S], U8, name="y_sc", align_bytes=64)
         y_rows = out_0.rearrange("(p t) j -> p t j", t=4)
@@ -235,7 +226,7 @@ def tile_list_syntax_node_latency_kernel(tc, tab_words, tab_scales, offs, offs2,
             h_w = placed([P, G, width], U32, "h_w%d" % j0, H_W_AT.get(j0))
             h_sc = ring.tile([P, G, width], U8, name="h_sc", align_bytes=64)
             nc.vector.quantize_mx(out=h_w[:].rearrange("p g j -> p (g j)").bitcast(E4M3), scales=h_sc[:].rearrange("p g j -> p (g j)"),
-                                  in_=h_bf)
+                                  in_=h_bf[:])
             return h_w, h_sc
 
         def second_product(h_q, sums):
@@ -276,70 +267,63 @@ def tile_list_syntax_node_latency_kernel(tc, tab_words, tab_scales, offs, offs2,
                 queue = nc.sync if j1 < S or q % 2 == 0 else nc.scalar
                 queue.dma_start(out_2[0][4 * q:4 * q + 4, j0:j1].bitcast(I32), y_sc[32 * q:32 * q + 4, j0:j1].bitcast(I32))
 
-        for n in range(EARLY_RELUS):
-            rectify_left()
+        for n in range(UNITS):
+            rectify_left(n)
 
-        wp_bf = cast_wp(0)
-        wr_w = placed([P, H], I32, "wr_w", WP_AT[0])
-        wr_sc = placed([P, H], U8, "wr_sc", WP_AT[0] + 4 * KB)
+        wp_bf = [cast_wp(g) for g in range(G)]
+        wr_w = placed([P, H], I32, "wr_w", WP1_AT)
+        wr_sc = placed([P, H], U8, "wr_sc", WP1_AT + 4 * KB)
         deal(wr_w[:], wr_raw, 4)
         deal_scales(wr_sc[:].bitcast(I32), wr_sc_raw)
-        wp_q = [quantize(wp_bf, "wp0")]
-        gather_scales("r", 0, S, RIGHT_AT + 2 * KB)
-        gather_words("r", 0, 256, RIGHT_AT + 4 * KB)
-        gather_words("r", 256, 768, RIGHT_AT + 5 * KB)
-        copy_parent(0)
-        wp_bf = cast_wp(1)
-        product(0)
-        wp_q.append(quantize(wp_bf, "wp1"))
+        wp_q = [quantize(wp_bf[0], "wp0", WP1_AT + 5 * KB, WP1_AT + 7 * KB), quantize(wp_bf[1], "wp1")]
 
-        open_h(0, 256, WP_BF_AT[1])
-        w2_bf = [cast_w2(0, None, 4)]
-        copy_parent(2)
-        copy_parent(1)
-        w2_bf.append(cast_w2(1, 84 * KB, 10))
-        for n in (2, 1, 3, 4):
+        w2_bf = [cast_w2(0)]
+        gather_words("r", 0, 256, WP_BF_AT[0])
+        gather_words("p", 512, 512, WP_BF_AT[0] + KB)
+        for n in (0, 1, 2):
+            copy_parent(n)
+        w2_bf.append(cast_w2(1))
+        open_h(0, 256, H_AT)
+        product(0)
+        product(1)
+        gather_words("r", 256, 768, RELU_AT[0])
+        for n in (2, 3, 4):
             product(n)
         add_on_vector(3)
-        for n in (0, 2):
+        for n in (0, 1, 2):
             add_on_gpsimd(n)
-        for n in (6, 5):
-            product(n)
-        for n in (4, 6, 5):
+        for n in (4, 5, 6, 8, 9, 10, 12):
             copy_parent(n)
-        w2_q = [quantize(w2_bf[0], "w20", 44 * KB, 40 * KB)]
-        h_q = quantize_h(0)
-        w2_q.append(quantize(w2_bf[1], "w21", 46 * KB, 40 * KB + 512))
-        sums = second_product(h_q, wide_banks())
+        w2_q = [quantize(w2_bf[0], "w20", PROD_AT[2], RELU_AT[4]), quantize(w2_bf[1], "w21", P_SB_AT[2], RELU_AT[4] + 512)]
+        sums = second_product(quantize_h(0), wide_banks())
 
         open_h(256, 256, H_AT)
-        for n in (8, 12, 14):
-            copy_parent(n)
-        product(7)
-        product(8)
+        for n in (5, 6, 7, 8):
+            product(n)
         add_on_vector(7)
-        for n in (4, 6):
+        for n in (4, 5, 6):
             add_on_gpsimd(n)
         cast_y(0, 256, add_bias(0, 256, sums, ()), nc.scalar.copy)
-        for n in (10, 9, 11, 12):
+        for n in (9, 10):
             product(n)
         sums = second_product(quantize_h(256), wide_banks())
 
         open_h(512, 256, H_AT)
-        add_on_gpsimd(8)
-        for n in (9, 10, 11):
-            add_on_vector(n)
+        for n in (11, 12, 13):
+            product(n)
+        add_on_vector(11)
+        for n in (8, 9, 10):
+            add_on_gpsimd(n)
         cast_y(256, 256, add_bias(256, 256, sums, ()), nc.scalar.copy)
+        for n in (14, 15):
+            product(n)
         sums = second_product(quantize_h(512), wide_banks("scalar"))
 
-        open_h(768, JT, H_AT, 2)
-        open_h(896, JT, H_AT + 2 * KB, 2)
-        for n in (14, 13, 15):
-            product(n)
+        open_h(768, JT, H_AT)
+        open_h(896, JT, H_AT + 2 * KB)
         add_on_gpsimd(12)
-        add_on_gpsimd(14)
-        add_on_vector(13)
-        add_on_vector(15)
+        for n in (13, 14, 15):
+            add_on_vector(n)
         cast_y(512, 256, add_bias(512, 256, sums, ()), nc.scalar.copy)
         bank = next_bank("wide")
         sums = second_product(quantize_h(768), [bank[:, t, :] for t in range(4)])

@@ -21,16 +21,20 @@ G = H // 512
 JT = 128
 KB = 1024
 UNITS = G * S // JT
-LEFT_AT = 3 * KB
+LEFT_SC_AT = 64 * KB
+LEFT_W_AT = 69 * KB
+LEFT_AT = 72 * KB - 64
+RIGHT_AT = 0
 WP1_AT = 8 * KB
-WP_BF_AT = [16 * KB, 20 * KB]
-W2_BF_AT = [20 * KB, 24 * KB]
+WP_BF_AT = [65 * KB, 20 * KB]
+W2_BF_AT = [RIGHT_AT, 26 * KB]
 W21_AT = 38 * KB
 H_AT = 46 * KB
-RELU_AT = {0: 28 * KB, 4: 36 * KB, 9: 54 * KB, 14: 56 * KB}
-PROD_AT = {2: 32 * KB, 5: 24 * KB, 6: 26 * KB, 7: 20 * KB, 14: 58 * KB}
-P_SB_AT = {2: 34 * KB, 5: W21_AT, 6: W21_AT + 2 * KB, 8: W21_AT + 4 * KB}
-H_W_AT = {256: RELU_AT[9], 512: RELU_AT[14], 768: PROD_AT[14]}
+RELU_AT = {6: 36 * KB, 11: 54 * KB}
+PROD_AT = {2: 32 * KB, 7: RIGHT_AT, 8: 26 * KB, 10: 28 * KB, 11: 56 * KB, 13: 56 * KB, 9: 58 * KB, 14: 58 * KB, 15: 60 * KB}
+P_SB_AT = {4: W21_AT, 6: W21_AT + 2 * KB, 8: 60 * KB}
+H_W_AT = {256: RELU_AT[11]}
+RUNS = [(0,), (2, 1), (4,), (6, 5), (8,), (12,), (14,)]
 
 
 def tile_list_syntax_node_latency_kernel(tc, tab_words, tab_scales, offs, offs2, offs3, wp, wl_words, wl_scales,
@@ -51,9 +55,10 @@ def tile_list_syntax_node_latency_kernel(tc, tab_words, tab_scales, offs, offs2,
         left_raw = placed([P, 768], I32, "left_raw", LEFT_AT)
         wl_raw = left_raw[:, 0:H // 2]
         wl_sc_raw = left_raw[:, H // 2:H // 2 + H // 4]
-        right_raw = placed([P, 1280], I32, "right_raw", None)
+        right_raw = placed([P, 1280], I32, "right_raw", RIGHT_AT)
         wr_raw = right_raw[:, 0:H]
         wr_sc_raw = right_raw[:, H:H + H // 4]
+        nc.gpsimd.memset(tab_sc[:].bitcast(I32), 0)
         nc.gpsimd.memset(wl_sc_raw, 0)
         nc.gpsimd.memset(wr_sc_raw, 0)
 
@@ -72,15 +77,13 @@ def tile_list_syntax_node_latency_kernel(tc, tab_words, tab_scales, offs, offs2,
         w2_rows = w2.rearrange("(g m t e) n -> g t m (e n)", g=G, t=4, e=4)
 
         nc.sync.dma_start(list_l[:], offs2)
-        for q in range(4):
-            nc.sync.dma_start(tab_sc[:].bitcast(I32)[32 * q:32 * q + 32, :],
-                              tab_scales[0][4 * q:4 * q + 4, :].bitcast(I32).unsqueeze(0).to_broadcast([8, 4, T // 4]))
+        nc.sync.dma_start(list_r[:], offs3)
+        nc.sync.dma_start(list_p[:], offs)
+        load_scale_rows(tab_sc[:].bitcast(I32), tab_scales[0])
         nc.sync.dma_start(tab_w[:], tab_words[0].rearrange("p n t -> p (n t)").bitcast(I32))
         nc.sync.dma_start(wl_raw, wl_words[0].bitcast(I32))
         load_scale_rows(wl_sc_raw, wl_scales[0])
-        nc.sync.dma_start(list_p[:], offs)
         nc.sync.dma_start(wp_raw[0][:], wp_rows[0])
-        nc.sync.dma_start(list_r[:], offs3)
         nc.sync.dma_start(wp_raw[1][:], wp_rows[1])
         nc.sync.dma_start(wr_raw, wr_words[0].rearrange("p n t -> p (n t)").bitcast(I32))
         load_scale_rows(wr_sc_raw, wr_scales[0])
@@ -108,13 +111,13 @@ def tile_list_syntax_node_latency_kernel(tc, tab_words, tab_scales, offs, offs2,
             j0, width, got = [piece for piece in store[side] if piece[0] <= j < piece[0] + piece[1]][0]
             return got[:, j - j0:j - j0 + JT]
 
-        def deal(dealt, raw, run):
-            nc.vector.tensor_copy(dealt.rearrange("p (g t m e) -> p g t m e", g=G, t=4, e=run),
-                                  raw.rearrange("p (g m t e) -> p g t m e", g=G, t=4, e=run))
+        def deal(engine, dealt, raw, run):
+            engine.tensor_copy(dealt.rearrange("p (g t m e) -> p g t m e", g=G, t=4, e=run),
+                               raw.rearrange("p (g m t e) -> p g t m e", g=G, t=4, e=run))
 
-        def deal_scales(dealt, raw):
-            nc.vector.tensor_copy(dealt.rearrange("p (g t c i) -> p g c t i", g=G, t=4, i=4),
-                                  raw.rearrange("p (g c i t) -> p g c t i", g=G, t=4, i=4))
+        def deal_scales(engine, dealt, raw):
+            engine.tensor_copy(dealt.rearrange("p (g t c i) -> p g c t i", g=G, t=4, i=4),
+                               raw.rearrange("p (g c i t) -> p g c t i", g=G, t=4, i=4))
 
         def quantize(grouped, name, codes_at=None, plane_at=None):
             codes = placed([P, 512], U32, name + "_w", codes_at)
@@ -160,14 +163,13 @@ def tile_list_syntax_node_latency_kernel(tc, tab_words, tab_scales, offs, offs2,
 
         wl_w = keep.tile([P, H // 2], I32, name="wl_w", align_bytes=64)
         wl_sc = keep.tile([P, H], U8, name="wl_sc", align_bytes=64)
-        gather_scales("l", 0, S)
+        gather_scales("l", 0, S, LEFT_SC_AT)
         gather_words("l", 0, 256)
-        deal(wl_w[:], wl_raw, 2)
-        deal_scales(wl_sc[:].bitcast(I32), wl_sc_raw)
-        gather_words("l", 256, 768, 64)
+        deal(nc.vector, wl_w[:], wl_raw, 2)
+        deal_scales(nc.vector, wl_sc[:].bitcast(I32), wl_sc_raw)
+        gather_words("l", 256, 768, LEFT_W_AT)
         gather_scales("p", 0, S, LEFT_AT + 64)
-        gather_scales("r", 0, S, LEFT_AT + KB + 64)
-        gather_words("p", 0, 512, LEFT_AT + 2 * KB + 64)
+        gather_words("p", 0, S, LEFT_AT + KB + 64)
 
         def left(g, t):
             c = 512 * g + P * t
@@ -186,36 +188,40 @@ def tile_list_syntax_node_latency_kernel(tc, tab_words, tab_scales, offs, offs2,
         copied = {}
         h_tiles = {}
 
-        def unit_tile(store, places, name, n):
-            store[n] = placed([P, JT, 4], F32, "%s%d" % (name, n), places.get(n))
-            return store[n][:]
+        def unit_tile(store, places, name, n, runs):
+            run = ([run for run in runs if n in run] + [(n,)])[0]
+            if run not in store:
+                store[run] = placed([P, len(run) * JT, 4], F32, "%s%d" % (name, n), places.get(run[0]))[:]
+                for i, m in enumerate(run):
+                    store[m] = store[run][:, i * JT:(i + 1) * JT, :]
+            return store[n]
 
         def rectify_left(n):
-            nc.scalar.activation(unit_tile(relu_a, RELU_AT, "relu_a", n),
-                                 first_product(n, "l", left, "vector" if n >= UNITS - 3 else "scalar"), ACT.Relu)
+            nc.scalar.activation(unit_tile(relu_a, RELU_AT, "relu_a", n, []),
+                                 first_product(n, "l", left, "scalar"), ACT.Relu)
 
         def product(n):
-            nc.vector.scalar_tensor_tensor(unit_tile(prods, PROD_AT, "prod", n), first_product(n, "r", right, "vector"), 0.0,
-                                           relu_a[n][:], ALU.max, ALU.mult)
+            nc.vector.scalar_tensor_tensor(unit_tile(prods, PROD_AT, "prod", n, RUNS), first_product(n, "r", right, "vector"), 0.0,
+                                           relu_a[n], ALU.max, ALU.mult)
 
         def copy_parent(n):
-            nc.scalar.copy(unit_tile(copied, P_SB_AT, "p_sb", n), first_product(n, "p", parent, "scalar"))
+            nc.scalar.copy(unit_tile(copied, P_SB_AT, "p_sb", n, RUNS), first_product(n, "p", parent, "scalar"))
 
         def open_h(j0, width, at):
             h_tiles[j0] = (width, placed([P, G * width * 4], BF16, "h_bf%d" % j0, at))
 
-        def h_part(n):
+        def h_part(n, units=1):
             jt, g = divmod(n, G)
             j0 = max(j for j in h_tiles if j <= jt * JT)
             width, h_bf = h_tiles[j0]
             at = 4 * (g * width + jt * JT - j0)
-            return h_bf[:, at:at + 4 * JT].rearrange("p (j t) -> p j t", t=4)
+            return h_bf[:, at:at + 4 * JT * units].rearrange("p (j t) -> p j t", t=4)
 
-        def add_on_gpsimd(n):
-            nc.gpsimd.tensor_tensor(h_part(n), copied[n][:], prods[n][:], ALU.add)
+        def add_on_gpsimd(run):
+            nc.gpsimd.tensor_tensor(h_part(run[0], len(run)), copied[run], prods[run], ALU.add)
 
         def add_on_vector(n):
-            nc.vector.tensor_tensor(h_part(n), first_product(n, "p", parent, "vector"), prods[n][:], ALU.add)
+            nc.vector.tensor_tensor(h_part(n), first_product(n, "p", parent, "vector"), prods[n], ALU.add)
 
         y_sc = keep.tile([P, S], U8, name="y_sc", align_bytes=64)
         y_rows = out_0.rearrange("(p t) j -> p t j", t=4)
@@ -271,59 +277,58 @@ def tile_list_syntax_node_latency_kernel(tc, tab_words, tab_scales, offs, offs2,
             rectify_left(n)
 
         wp_bf = [cast_wp(g) for g in range(G)]
-        wr_w = placed([P, H], I32, "wr_w", WP1_AT)
-        wr_sc = placed([P, H], U8, "wr_sc", WP1_AT + 4 * KB)
-        deal(wr_w[:], wr_raw, 4)
-        deal_scales(wr_sc[:].bitcast(I32), wr_sc_raw)
-        wp_q = [quantize(wp_bf[0], "wp0", WP1_AT + 5 * KB, WP1_AT + 7 * KB), quantize(wp_bf[1], "wp1")]
-
+        wp_q = [quantize(wp_bf[0], "wp0", WP1_AT, WP1_AT + 2 * KB), quantize(wp_bf[1], "wp1")]
+        wr_w = placed([P, H], I32, "wr_w", WP_BF_AT[1] - 512)
+        wr_sc = placed([P, H], U8, "wr_sc", WP_BF_AT[1] + 4 * KB - 512)
+        deal(nc.gpsimd, wr_w[:], wr_raw, 4)
+        deal_scales(nc.gpsimd, wr_sc[:].bitcast(I32), wr_sc_raw)
         w2_bf = [cast_w2(0)]
-        gather_words("r", 0, 256, WP_BF_AT[0])
-        gather_words("p", 512, 512, WP_BF_AT[0] + KB)
-        for n in (0, 1, 2):
+        gather_scales("r", 0, S, LEFT_W_AT - 512 - KB)
+        for n in (0, 2, 1):
             copy_parent(n)
+        gather_words("r", 0, 256, LEFT_W_AT - 512)
+        gather_words("r", 256, 768, LEFT_SC_AT + 512)
         w2_bf.append(cast_w2(1))
         open_h(0, 256, H_AT)
-        product(0)
-        product(1)
-        gather_words("r", 256, 768, RELU_AT[0])
-        for n in (2, 3, 4):
+        for n in (0, 2, 1, 3, 4):
             product(n)
         add_on_vector(3)
-        for n in (0, 1, 2):
-            add_on_gpsimd(n)
-        for n in (4, 5, 6, 8, 9, 10, 12):
+        for run in RUNS[0:2]:
+            add_on_gpsimd(run)
+        for n, m in ((6, 4), (5, 6)):
+            product(n)
+            copy_parent(m)
+        for n in (5, 8, 12, 14):
             copy_parent(n)
-        w2_q = [quantize(w2_bf[0], "w20", PROD_AT[2], RELU_AT[4]), quantize(w2_bf[1], "w21", P_SB_AT[2], RELU_AT[4] + 512)]
+        w2_q = [quantize(w2_bf[g], "w2%d" % g, PROD_AT[2] + 2 * KB * g, RELU_AT[6] + 512 * g) for g in range(G)]
         sums = second_product(quantize_h(0), wide_banks())
 
         open_h(256, 256, H_AT)
-        for n in (5, 6, 7, 8):
+        for n in (7, 8, 10):
             product(n)
         add_on_vector(7)
-        for n in (4, 5, 6):
-            add_on_gpsimd(n)
+        for run in RUNS[2:4]:
+            add_on_gpsimd(run)
         cast_y(0, 256, add_bias(0, 256, sums, ()), nc.scalar.copy)
-        for n in (9, 10):
+        for n in (9, 11, 12):
             product(n)
         sums = second_product(quantize_h(256), wide_banks())
 
         open_h(512, 256, H_AT)
-        for n in (11, 12, 13):
-            product(n)
-        add_on_vector(11)
-        for n in (8, 9, 10):
-            add_on_gpsimd(n)
+        add_on_gpsimd(RUNS[4])
+        for n in (9, 10, 11):
+            add_on_vector(n)
         cast_y(256, 256, add_bias(256, 256, sums, ()), nc.scalar.copy)
-        for n in (14, 15):
-            product(n)
         sums = second_product(quantize_h(512), wide_banks("scalar"))
 
         open_h(768, JT, H_AT)
         open_h(896, JT, H_AT + 2 * KB)
-        add_on_gpsimd(12)
-        for n in (13, 14, 15):
-            add_on_vector(n)
+        for n in (14, 13, 15):
+            product(n)
+        for run in RUNS[5:7]:
+            add_on_gpsimd(run)
+        add_on_vector(13)
+        add_on_vector(15)
         cast_y(512, 256, add_bias(512, 256, sums, ()), nc.scalar.copy)
         bank = next_bank("wide")
         sums = second_product(quantize_h(768), [bank[:, t, :] for t in range(4)])

@@ -30,7 +30,7 @@ WP_BF_AT = [65 * KB, 20 * KB]
 W2_BF_AT = [RIGHT_AT, 26 * KB]
 W21_AT = 38 * KB
 H_AT = 46 * KB
-RELU_AT = {6: 36 * KB, 11: 54 * KB}
+RELU_AT = {0: 26 * KB, 6: 36 * KB, 11: 54 * KB}
 PROD_AT = {2: 32 * KB, 7: RIGHT_AT, 8: 26 * KB, 10: 28 * KB, 11: 56 * KB, 13: 56 * KB, 9: 58 * KB, 14: 58 * KB, 15: 60 * KB}
 P_SB_AT = {4: W21_AT, 6: W21_AT + 2 * KB, 8: 60 * KB}
 H_W_AT = {256: RELU_AT[11]}
@@ -84,9 +84,9 @@ def tile_list_syntax_node_latency_kernel(tc, tab_words, tab_scales, offs, offs2,
         nc.sync.dma_start(wl_raw, wl_words[0].bitcast(I32))
         load_scale_rows(wl_sc_raw, wl_scales[0])
         nc.sync.dma_start(wp_raw[0][:], wp_rows[0])
-        nc.sync.dma_start(wp_raw[1][:], wp_rows[1])
         nc.sync.dma_start(wr_raw, wr_words[0].rearrange("p n t -> p (n t)").bitcast(I32))
         load_scale_rows(wr_sc_raw, wr_scales[0])
+        nc.sync.dma_start(wp_raw[1][:], wp_rows[1])
         for g in range(G):
             for t in range(4):
                 nc.sync.dma_start(w2_raw[g][:, t, :], w2_rows[g, t])
@@ -133,13 +133,7 @@ def tile_list_syntax_node_latency_kernel(tc, tab_words, tab_scales, offs, offs2,
 
         def cast_w2(g):
             w2_bf = placed([P, 2048], BF16, "w2_bf%d" % g, W2_BF_AT[g])
-            dealt = w2_bf[:].rearrange("p (u c t) -> p c t u", u=4, t=4)
-            raw = w2_raw[g][:].rearrange("p t (c u) -> p c t u", u=4)
-            if g == 0:
-                nc.gpsimd.tensor_scalar(dealt.rearrange("p c t u -> p c u t"), raw.rearrange("p c t u -> p c u t"),
-                                        1.0, 0.0, ALU.mult, ALU.add)
-            else:
-                nc.scalar.copy(dealt, raw)
+            nc.scalar.copy(w2_bf[:].rearrange("p (u c t) -> p c t u", u=4, t=4), w2_raw[g][:].rearrange("p t (c u) -> p c t u", u=4))
             return w2_bf[:]
 
         banks = {reader: [psum.tile([P, 4, JT], F32, name="bank_%s%d" % (reader, b), bufs=1) for b in range(count)]
@@ -169,7 +163,8 @@ def tile_list_syntax_node_latency_kernel(tc, tab_words, tab_scales, offs, offs2,
         deal_scales(nc.vector, wl_sc[:].bitcast(I32), wl_sc_raw)
         gather_words("l", 256, 768, LEFT_W_AT)
         gather_scales("p", 0, S, LEFT_AT + 64)
-        gather_words("p", 0, S, LEFT_AT + KB + 64)
+        gather_scales("r", 0, S, LEFT_AT + KB + 64)
+        gather_words("p", 0, S, LEFT_AT + 2 * KB + 64)
 
         def left(g, t):
             c = 512 * g + P * t
@@ -276,18 +271,18 @@ def tile_list_syntax_node_latency_kernel(tc, tab_words, tab_scales, offs, offs2,
         for n in range(UNITS):
             rectify_left(n)
 
-        wp_bf = [cast_wp(g) for g in range(G)]
-        wp_q = [quantize(wp_bf[0], "wp0", WP1_AT, WP1_AT + 2 * KB), quantize(wp_bf[1], "wp1")]
-        wr_w = placed([P, H], I32, "wr_w", WP_BF_AT[1] - 512)
-        wr_sc = placed([P, H], U8, "wr_sc", WP_BF_AT[1] + 4 * KB - 512)
+        wp_bf = [cast_wp(0)]
+        wr_w = placed([P, H], I32, "wr_w", None)
+        wr_sc = placed([P, H], U8, "wr_sc", None)
         deal(nc.gpsimd, wr_w[:], wr_raw, 4)
         deal_scales(nc.gpsimd, wr_sc[:].bitcast(I32), wr_sc_raw)
-        w2_bf = [cast_w2(0)]
-        gather_scales("r", 0, S, LEFT_W_AT - 512 - KB)
-        for n in (0, 2, 1):
-            copy_parent(n)
+        wp_bf.append(cast_wp(1))
+        wp_q = [quantize(wp_bf[0], "wp0", WP1_AT, WP1_AT + 2 * KB), quantize(wp_bf[1], "wp1")]
         gather_words("r", 0, 256, LEFT_W_AT - 512)
         gather_words("r", 256, 768, LEFT_SC_AT + 512)
+        w2_bf = [cast_w2(0)]
+        for n in (0, 2, 1):
+            copy_parent(n)
         w2_bf.append(cast_w2(1))
         open_h(0, 256, H_AT)
         for n in (0, 2, 1, 3, 4):

@@ -21,20 +21,18 @@ G = H // 512
 JT = 128
 KB = 1024
 UNITS = G * S // JT
-LEFT_SC_AT = 64 * KB
-LEFT_W_AT = 69 * KB
-LEFT_AT = 72 * KB - 64
-RIGHT_AT = 0
+EARLY_RELUS = 12
 WP1_AT = 8 * KB
-WP_BF_AT = [65 * KB, 20 * KB]
-W2_BF_AT = [RIGHT_AT, 26 * KB]
+RIGHT_AT = KB
+WP_BF_AT = [84 * KB, RIGHT_AT]
+W2_BF_AT = [22 * KB, 26 * KB]
 W21_AT = 38 * KB
-H_AT = 46 * KB
-RELU_AT = {0: 26 * KB, 6: 36 * KB, 11: 54 * KB}
-PROD_AT = {2: 32 * KB, 7: RIGHT_AT, 8: 26 * KB, 10: 28 * KB, 11: 56 * KB, 13: 56 * KB, 9: 58 * KB, 14: 58 * KB, 15: 60 * KB}
-P_SB_AT = {4: W21_AT, 6: W21_AT + 2 * KB, 8: 60 * KB}
+H_AT = WP_BF_AT[1]
+RELU_AT = {6: 36 * KB, 11: 54 * KB}
+PROD_AT = {0: WP1_AT, 2: WP1_AT + 2 * KB, 1: WP1_AT + 4 * KB, 7: W2_BF_AT[0], 8: 26 * KB, 10: 28 * KB, 11: 56 * KB, 13: 56 * KB, 9: 58 * KB, 14: 58 * KB, 15: 60 * KB}
+P_SB_AT = {1: 32 * KB, 4: W21_AT, 6: W21_AT + 2 * KB, 8: 60 * KB}
 H_W_AT = {256: RELU_AT[11]}
-RUNS = [(0,), (2, 1), (4,), (6, 5), (8,), (12,), (14,)]
+RUNS = [(0,), (2,), (1,), (4,), (6, 5), (8,), (12,), (14,)]
 
 
 def tile_list_syntax_node_latency_kernel(tc, tab_words, tab_scales, offs, offs2, offs3, wp, wl_words, wl_scales,
@@ -52,7 +50,7 @@ def tile_list_syntax_node_latency_kernel(tc, tab_words, tab_scales, offs, offs2,
             return shared.tile(shape, dtype, name=name, align_bytes=64, offset=at)
 
         tab_sc = keep.tile([P, T], U8, name="tab_sc", align_bytes=64)
-        left_raw = placed([P, 768], I32, "left_raw", LEFT_AT)
+        left_raw = placed([P, 768], I32, "left_raw", None)
         wl_raw = left_raw[:, 0:H // 2]
         wl_sc_raw = left_raw[:, H // 2:H // 2 + H // 4]
         right_raw = placed([P, 1280], I32, "right_raw", RIGHT_AT)
@@ -71,16 +69,17 @@ def tile_list_syntax_node_latency_kernel(tc, tab_words, tab_scales, offs, offs2,
         list_p = keep.tile([P, S // 16], U16, name="list_p")
         tab_w = keep.tile([P, T], I32, name="tab_w", align_bytes=64)
         wp_raw = [placed([P, 4, 512], F32, "wp_raw%d" % g, [None, WP1_AT][g]) for g in range(G)]
-        w2_raw = [placed([P, 4, N], F32, "w2_raw%d" % g, [H_AT, W21_AT][g]) for g in range(G)]
+        w2_raw = [placed([P, 4, N], F32, "w2_raw%d" % g, [None, W21_AT][g]) for g in range(G)]
         bias = keep.tile([P, 4], F32, name="bias")
         wp_rows = wp.rearrange("(p i) (g r) -> g p i r", i=4, g=G)
         w2_rows = w2.rearrange("(g m t e) n -> g t m (e n)", g=G, t=4, e=4)
 
         nc.sync.dma_start(list_l[:], offs2)
         nc.sync.dma_start(list_r[:], offs3)
-        nc.sync.dma_start(list_p[:], offs)
+        nc.sync.dma_start(bias[:], b2.rearrange("(p t) -> p t", t=4))
         load_scale_rows(tab_sc[:].bitcast(I32), tab_scales[0])
         nc.sync.dma_start(tab_w[:], tab_words[0].rearrange("p n t -> p (n t)").bitcast(I32))
+        nc.sync.dma_start(list_p[:], offs)
         nc.sync.dma_start(wl_raw, wl_words[0].bitcast(I32))
         load_scale_rows(wl_sc_raw, wl_scales[0])
         nc.sync.dma_start(wp_raw[0][:], wp_rows[0])
@@ -90,7 +89,6 @@ def tile_list_syntax_node_latency_kernel(tc, tab_words, tab_scales, offs, offs2,
         for g in range(G):
             for t in range(4):
                 nc.sync.dma_start(w2_raw[g][:, t, :], w2_rows[g, t])
-        nc.sync.dma_start(bias[:], b2.rearrange("(p t) -> p t", t=4))
 
         lists = {"l": list_l, "r": list_r, "p": list_p}
         got_words = {"l": [], "r": [], "p": []}
@@ -157,14 +155,14 @@ def tile_list_syntax_node_latency_kernel(tc, tab_words, tab_scales, offs, offs2,
 
         wl_w = keep.tile([P, H // 2], I32, name="wl_w", align_bytes=64)
         wl_sc = keep.tile([P, H], U8, name="wl_sc", align_bytes=64)
-        gather_scales("l", 0, S, LEFT_SC_AT)
-        gather_words("l", 0, 256)
-        deal(nc.vector, wl_w[:], wl_raw, 2)
-        deal_scales(nc.vector, wl_sc[:].bitcast(I32), wl_sc_raw)
-        gather_words("l", 256, 768, LEFT_W_AT)
-        gather_scales("p", 0, S, LEFT_AT + 64)
-        gather_scales("r", 0, S, LEFT_AT + KB + 64)
-        gather_words("p", 0, S, LEFT_AT + 2 * KB + 64)
+        gather_scales("l", 0, 768, W2_BF_AT[1] - 384)
+        gather_scales("l", 768, 256)
+        gather_words("l", 0, 512)
+        deal(nc.gpsimd, wl_w[:], wl_raw, 2)
+        deal_scales(nc.gpsimd, wl_sc[:].bitcast(I32), wl_sc_raw)
+        gather_words("l", 512, 512)
+        gather_scales("p", 0, S)
+        gather_words("p", 0, 768)
 
         def left(g, t):
             c = 512 * g + P * t
@@ -268,49 +266,57 @@ def tile_list_syntax_node_latency_kernel(tc, tab_words, tab_scales, offs, offs2,
                 queue = nc.sync if j1 < S or q % 2 == 0 else nc.scalar
                 queue.dma_start(out_2[0][4 * q:4 * q + 4, j0:j1].bitcast(I32), y_sc[32 * q:32 * q + 4, j0:j1].bitcast(I32))
 
-        for n in range(UNITS):
+        for n in range(EARLY_RELUS):
             rectify_left(n)
 
         wp_bf = [cast_wp(0)]
-        wr_w = placed([P, H], I32, "wr_w", None)
+        wr_w = placed([P, H], I32, "wr_w", WP_BF_AT[0] + 256 - 4 * KB)
         wr_sc = placed([P, H], U8, "wr_sc", None)
-        deal(nc.gpsimd, wr_w[:], wr_raw, 4)
         deal_scales(nc.gpsimd, wr_sc[:].bitcast(I32), wr_sc_raw)
+        wp_q = [quantize(wp_bf[0], "wp0")]
+        deal(nc.gpsimd, wr_w[:], wr_raw, 4)
         wp_bf.append(cast_wp(1))
-        wp_q = [quantize(wp_bf[0], "wp0", WP1_AT, WP1_AT + 2 * KB), quantize(wp_bf[1], "wp1")]
-        gather_words("r", 0, 256, LEFT_W_AT - 512)
-        gather_words("r", 256, 768, LEFT_SC_AT + 512)
+        gather_scales("r", 0, S, WP_BF_AT[0] + 256)
+        gather_words("p", 768, 256, WP_BF_AT[0] + 256 + KB)
+        copy_parent(0)
         w2_bf = [cast_w2(0)]
-        for n in (0, 2, 1):
-            copy_parent(n)
+        gather_words("r", 0, 256, WP_BF_AT[0] + 256 + 2 * KB)
+        gather_words("r", 256, 768, WP_BF_AT[0] + 256 + 3 * KB)
+        wp_q.append(quantize(wp_bf[1], "wp1"))
+        copy_parent(2)
         w2_bf.append(cast_w2(1))
+        copy_parent(1)
         open_h(0, 256, H_AT)
         for n in (0, 2, 1, 3, 4):
             product(n)
         add_on_vector(3)
-        for run in RUNS[0:2]:
+        for run in RUNS[0:3]:
             add_on_gpsimd(run)
         for n, m in ((6, 4), (5, 6)):
             product(n)
             copy_parent(m)
-        for n in (5, 8, 12, 14):
+        for n in (5, 8):
             copy_parent(n)
-        w2_q = [quantize(w2_bf[g], "w2%d" % g, PROD_AT[2] + 2 * KB * g, RELU_AT[6] + 512 * g) for g in range(G)]
+        for n in range(EARLY_RELUS, UNITS):
+            rectify_left(n)
+        w2_q = [quantize(w2_bf[g], "w2%d" % g, [PROD_AT[1], P_SB_AT[1]][g], RELU_AT[6] + 512 * g) for g in range(G)]
         sums = second_product(quantize_h(0), wide_banks())
 
         open_h(256, 256, H_AT)
         for n in (7, 8, 10):
             product(n)
         add_on_vector(7)
-        for run in RUNS[2:4]:
+        for run in RUNS[3:5]:
             add_on_gpsimd(run)
         cast_y(0, 256, add_bias(0, 256, sums, ()), nc.scalar.copy)
+        for n in (12, 14):
+            copy_parent(n)
         for n in (9, 11, 12):
             product(n)
         sums = second_product(quantize_h(256), wide_banks())
 
         open_h(512, 256, H_AT)
-        add_on_gpsimd(RUNS[4])
+        add_on_gpsimd(RUNS[5])
         for n in (9, 10, 11):
             add_on_vector(n)
         cast_y(256, 256, add_bias(256, 256, sums, ()), nc.scalar.copy)
@@ -320,7 +326,7 @@ def tile_list_syntax_node_latency_kernel(tc, tab_words, tab_scales, offs, offs2,
         open_h(896, JT, H_AT + 2 * KB)
         for n in (14, 13, 15):
             product(n)
-        for run in RUNS[5:7]:
+        for run in RUNS[6:8]:
             add_on_gpsimd(run)
         add_on_vector(13)
         add_on_vector(15)

@@ -21,18 +21,18 @@ G = H // 512
 JT = 128
 KB = 1024
 UNITS = G * S // JT
-EARLY_RELUS = 12
+EARLY_RELUS = 13
 WP1_AT = 8 * KB
 RIGHT_AT = KB
 WP_BF_AT = [84 * KB, RIGHT_AT]
 W2_BF_AT = [22 * KB, 26 * KB]
 W21_AT = 38 * KB
 H_AT = WP_BF_AT[1]
-RELU_AT = {6: 36 * KB, 11: 54 * KB}
-PROD_AT = {0: WP1_AT, 2: WP1_AT + 2 * KB, 1: WP1_AT + 4 * KB, 7: W2_BF_AT[0], 8: 26 * KB, 10: 28 * KB, 11: 56 * KB, 13: 56 * KB, 9: 58 * KB, 14: 58 * KB, 15: 60 * KB}
-P_SB_AT = {1: 32 * KB, 4: W21_AT, 6: W21_AT + 2 * KB, 8: 60 * KB}
+RELU_AT = {2: W2_BF_AT[1], 6: 36 * KB, 11: 54 * KB}
+PROD_AT = {0: WP1_AT, 2: WP1_AT + 2 * KB, 7: W2_BF_AT[0], 8: 26 * KB, 10: 28 * KB, 11: 56 * KB, 13: 56 * KB, 9: 58 * KB, 14: 58 * KB, 15: 60 * KB}
+P_SB_AT = {4: W21_AT, 6: W21_AT + 2 * KB, 8: 60 * KB}
 H_W_AT = {256: RELU_AT[11]}
-RUNS = [(0,), (2,), (1,), (4,), (6, 5), (8,), (12,), (14,)]
+RUNS = [(0,), (2, 1), (4,), (6, 5), (8,), (12,), (14,)]
 
 
 def tile_list_syntax_node_latency_kernel(tc, tab_words, tab_scales, offs, offs2, offs3, wp, wl_words, wl_scales,
@@ -155,7 +155,7 @@ def tile_list_syntax_node_latency_kernel(tc, tab_words, tab_scales, offs, offs2,
 
         wl_w = keep.tile([P, H // 2], I32, name="wl_w", align_bytes=64)
         wl_sc = keep.tile([P, H], U8, name="wl_sc", align_bytes=64)
-        gather_scales("l", 0, 768, W2_BF_AT[1] - 384)
+        gather_scales("l", 0, 768, W2_BF_AT[0])
         gather_scales("l", 768, 256)
         gather_words("l", 0, 512)
         deal(nc.gpsimd, wl_w[:], wl_raw, 2)
@@ -197,8 +197,8 @@ def tile_list_syntax_node_latency_kernel(tc, tab_words, tab_scales, offs, offs2,
             nc.vector.scalar_tensor_tensor(unit_tile(prods, PROD_AT, "prod", n, RUNS), first_product(n, "r", right, "vector"), 0.0,
                                            relu_a[n], ALU.max, ALU.mult)
 
-        def copy_parent(n):
-            nc.scalar.copy(unit_tile(copied, P_SB_AT, "p_sb", n, RUNS), first_product(n, "p", parent, "scalar"))
+        def copy_parent(n, reader="scalar"):
+            nc.scalar.copy(unit_tile(copied, P_SB_AT, "p_sb", n, RUNS), first_product(n, "p", parent, reader))
 
         def open_h(j0, width, at):
             h_tiles[j0] = (width, placed([P, G * width * 4], BF16, "h_bf%d" % j0, at))
@@ -284,13 +284,13 @@ def tile_list_syntax_node_latency_kernel(tc, tab_words, tab_scales, offs, offs2,
         gather_words("r", 256, 768, WP_BF_AT[0] + 256 + 3 * KB)
         wp_q.append(quantize(wp_bf[1], "wp1"))
         copy_parent(2)
-        w2_bf.append(cast_w2(1))
         copy_parent(1)
+        w2_bf.append(cast_w2(1))
         open_h(0, 256, H_AT)
         for n in (0, 2, 1, 3, 4):
             product(n)
         add_on_vector(3)
-        for run in RUNS[0:3]:
+        for run in RUNS[0:2]:
             add_on_gpsimd(run)
         for n, m in ((6, 4), (5, 6)):
             product(n)
@@ -299,24 +299,25 @@ def tile_list_syntax_node_latency_kernel(tc, tab_words, tab_scales, offs, offs2,
             copy_parent(n)
         for n in range(EARLY_RELUS, UNITS):
             rectify_left(n)
-        w2_q = [quantize(w2_bf[g], "w2%d" % g, [PROD_AT[1], P_SB_AT[1]][g], RELU_AT[6] + 512 * g) for g in range(G)]
+        w2_q = [quantize(w2_bf[g], "w2%d" % g, PROD_AT[2] + 2 * KB * g, RELU_AT[6] + 512 * g) for g in range(G)]
         sums = second_product(quantize_h(0), wide_banks())
 
         open_h(256, 256, H_AT)
         for n in (7, 8, 10):
             product(n)
         add_on_vector(7)
-        for run in RUNS[3:5]:
+        for run in RUNS[2:4]:
             add_on_gpsimd(run)
-        cast_y(0, 256, add_bias(0, 256, sums, ()), nc.scalar.copy)
+        y = add_bias(0, 256, sums, ())
         for n in (12, 14):
-            copy_parent(n)
+            copy_parent(n, "wide")
+        cast_y(0, 256, y, nc.scalar.copy)
         for n in (9, 11, 12):
             product(n)
         sums = second_product(quantize_h(256), wide_banks())
 
         open_h(512, 256, H_AT)
-        add_on_gpsimd(RUNS[5])
+        add_on_gpsimd(RUNS[4])
         for n in (9, 10, 11):
             add_on_vector(n)
         cast_y(256, 256, add_bias(256, 256, sums, ()), nc.scalar.copy)
@@ -326,7 +327,7 @@ def tile_list_syntax_node_latency_kernel(tc, tab_words, tab_scales, offs, offs2,
         open_h(896, JT, H_AT + 2 * KB)
         for n in (14, 13, 15):
             product(n)
-        for run in RUNS[6:8]:
+        for run in RUNS[5:7]:
             add_on_gpsimd(run)
         add_on_vector(13)
         add_on_vector(15)

@@ -242,21 +242,24 @@ def tile_list_syntax_node_latency_kernel(tc, tab_words, tab_scales, offs, offs2,
             pairs = [next_bank(reader)[:].rearrange("p (a b) j -> p a (b j)", a=2) for pair in range(2)]
             return [pairs[t // 2][:, t % 2, :] for t in range(4)]
 
-        def add_bias(j0, width, sums, on_vector):
-            y = ring.tile([P, 4, width], F32, name="y")
+        def add_bias_into(y, sums, on_vector):
             for t in range(4):
                 if t in on_vector:
                     nc.vector.tensor_scalar(y[:, t, :], sums[t], bias[:, t:t + 1], None, ALU.add)
                 else:
                     nc.scalar.activation(y[:, t, :], sums[t], ACT.Identity, bias=bias[:, t:t + 1])
+
+        def add_bias(j0, width, sums, on_vector):
+            y = ring.tile([P, 4, width], F32, name="y")
+            add_bias_into(y[:], sums, on_vector)
             nc.sync.dma_start(y_rows[:, :, j0:j0 + width], y[:])
-            return y
+            return y[:]
 
         y_bf = keep.tile([P, 4 * S], BF16, name="y_bf", align_bytes=64)
 
         def cast_y(j0, width, y, copy):
             copy(y_bf[:, 4 * j0:4 * (j0 + width)].rearrange("p (c i t) -> p c t i", i=4, t=4),
-                 y[:].rearrange("p t (c i) -> p c t i", i=4))
+                 y.rearrange("p t (c i) -> p c t i", i=4))
 
         def planes(y_w, at, j0, j1):
             nc.vector.quantize_mx(out=y_w[:, j0 - at:j1 - at].bitcast(E4M3), scales=y_sc[:, j0:j1], in_=y_bf[:, 4 * j0:4 * j1])
@@ -337,13 +340,15 @@ def tile_list_syntax_node_latency_kernel(tc, tab_words, tab_scales, offs, offs2,
         pairs = [next_bank("wide"), next_bank("vector")]
         last_sums = second_product(quantize_h(896), [pairs[t // 2][:, t % 2, :] for t in range(4)])
         y_w = placed([P, 768], U32, "y_w_first", H_AT - KB)
-        planes(y_w, 0, 0, 512)
-        planes(y_w, 0, 512, 768)
-        nc.sync.dma_start(y_words[:, 0:768], y_w[:].bitcast(I32))
-        before = add_bias(768, JT, sums, ())
-        y = add_bias(896, JT, last_sums, (2, 3))
-        cast_y(768, JT, before, nc.scalar.copy)
-        cast_y(896, JT, y, nc.vector.tensor_copy)
+        for j0, j1 in ((0, 512), (512, 768)):
+            planes(y_w, 0, j0, j1)
+            nc.sync.dma_start(y_words[:, j0:j1], y_w[:, j0:j1].bitcast(I32))
+        y = ring.tile([P, 4, 2 * JT], F32, name="y")
+        add_bias_into(y[:, :, 0:JT], sums, ())
+        add_bias_into(y[:, :, JT:2 * JT], last_sums, (2, 3))
+        nc.sync.dma_start(y_rows[:, :, 768:S], y[:])
+        cast_y(768, JT, y[:, :, 0:JT], nc.scalar.copy)
+        cast_y(896, JT, y[:, :, JT:2 * JT], nc.vector.tensor_copy)
         y_w = placed([P, 256], U32, "y_w_last", None)
         planes(y_w, 768, 768, S)
         nc.sync.dma_start(y_words[:, 768:S], y_w[:].bitcast(I32))

@@ -19,20 +19,17 @@ ACT = mybir.ActivationFunctionType
 P = 128
 G = H // 512
 JT = 128
+CW = 256
+CHUNKS = S // CW
 KB = 1024
-UNITS = G * S // JT
-EARLY_RELUS = 13
-WP1_AT = 8 * KB
-RIGHT_AT = KB
-WP_BF_AT = [84 * KB, RIGHT_AT]
-W2_BF_AT = [22 * KB, 26 * KB]
-W21_AT = 38 * KB
-H_AT = WP_BF_AT[1]
-RELU_AT = {2: W2_BF_AT[1], 6: 36 * KB, 11: 54 * KB}
-PROD_AT = {0: WP1_AT, 2: WP1_AT + 2 * KB, 7: W2_BF_AT[0], 8: 26 * KB, 10: 28 * KB, 11: 56 * KB, 13: 56 * KB, 9: 58 * KB, 14: 58 * KB, 15: 60 * KB}
-P_SB_AT = {4: W21_AT, 6: W21_AT + 2 * KB, 8: 60 * KB}
-H_W_AT = {256: RELU_AT[11]}
-RUNS = [(0,), (2, 1), (4,), (6, 5), (8,), (12,), (14,)]
+
+WP_STAGE_AT = 0
+W2_BF_AT = 24 * KB
+RELU_A_AT = {(1, 1): 32 * KB}
+RELU_B_AT = {(1, 0): 36 * KB, (2, 0): 44 * KB, (3, 0): 48 * KB}
+H_AT = {0: 40 * KB, 256: 40 * KB, 512: 52 * KB, 896: 54 * KB}
+PROD_AT = {(0, 0): WP_STAGE_AT, (0, 1): WP_STAGE_AT + 4 * KB, (1, 0): WP_STAGE_AT + 8 * KB, (2, 0): W2_BF_AT + 4 * KB, (3, 0): H_AT[256]}
+H_CODES_AT = {0: RELU_B_AT[1, 0] + KB, 256: RELU_B_AT[2, 0], 512: RELU_B_AT[3, 0]}
 
 
 def tile_list_syntax_node_latency_kernel(tc, tab_words, tab_scales, offs, offs2, offs3, wp, wl_words, wl_scales,
@@ -42,314 +39,268 @@ def tile_list_syntax_node_latency_kernel(tc, tab_words, tab_scales, offs, offs2,
         keep = ctx.enter_context(tc.tile_pool(name="keep", bufs=1))
         shared = ctx.enter_context(tc.tile_pool(name="shared", bufs=1))
         ring = ctx.enter_context(tc.tile_pool(name="ring", bufs=3))
-        psum = ctx.enter_context(tc.psum_pool(name="psum", bufs=2))
+        psum = ctx.enter_context(tc.psum_pool(name="psum", bufs=1))
 
-        def placed(shape, dtype, name, at):
+        def placed(shape, dtype, name, at=None):
             if at is None:
                 return keep.tile(shape, dtype, name=name, align_bytes=64)
             return shared.tile(shape, dtype, name=name, align_bytes=64, offset=at)
 
-        tab_sc = keep.tile([P, T], U8, name="tab_sc", align_bytes=64)
-        left_raw = placed([P, 768], I32, "left_raw", None)
-        wl_raw = left_raw[:, 0:H // 2]
-        wl_sc_raw = left_raw[:, H // 2:H // 2 + H // 4]
-        right_raw = placed([P, 1280], I32, "right_raw", RIGHT_AT)
-        wr_raw = right_raw[:, 0:H]
-        wr_sc_raw = right_raw[:, H:H + H // 4]
+        tab_sc = placed([P, T], U8, "tab_sc")
+        wl_sc_raw = placed([P, H // 4], I32, "wl_sc_raw")
+        wr_sc_raw = placed([P, H // 4], I32, "wr_sc_raw")
         nc.gpsimd.memset(tab_sc[:].bitcast(I32), 0)
-        nc.gpsimd.memset(wl_sc_raw, 0)
-        nc.gpsimd.memset(wr_sc_raw, 0)
+        nc.gpsimd.memset(wl_sc_raw[:], 0)
+        nc.gpsimd.memset(wr_sc_raw[:], 0)
 
         def load_scale_rows(plane, rows):
             for q in range(4):
                 nc.sync.dma_start(plane[32 * q:32 * q + 4, :], rows[4 * q:4 * q + 4, :].bitcast(I32))
 
-        list_l = keep.tile([P, S // 16], U16, name="list_l")
-        list_r = keep.tile([P, S // 16], U16, name="list_r")
-        list_p = keep.tile([P, S // 16], U16, name="list_p")
-        tab_w = keep.tile([P, T], I32, name="tab_w", align_bytes=64)
-        wp_raw = [placed([P, 4, 512], F32, "wp_raw%d" % g, [None, WP1_AT][g]) for g in range(G)]
-        w2_raw = [placed([P, 4, N], F32, "w2_raw%d" % g, [None, W21_AT][g]) for g in range(G)]
-        bias = keep.tile([P, 4], F32, name="bias")
+        lists = {side: keep.tile([P, S // 16], U16, name="list_" + side) for side in "lrp"}
+        tab_w = placed([P, T], I32, "tab_w")
+        wl_raw = placed([P, H // 2], I32, "wl_raw")
+        wr_raw = placed([P, H], I32, "wr_raw")
+        wp_stage = placed([P, 6144], F32, "wp_stage", WP_STAGE_AT)
+        wp_raw = [wp_stage[:, 2048 * g:2048 * (g + 1)] for g in range(G)]
+        wp_bf = wp_stage[:, 4096:6144].bitcast(BF16)
+        w2_raw = [placed([P, 4, N], F32, "w2_raw%d" % g) for g in range(G)]
+        bias = placed([P, 4], F32, "bias")
         wp_rows = wp.rearrange("(p i) (g r) -> g p i r", i=4, g=G)
         w2_rows = w2.rearrange("(g m t e) n -> g t m (e n)", g=G, t=4, e=4)
 
-        nc.sync.dma_start(list_l[:], offs2)
-        nc.sync.dma_start(list_r[:], offs3)
+        nc.sync.dma_start(lists["l"][:], offs2)
+        nc.sync.dma_start(wl_raw[:], wl_words[0].bitcast(I32))
         nc.sync.dma_start(bias[:], b2.rearrange("(p t) -> p t", t=4))
         load_scale_rows(tab_sc[:].bitcast(I32), tab_scales[0])
         nc.sync.dma_start(tab_w[:], tab_words[0].rearrange("p n t -> p (n t)").bitcast(I32))
-        nc.sync.dma_start(list_p[:], offs)
-        nc.sync.dma_start(wl_raw, wl_words[0].bitcast(I32))
-        load_scale_rows(wl_sc_raw, wl_scales[0])
-        nc.sync.dma_start(wp_raw[0][:], wp_rows[0])
-        nc.sync.dma_start(wr_raw, wr_words[0].rearrange("p n t -> p (n t)").bitcast(I32))
-        load_scale_rows(wr_sc_raw, wr_scales[0])
-        nc.sync.dma_start(wp_raw[1][:], wp_rows[1])
+        nc.sync.dma_start(lists["r"][:], offs3)
+        load_scale_rows(wl_sc_raw[:], wl_scales[0])
+        nc.sync.dma_start(wp_raw[0].rearrange("p (i r) -> p i r", i=4), wp_rows[0])
+        nc.sync.dma_start(wr_raw[:], wr_words[0].rearrange("p n t -> p (n t)").bitcast(I32))
+        load_scale_rows(wr_sc_raw[:], wr_scales[0])
+        nc.sync.dma_start(wp_raw[1].rearrange("p (i r) -> p i r", i=4), wp_rows[1])
+        nc.sync.dma_start(lists["p"][:], offs)
         for g in range(G):
             for t in range(4):
                 nc.sync.dma_start(w2_raw[g][:, t, :], w2_rows[g, t])
 
-        lists = {"l": list_l, "r": list_r, "p": list_p}
-        got_words = {"l": [], "r": [], "p": []}
-        got_scales = {"l": [], "r": [], "p": []}
+        got = {(kind, side): [] for kind in ("words", "scales") for side in "lrp"}
 
-        def gather(store, window, dtype, side, j0, width, at):
-            got = placed([P, width], dtype, "got_%s%d_%d" % (side, j0, len(store[side]) + (8 if dtype == U8 else 0)), at)
-            nc.vector.tensor_copy(got[:], window.indirect(lists[side][:, j0 // 16:(j0 + width) // 16]))
-            store[side].append((j0, width, got))
+        def gather(kind, side, j0, width, at=None):
+            dtype = U32 if kind == "words" else U8
+            window = tab_w[:].bitcast(U32) if kind == "words" else tab_sc[:]
+            piece = placed([P, width], dtype, "got_%s_%s%d" % (kind, side, j0), at)
+            nc.vector.tensor_copy(piece[:], window.indirect(lists[side][:, j0 // 16:(j0 + width) // 16]))
+            got[kind, side].append((j0, width, piece))
 
-        def gather_scales(side, j0, width, at=None):
-            gather(got_scales, tab_sc[:], U8, side, j0, width, at)
+        def picked(kind, side, j):
+            j0, width, piece = [one for one in got[kind, side] if one[0] <= j < one[0] + one[1]][0]
+            return piece[:, j - j0:j - j0 + JT]
 
-        def gather_words(side, j0, width, at=None):
-            gather(got_words, tab_w[:].bitcast(U32), U32, side, j0, width, at)
+        def deal(copy, dealt, raw, run):
+            copy(dealt.rearrange("p (g t m e) -> p g t m e", g=G, t=4, e=run),
+                 raw.rearrange("p (g m t e) -> p g t m e", g=G, t=4, e=run))
 
-        def picked(store, side, j):
-            j0, width, got = [piece for piece in store[side] if piece[0] <= j < piece[0] + piece[1]][0]
-            return got[:, j - j0:j - j0 + JT]
-
-        def deal(engine, dealt, raw, run):
-            engine.tensor_copy(dealt.rearrange("p (g t m e) -> p g t m e", g=G, t=4, e=run),
-                               raw.rearrange("p (g m t e) -> p g t m e", g=G, t=4, e=run))
-
-        def deal_scales(engine, dealt, raw):
-            engine.tensor_copy(dealt.rearrange("p (g t c i) -> p g c t i", g=G, t=4, i=4),
-                               raw.rearrange("p (g c i t) -> p g c t i", g=G, t=4, i=4))
+        def deal_scales(copy, dealt, raw):
+            copy(dealt.rearrange("p (g t c i) -> p g c t i", g=G, t=4, i=4),
+                 raw.rearrange("p (g c i t) -> p g c t i", g=G, t=4, i=4))
 
         def quantize(grouped, name, codes_at=None, plane_at=None):
-            codes = placed([P, 512], U32, name + "_w", codes_at)
-            plane = placed([P, 512], U8, name + "_sc", plane_at)
+            width = grouped.shape[1] // 4
+            codes = placed([P, width], U32, name + "_codes", codes_at)
+            plane = placed([P, width], U8, name + "_plane", plane_at)
             nc.vector.quantize_mx(out=codes[:].bitcast(E4M3), scales=plane[:], in_=grouped)
             return codes, plane
 
-        def cast_wp(g):
-            wp_bf = placed([P, 2048], BF16, "wp_bf%d" % g, WP_BF_AT[g])
-            nc.gpsimd.tensor_scalar(wp_bf[:].rearrange("p (t m e i) -> p m t e i", t=4, e=4, i=4),
-                                    wp_raw[g][:].rearrange("p i (m t e) -> p m t e i", t=4, e=4), 1.0, 0.0, ALU.mult, ALU.add)
-            return wp_bf[:]
-
-        def cast_w2(g):
-            w2_bf = placed([P, 2048], BF16, "w2_bf%d" % g, W2_BF_AT[g])
-            nc.scalar.copy(w2_bf[:].rearrange("p (u c t) -> p c t u", u=4, t=4), w2_raw[g][:].rearrange("p t (c u) -> p c t u", u=4))
-            return w2_bf[:]
-
-        banks = {reader: [psum.tile([P, 4, JT], F32, name="bank_%s%d" % (reader, b), bufs=1) for b in range(count)]
-                 for reader, count in (("vector", 3), ("scalar", 3), ("wide", 2))}
+        banks = {reader: [psum.tile([P, 4, JT], F32, name="bank_%s%d" % (reader, b)) for b in range(count)]
+                 for reader, count in (("vector", 4), ("scalar", 4))}
         turns = {reader: [] for reader in banks}
 
         def next_bank(reader):
             turns[reader].append(reader)
             return banks[reader][len(turns[reader]) % len(banks[reader])]
 
-        def first_product(n, side, weights, reader):
-            jt, g = divmod(n, G)
-            words = picked(got_words, side, jt * JT)
-            plane = picked(got_scales, side, jt * JT)
+        wl_w = placed([P, H // 2], I32, "wl_w")
+        wl_sc = placed([P, H], U8, "wl_sc")
+        wr_w = placed([P, H], I32, "wr_w")
+        wr_sc = placed([P, H], U8, "wr_sc")
+        quantised = {}
+
+        def stationary(side, c):
+            if side == "l":
+                return wl_w[:, c // 2:(c + P) // 2].bitcast(U8).bitcast(E2M1), wl_sc[:, c:c + P]
+            if side == "r":
+                return wr_w[:, c:c + P].bitcast(E4M3), wr_sc[:, c:c + P]
+            codes, plane = quantised[side]
+            return codes[:, c:c + P].bitcast(E4M3), plane[:, c:c + P]
+
+        def first_product(side, jt, g, reader):
             bank = next_bank(reader)
             for t in range(4):
-                w_codes, w_plane = weights(g, t)
-                nc.tensor.matmul_mx(out=bank[:, t, :], lhsT=w_codes, lhsT_scale=w_plane, rhs=words.bitcast(E4M3),
-                                    rhs_scale=plane, start=True, stop=True)
+                w_codes, w_plane = stationary(side, 512 * g + P * t)
+                nc.tensor.matmul_mx(out=bank[:, t, :], lhsT=w_codes, lhsT_scale=w_plane,
+                                    rhs=picked("words", side, jt * JT).bitcast(E4M3), rhs_scale=picked("scales", side, jt * JT),
+                                    start=True, stop=True)
             return bank[:].rearrange("p t j -> p j t")
 
-        wl_w = keep.tile([P, H // 2], I32, name="wl_w", align_bytes=64)
-        wl_sc = keep.tile([P, H], U8, name="wl_sc", align_bytes=64)
-        gather_scales("l", 0, 768, W2_BF_AT[0])
-        gather_scales("l", 768, 256)
-        gather_words("l", 0, 512)
-        deal(nc.gpsimd, wl_w[:], wl_raw, 2)
-        deal_scales(nc.gpsimd, wl_sc[:].bitcast(I32), wl_sc_raw)
-        gather_words("l", 512, 512)
-        gather_scales("p", 0, S)
-        gather_words("p", 0, 768)
-
-        def left(g, t):
-            c = 512 * g + P * t
-            return wl_w[:, c // 2:(c + P) // 2].bitcast(U8).bitcast(E2M1), wl_sc[:, c:c + P]
-
-        def right(g, t):
-            c = 512 * g + P * t
-            return wr_w[:, c:c + P].bitcast(E4M3), wr_sc[:, c:c + P]
-
-        def parent(g, t):
-            codes, plane = wp_q[g]
-            return codes[:, P * t:P * t + P].bitcast(E4M3), plane[:, P * t:P * t + P]
-
-        relu_a = {}
+        relus = {}
         prods = {}
-        copied = {}
         h_tiles = {}
 
-        def unit_tile(store, places, name, n, runs):
-            run = ([run for run in runs if n in run] + [(n,)])[0]
-            if run not in store:
-                store[run] = placed([P, len(run) * JT, 4], F32, "%s%d" % (name, n), places.get(run[0]))[:]
-                for i, m in enumerate(run):
-                    store[m] = store[run][:, i * JT:(i + 1) * JT, :]
-            return store[n]
+        def rectify(side, c, g):
+            at = (RELU_A_AT if side == "l" else RELU_B_AT).get((c, g))
+            relus[side, c, g] = placed([P, CW, 4], F32, "relu_%s%d%d" % (side, c, g), at)
+            for i in range(2):
+                nc.scalar.activation(relus[side, c, g][:, i * JT:(i + 1) * JT, :], first_product(side, 2 * c + i, g, "scalar"), ACT.Relu)
 
-        def rectify_left(n):
-            nc.scalar.activation(unit_tile(relu_a, RELU_AT, "relu_a", n, []),
-                                 first_product(n, "l", left, "scalar"), ACT.Relu)
+        def multiply_on_gpsimd(c, g):
+            prods[c, g] = placed([P, CW, 4], F32, "prod%d%d" % (c, g), PROD_AT[c, g])
+            nc.gpsimd.tensor_tensor(prods[c, g][:], relus["l", c, g][:], relus["r", c, g][:], ALU.mult)
 
-        def product(n):
-            nc.vector.scalar_tensor_tensor(unit_tile(prods, PROD_AT, "prod", n, RUNS), first_product(n, "r", right, "vector"), 0.0,
-                                           relu_a[n], ALU.max, ALU.mult)
+        def multiply_on_vector(c, g):
+            prods[c, g] = placed([P, CW, 4], F32, "prod%d%d" % (c, g))
+            for i in range(2):
+                part = slice(i * JT, (i + 1) * JT)
+                nc.vector.scalar_tensor_tensor(prods[c, g][:, part, :], first_product("r", 2 * c + i, g, "vector"), 0.0,
+                                               relus["l", c, g][:, part, :], ALU.max, ALU.mult)
 
-        def copy_parent(n, reader="scalar"):
-            nc.scalar.copy(unit_tile(copied, P_SB_AT, "p_sb", n, RUNS), first_product(n, "p", parent, reader))
+        def open_h(j0, width):
+            h_tiles[j0] = placed([P, G, width, 4], BF16, "h_bf%d" % j0, H_AT.get(j0))
 
-        def open_h(j0, width, at):
-            h_tiles[j0] = (width, placed([P, G * width * 4], BF16, "h_bf%d" % j0, at))
-
-        def h_part(n, units=1):
-            jt, g = divmod(n, G)
+        def h_part(jt, g):
             j0 = max(j for j in h_tiles if j <= jt * JT)
-            width, h_bf = h_tiles[j0]
-            at = 4 * (g * width + jt * JT - j0)
-            return h_bf[:, at:at + 4 * JT * units].rearrange("p (j t) -> p j t", t=4)
+            return h_tiles[j0][:, g, jt * JT - j0:(jt + 1) * JT - j0, :]
 
-        def add_on_gpsimd(run):
-            nc.gpsimd.tensor_tensor(h_part(run[0], len(run)), copied[run], prods[run], ALU.add)
+        def prod_part(jt, g):
+            return prods[jt // 2, g][:, jt % 2 * JT:(jt % 2 + 1) * JT, :]
 
-        def add_on_vector(n):
-            nc.vector.tensor_tensor(h_part(n), first_product(n, "p", parent, "vector"), prods[n], ALU.add)
-
-        y_sc = keep.tile([P, S], U8, name="y_sc", align_bytes=64)
-        y_rows = out_0.rearrange("(p t) j -> p t j", t=4)
-        y_words = out_1[0].rearrange("p m t -> p (m t)").bitcast(I32)
+        def add_on_vector(jt, g):
+            nc.vector.tensor_tensor(h_part(jt, g), first_product("p", jt, g, "vector"), prod_part(jt, g), ALU.add)
 
         def quantize_h(j0):
-            width, h_bf = h_tiles[j0]
-            h_w = placed([P, G, width], U32, "h_w%d" % j0, H_W_AT.get(j0))
-            h_sc = ring.tile([P, G, width], U8, name="h_sc", align_bytes=64)
-            nc.vector.quantize_mx(out=h_w[:].rearrange("p g j -> p (g j)").bitcast(E4M3), scales=h_sc[:].rearrange("p g j -> p (g j)"),
-                                  in_=h_bf[:])
-            return h_w, h_sc
+            return quantize(h_tiles[j0][:].rearrange("p g j t -> p (g j t)"), "h%d" % j0, H_CODES_AT.get(j0))
 
         def second_product(h_q, sums):
-            h_w, h_sc = h_q
+            h_codes, h_plane = h_q
+            width = h_codes.shape[1] // G
             for t in range(4):
                 for g in range(G):
-                    codes, plane = w2_q[g]
-                    nc.tensor.matmul_mx(out=sums[t], lhsT=codes[:, P * t:P * t + P].bitcast(E4M3),
-                                        lhsT_scale=plane[:, P * t:P * t + P], rhs=h_w[:, g, :].bitcast(E4M3),
-                                        rhs_scale=h_sc[:, g, :], start=(g == 0), stop=(g == G - 1))
+                    w_codes, w_plane = stationary("w2", 512 * g + P * t)
+                    nc.tensor.matmul_mx(out=sums[t], lhsT=w_codes, lhsT_scale=w_plane,
+                                        rhs=h_codes[:, g * width:(g + 1) * width].bitcast(E4M3),
+                                        rhs_scale=h_plane[:, g * width:(g + 1) * width], start=(g == 0), stop=(g == G - 1))
             return sums
 
-        def wide_banks(reader="wide"):
+        def wide_banks(reader):
             pairs = [next_bank(reader)[:].rearrange("p (a b) j -> p a (b j)", a=2) for pair in range(2)]
             return [pairs[t // 2][:, t % 2, :] for t in range(4)]
 
-        def add_bias_into(y, sums, on_vector):
+        y_sc = placed([P, S], U8, "y_sc")
+        y_bf = placed([P, 4 * S], BF16, "y_bf")
+        y_rows = out_0.rearrange("(p t) j -> p t j", t=4)
+        y_words = out_1[0].rearrange("p m t -> p (m t)").bitcast(I32)
+
+        def add_bias_into(y, sums, on_vector=()):
             for t in range(4):
                 if t in on_vector:
                     nc.vector.tensor_scalar(y[:, t, :], sums[t], bias[:, t:t + 1], None, ALU.add)
                 else:
                     nc.scalar.activation(y[:, t, :], sums[t], ACT.Identity, bias=bias[:, t:t + 1])
 
-        def add_bias(j0, width, sums, on_vector):
-            y = ring.tile([P, 4, width], F32, name="y")
-            add_bias_into(y[:], sums, on_vector)
-            nc.sync.dma_start(y_rows[:, :, j0:j0 + width], y[:])
-            return y[:]
-
-        y_bf = keep.tile([P, 4 * S], BF16, name="y_bf", align_bytes=64)
-
         def cast_y(j0, width, y, copy):
             copy(y_bf[:, 4 * j0:4 * (j0 + width)].rearrange("p (c i t) -> p c t i", i=4, t=4),
                  y.rearrange("p t (c i) -> p c t i", i=4))
 
+        def finish_chunk(c, sums):
+            y = ring.tile([P, 4, CW], F32, name="y")
+            add_bias_into(y[:], sums)
+            nc.sync.dma_start(y_rows[:, :, c * CW:(c + 1) * CW], y[:])
+            return y[:]
+
         def planes(y_w, at, j0, j1):
             nc.vector.quantize_mx(out=y_w[:, j0 - at:j1 - at].bitcast(E4M3), scales=y_sc[:, j0:j1], in_=y_bf[:, 4 * j0:4 * j1])
+            nc.sync.dma_start(y_words[:, j0:j1], y_w[:, j0 - at:j1 - at].bitcast(I32))
 
-        def store_scale_rows(j0, j1):
-            for q in range(4):
-                queue = nc.sync if j1 < S or q % 2 == 0 else nc.scalar
-                queue.dma_start(out_2[0][4 * q:4 * q + 4, j0:j1].bitcast(I32), y_sc[32 * q:32 * q + 4, j0:j1].bitcast(I32))
+        gather("scales", "l", 0, 256)
+        gather("scales", "l", 256, 768)
+        gather("words", "l", 0, 256)
+        gather("words", "l", 256, 768)
+        gather("scales", "r", 0, S)
+        gather("words", "r", 0, 256, W2_BF_AT)
+        gather("words", "r", 256, 768)
+        gather("scales", "p", 0, 256)
 
-        for n in range(EARLY_RELUS):
-            rectify_left(n)
+        deal(nc.gpsimd.tensor_copy, wl_w[:], wl_raw[:], 2)
+        deal_scales(nc.gpsimd.tensor_copy, wl_sc[:].bitcast(I32), wl_sc_raw[:])
+        for g in range(G):
+            nc.gpsimd.tensor_scalar(wp_bf[:, 2048 * g:2048 * (g + 1)].rearrange("p (t m e i) -> p m t e i", t=4, e=4, i=4),
+                                    wp_raw[g].rearrange("p (i m t e) -> p m t e i", i=4, t=4, e=4), 1.0, 0.0, ALU.mult, ALU.add)
+        quantised["p"] = quantize(wp_bf, "wp")
+        gather("words", "p", 0, 256, WP_STAGE_AT + 12 * KB)
+        gather("scales", "p", 256, 768, WP_STAGE_AT + 13 * KB)
+        gather("words", "p", 256, 768, WP_STAGE_AT + 14 * KB)
 
-        wp_bf = [cast_wp(0)]
-        wr_w = placed([P, H], I32, "wr_w", WP_BF_AT[0] + 256 - 4 * KB)
-        wr_sc = placed([P, H], U8, "wr_sc", None)
-        deal_scales(nc.gpsimd, wr_sc[:].bitcast(I32), wr_sc_raw)
-        wp_q = [quantize(wp_bf[0], "wp0")]
-        deal(nc.gpsimd, wr_w[:], wr_raw, 4)
-        wp_bf.append(cast_wp(1))
-        gather_scales("r", 0, S, WP_BF_AT[0] + 256)
-        gather_words("p", 768, 256, WP_BF_AT[0] + 256 + KB)
-        copy_parent(0)
-        w2_bf = [cast_w2(0)]
-        gather_words("r", 0, 256, WP_BF_AT[0] + 256 + 2 * KB)
-        gather_words("r", 256, 768, WP_BF_AT[0] + 256 + 3 * KB)
-        wp_q.append(quantize(wp_bf[1], "wp1"))
-        copy_parent(2)
-        copy_parent(1)
-        w2_bf.append(cast_w2(1))
-        open_h(0, 256, H_AT)
-        for n in (0, 2, 1, 3, 4):
-            product(n)
-        add_on_vector(3)
-        for run in RUNS[0:2]:
-            add_on_gpsimd(run)
-        for n, m in ((6, 4), (5, 6)):
-            product(n)
-            copy_parent(m)
-        for n in (5, 8):
-            copy_parent(n)
-        for n in range(EARLY_RELUS, UNITS):
-            rectify_left(n)
-        w2_q = [quantize(w2_bf[g], "w2%d" % g, PROD_AT[2] + 2 * KB * g, RELU_AT[6] + 512 * g) for g in range(G)]
-        sums = second_product(quantize_h(0), wide_banks())
+        for c, g in ((0, 0), (0, 1)):
+            rectify("l", c, g)
+        deal(nc.scalar.copy, wr_w[:].bitcast(U32), wr_raw[:].bitcast(U32), 4)
+        deal_scales(nc.scalar.copy, wr_sc[:].bitcast(U32), wr_sc_raw[:].bitcast(U32))
+        for c, g in ((1, 0), (1, 1)):
+            rectify("l", c, g)
+        for c, g in ((0, 0), (0, 1), (1, 0)):
+            rectify("r", c, g)
+            multiply_on_gpsimd(c, g)
+        rectify("l", 2, 0)
+        w2_bf = placed([P, G, 2048], BF16, "w2_bf", W2_BF_AT)
+        for g in range(G):
+            nc.scalar.copy(w2_bf[:, g, :].rearrange("p (u c t) -> p c t u", u=4, t=4), w2_raw[g][:].rearrange("p t (c u) -> p c t u", u=4))
 
-        open_h(256, 256, H_AT)
-        for n in (7, 8, 10):
-            product(n)
-        add_on_vector(7)
-        for run in RUNS[2:4]:
-            add_on_gpsimd(run)
-        y = add_bias(0, 256, sums, ())
-        for n in (12, 14):
-            copy_parent(n, "wide")
-        cast_y(0, 256, y, nc.scalar.copy)
-        for n in (9, 11, 12):
-            product(n)
-        sums = second_product(quantize_h(256), wide_banks())
+        open_h(0, CW)
+        for g in range(G):
+            for jt in range(2):
+                add_on_vector(jt, g)
+        multiply_on_vector(1, 1)
+        for side, c, g in (("r", 2, 0), ("l", 2, 1), ("l", 3, 0), ("r", 3, 0), ("l", 3, 1)):
+            rectify(side, c, g)
+        h_q = quantize_h(0)
+        quantised["w2"] = quantize(w2_bf[:].rearrange("p g c -> p (g c)"), "w2", RELU_A_AT[1, 1], RELU_B_AT[1, 0])
+        sums = second_product(h_q, wide_banks("scalar"))
 
-        open_h(512, 256, H_AT)
-        add_on_gpsimd(RUNS[4])
-        for n in (9, 10, 11):
-            add_on_vector(n)
-        cast_y(256, 256, add_bias(256, 256, sums, ()), nc.scalar.copy)
-        sums = second_product(quantize_h(512), wide_banks("scalar"))
+        for c in (1, 2):
+            multiply_on_gpsimd(c + 1, 0)
+            open_h(c * CW, CW)
+            for g in range(G):
+                for jt in range(2 * c, 2 * c + 2):
+                    add_on_vector(jt, g)
+            multiply_on_vector(c + 1, 1)
+            cast_y((c - 1) * CW, CW, finish_chunk(c - 1, sums), nc.scalar.copy)
+            if c == 1:
+                p_last = placed([P, JT, 4], F32, "p_last")
+                nc.scalar.copy(p_last[:], first_product("p", 7, 0, "scalar"))
+            sums = second_product(quantize_h(c * CW), wide_banks("scalar"))
 
-        open_h(768, JT, H_AT)
-        open_h(896, JT, H_AT + 2 * KB)
-        for n in (14, 13, 15):
-            product(n)
-        for run in RUNS[5:7]:
-            add_on_gpsimd(run)
-        add_on_vector(13)
-        add_on_vector(15)
-        cast_y(512, 256, add_bias(512, 256, sums, ()), nc.scalar.copy)
-        bank = next_bank("wide")
+        open_h(768, JT)
+        open_h(896, JT)
+        nc.gpsimd.tensor_tensor(h_part(7, 0), p_last[:], prod_part(7, 0), ALU.add)
+        for jt, g in ((6, 0), (6, 1), (7, 1)):
+            add_on_vector(jt, g)
+        y = finish_chunk(2, sums)
+        bank = next_bank("scalar")
         sums = second_product(quantize_h(768), [bank[:, t, :] for t in range(4)])
-        pairs = [next_bank("wide"), next_bank("vector")]
+        pairs = [next_bank("scalar"), next_bank("vector")]
         last_sums = second_product(quantize_h(896), [pairs[t // 2][:, t % 2, :] for t in range(4)])
-        y_w = placed([P, 768], U32, "y_w_first", H_AT - KB)
-        for j0, j1 in ((0, 512), (512, 768)):
-            planes(y_w, 0, j0, j1)
-            nc.sync.dma_start(y_words[:, j0:j1], y_w[:, j0:j1].bitcast(I32))
+        cast_y(512, CW, y, nc.vector.tensor_copy)
+        y_w = placed([P, 768], U32, "y_w_first", H_AT[896] - KB)
+        planes(y_w, 0, 0, 512)
+        planes(y_w, 0, 512, 768)
         y = ring.tile([P, 4, 2 * JT], F32, name="y")
-        add_bias_into(y[:, :, 0:JT], sums, ())
+        add_bias_into(y[:, :, 0:JT], sums)
         add_bias_into(y[:, :, JT:2 * JT], last_sums, (2, 3))
         nc.sync.dma_start(y_rows[:, :, 768:S], y[:])
         cast_y(768, JT, y[:, :, 0:JT], nc.scalar.copy)
         cast_y(896, JT, y[:, :, JT:2 * JT], nc.vector.tensor_copy)
-        y_w = placed([P, 256], U32, "y_w_last", None)
+        y_w = placed([P, 256], U32, "y_w_last")
         planes(y_w, 768, 768, S)
-        nc.sync.dma_start(y_words[:, 768:S], y_w[:].bitcast(I32))
-        store_scale_rows(0, S)
+        for q in range(4):
+            queue = nc.sync if q % 2 == 0 else nc.scalar
+            queue.dma_start(out_2[0][4 * q:4 * q + 4, :].bitcast(I32), y_sc[32 * q:32 * q + 4, :].bitcast(I32))

@@ -23,13 +23,15 @@ CW = 256
 CHUNKS = S // CW
 KB = 1024
 
+WP_PIECES = ((0, 512), (512, 768), (768, 1024))
 WP_STAGE_AT = 0
 W2_BF_AT = 24 * KB
-RELU_A_AT = {(1, 1): 32 * KB}
+RELU_A_AT = {(1, 1): 32 * KB, (2, 1): 60 * KB, (3, 1): 64 * KB}
 RELU_B_AT = {(1, 0): 36 * KB, (2, 0): 44 * KB, (3, 0): 48 * KB}
-H_AT = {0: 40 * KB, 256: 40 * KB, 512: 52 * KB, 896: 54 * KB}
-PROD_AT = {(0, 0): WP_STAGE_AT, (0, 1): WP_STAGE_AT + 4 * KB, (1, 0): WP_STAGE_AT + 8 * KB, (2, 0): W2_BF_AT + 4 * KB, (3, 0): H_AT[256]}
+H_AT = {0: W2_BF_AT - 4 * KB, 256: W2_BF_AT + 2 * KB, 512: 52 * KB, 896: 54 * KB}
+PROD_AT = {(0, 0): WP_STAGE_AT, (0, 1): WP_STAGE_AT + 4 * KB, (1, 0): WP_STAGE_AT + 8 * KB, (2, 0): W2_BF_AT - 2 * KB, (3, 0): H_AT[256]}
 H_CODES_AT = {0: RELU_B_AT[1, 0] + KB, 256: RELU_B_AT[2, 0], 512: RELU_B_AT[3, 0]}
+H_PLANE_AT = {256: RELU_A_AT[2, 1], 512: RELU_A_AT[3, 1]}
 
 
 def tile_list_syntax_node_latency_kernel(tc, tab_words, tab_scales, offs, offs2, offs3, wp, wl_words, wl_scales,
@@ -60,13 +62,12 @@ def tile_list_syntax_node_latency_kernel(tc, tab_words, tab_scales, offs, offs2,
         lists = {side: keep.tile([P, S // 16], U16, name="list_" + side) for side in "lrp"}
         tab_w = placed([P, T], I32, "tab_w")
         wl_raw = placed([P, H // 2], I32, "wl_raw")
-        wr_raw = placed([P, H], I32, "wr_raw")
+        wr_raw = placed([P, H], I32, "wr_raw", RELU_A_AT[1, 1])
         wp_stage = placed([P, 6144], F32, "wp_stage", WP_STAGE_AT)
-        wp_raw = [wp_stage[:, 2048 * g:2048 * (g + 1)] for g in range(G)]
         wp_bf = wp_stage[:, 4096:6144].bitcast(BF16)
         w2_raw = [placed([P, 4, N], F32, "w2_raw%d" % g) for g in range(G)]
         bias = placed([P, 4], F32, "bias")
-        wp_rows = wp.rearrange("(p i) (g r) -> g p i r", i=4, g=G)
+        wp_rows = wp.rearrange("(p i) r -> p i r", i=4)
         w2_rows = w2.rearrange("(g m t e) n -> g t m (e n)", g=G, t=4, e=4)
 
         nc.sync.dma_start(lists["l"][:], offs2)
@@ -76,10 +77,12 @@ def tile_list_syntax_node_latency_kernel(tc, tab_words, tab_scales, offs, offs2,
         nc.sync.dma_start(tab_w[:], tab_words[0].rearrange("p n t -> p (n t)").bitcast(I32))
         nc.sync.dma_start(lists["r"][:], offs3)
         load_scale_rows(wl_sc_raw[:], wl_scales[0])
-        nc.sync.dma_start(wp_raw[0].rearrange("p (i r) -> p i r", i=4), wp_rows[0])
-        nc.sync.dma_start(wr_raw[:], wr_words[0].rearrange("p n t -> p (n t)").bitcast(I32))
-        load_scale_rows(wr_sc_raw[:], wr_scales[0])
-        nc.sync.dma_start(wp_raw[1].rearrange("p (i r) -> p i r", i=4), wp_rows[1])
+        for piece, (r0, r1) in enumerate(WP_PIECES):
+            if piece == 1:
+                load_scale_rows(wr_sc_raw[:], wr_scales[0])
+            if piece == 2:
+                nc.sync.dma_start(wr_raw[:], wr_words[0].rearrange("p n t -> p (n t)").bitcast(I32))
+            nc.sync.dma_start(wp_stage[:, 4 * r0:4 * r1].rearrange("p (i r) -> p i r", i=4), wp_rows[:, :, r0:r1])
         nc.sync.dma_start(lists["p"][:], offs)
         for g in range(G):
             for t in range(4):
@@ -148,19 +151,21 @@ def tile_list_syntax_node_latency_kernel(tc, tab_words, tab_scales, offs, offs2,
         prods = {}
         h_tiles = {}
 
-        def rectify(side, c, g):
-            at = (RELU_A_AT if side == "l" else RELU_B_AT).get((c, g))
-            relus[side, c, g] = placed([P, CW, 4], F32, "relu_%s%d%d" % (side, c, g), at)
-            for i in range(2):
+        def rectify(side, c, g, halves=(0, 1)):
+            if 0 in halves:
+                at = (RELU_A_AT if side == "l" else RELU_B_AT).get((c, g))
+                relus[side, c, g] = placed([P, CW, 4], F32, "relu_%s%d%d" % (side, c, g), at)
+            for i in halves:
                 nc.scalar.activation(relus[side, c, g][:, i * JT:(i + 1) * JT, :], first_product(side, 2 * c + i, g, "scalar"), ACT.Relu)
 
         def multiply_on_gpsimd(c, g):
             prods[c, g] = placed([P, CW, 4], F32, "prod%d%d" % (c, g), PROD_AT[c, g])
             nc.gpsimd.tensor_tensor(prods[c, g][:], relus["l", c, g][:], relus["r", c, g][:], ALU.mult)
 
-        def multiply_on_vector(c, g):
-            prods[c, g] = placed([P, CW, 4], F32, "prod%d%d" % (c, g))
-            for i in range(2):
+        def multiply_on_vector(c, g, halves=(0, 1)):
+            if 0 in halves:
+                prods[c, g] = placed([P, CW, 4], F32, "prod%d%d" % (c, g))
+            for i in halves:
                 part = slice(i * JT, (i + 1) * JT)
                 nc.vector.scalar_tensor_tensor(prods[c, g][:, part, :], first_product("r", 2 * c + i, g, "vector"), 0.0,
                                                relus["l", c, g][:, part, :], ALU.max, ALU.mult)
@@ -175,11 +180,13 @@ def tile_list_syntax_node_latency_kernel(tc, tab_words, tab_scales, offs, offs2,
         def prod_part(jt, g):
             return prods[jt // 2, g][:, jt % 2 * JT:(jt % 2 + 1) * JT, :]
 
-        def add_on_vector(jt, g):
-            nc.vector.tensor_tensor(h_part(jt, g), first_product("p", jt, g, "vector"), prod_part(jt, g), ALU.add)
+        def add_on_vector(jt, g, parent=None):
+            if parent is None:
+                parent = first_product("p", jt, g, "vector")
+            nc.vector.tensor_tensor(h_part(jt, g), parent, prod_part(jt, g), ALU.add)
 
         def quantize_h(j0):
-            return quantize(h_tiles[j0][:].rearrange("p g j t -> p (g j t)"), "h%d" % j0, H_CODES_AT.get(j0))
+            return quantize(h_tiles[j0][:].rearrange("p g j t -> p (g j t)"), "h%d" % j0, H_CODES_AT.get(j0), H_PLANE_AT.get(j0))
 
         def second_product(h_q, sums):
             h_codes, h_plane = h_q
@@ -228,25 +235,27 @@ def tile_list_syntax_node_latency_kernel(tc, tab_words, tab_scales, offs, offs2,
         gather("words", "l", 256, 768)
         gather("scales", "r", 0, S)
         gather("words", "r", 0, 256, W2_BF_AT)
-        gather("words", "r", 256, 768)
+        gather("words", "r", 256, 256)
         gather("scales", "p", 0, 256)
+        gather("words", "p", 0, 256)
 
         deal(nc.gpsimd.tensor_copy, wl_w[:], wl_raw[:], 2)
         deal_scales(nc.gpsimd.tensor_copy, wl_sc[:].bitcast(I32), wl_sc_raw[:])
-        for g in range(G):
-            nc.gpsimd.tensor_scalar(wp_bf[:, 2048 * g:2048 * (g + 1)].rearrange("p (t m e i) -> p m t e i", t=4, e=4, i=4),
-                                    wp_raw[g].rearrange("p (i m t e) -> p m t e i", i=4, t=4, e=4), 1.0, 0.0, ALU.mult, ALU.add)
+        for r0, r1 in WP_PIECES:
+            g, m0, m1 = r0 // 512, r0 % 512 // 16, (r1 - 1) % 512 // 16 + 1
+            nc.gpsimd.tensor_scalar(wp_bf[:, 2048 * g:2048 * (g + 1)].rearrange("p (t m e i) -> p m t e i", t=4, e=4, i=4)[:, m0:m1],
+                                    wp_stage[:, 4 * r0:4 * r1].rearrange("p (i m t e) -> p m t e i", i=4, t=4, e=4), 1.0, 0.0, ALU.mult, ALU.add)
         quantised["p"] = quantize(wp_bf, "wp")
-        gather("words", "p", 0, 256, WP_STAGE_AT + 12 * KB)
-        gather("scales", "p", 256, 768, WP_STAGE_AT + 13 * KB)
-        gather("words", "p", 256, 768, WP_STAGE_AT + 14 * KB)
+        gather("words", "r", 512, 512, WP_STAGE_AT + 12 * KB)
+        gather("scales", "p", 256, 768, WP_STAGE_AT + 14 * KB)
+        gather("words", "p", 256, 768, WP_STAGE_AT + 15 * KB)
 
         for c, g in ((0, 0), (0, 1)):
             rectify("l", c, g)
-        deal(nc.scalar.copy, wr_w[:].bitcast(U32), wr_raw[:].bitcast(U32), 4)
         deal_scales(nc.scalar.copy, wr_sc[:].bitcast(U32), wr_sc_raw[:].bitcast(U32))
-        for c, g in ((1, 0), (1, 1)):
-            rectify("l", c, g)
+        rectify("l", 1, 0)
+        deal(nc.scalar.copy, wr_w[:].bitcast(U32), wr_raw[:].bitcast(U32), 4)
+        rectify("l", 1, 1)
         for c, g in ((0, 0), (0, 1), (1, 0)):
             rectify("r", c, g)
             multiply_on_gpsimd(c, g)
@@ -262,41 +271,60 @@ def tile_list_syntax_node_latency_kernel(tc, tab_words, tab_scales, offs, offs2,
         multiply_on_vector(1, 1)
         for side, c, g in (("r", 2, 0), ("l", 2, 1), ("l", 3, 0), ("r", 3, 0), ("l", 3, 1)):
             rectify(side, c, g)
-        h_q = quantize_h(0)
         quantised["w2"] = quantize(w2_bf[:].rearrange("p g c -> p (g c)"), "w2", RELU_A_AT[1, 1], RELU_B_AT[1, 0])
-        sums = second_product(h_q, wide_banks("scalar"))
+        h_q = quantize_h(0)
 
-        for c in (1, 2):
-            multiply_on_gpsimd(c + 1, 0)
-            open_h(c * CW, CW)
-            for g in range(G):
-                for jt in range(2 * c, 2 * c + 2):
-                    add_on_vector(jt, g)
-            multiply_on_vector(c + 1, 1)
-            cast_y((c - 1) * CW, CW, finish_chunk(c - 1, sums), nc.scalar.copy)
-            if c == 1:
-                p_last = placed([P, JT, 4], F32, "p_last")
-                nc.scalar.copy(p_last[:], first_product("p", 7, 0, "scalar"))
-            sums = second_product(quantize_h(c * CW), wide_banks("scalar"))
+        multiply_on_gpsimd(2, 0)
+        open_h(CW, CW)
+        for g in range(G):
+            for jt in (2, 3):
+                add_on_vector(jt, g)
+        multiply_on_vector(2, 1)
+        sums = second_product(h_q, wide_banks("vector"))
+        cast_y(0, CW, finish_chunk(0, sums), nc.scalar.copy)
+        h_q = quantize_h(CW)
+
+        early, late = banks["scalar"][3::-3], banks["scalar"][1:3]
+        first, second = banks["vector"][3::-3], banks["vector"][1:3]
+        banks["vector"] = [late[1], first[0], first[1], late[0]]
+        turns["vector"] = []
+        multiply_on_gpsimd(3, 0)
+        open_h(2 * CW, CW)
+        for g in range(G):
+            for jt in (4, 5):
+                add_on_vector(jt, g)
+        multiply_on_vector(3, 1)
+        banks["spare"] = [second[1], second[0]]
+        turns["spare"] = []
+        p_last = placed([P, JT, 4], F32, "p_last")
+        last_parent = first_product("p", 7, 1, "spare")
+        nc.scalar.copy(p_last[:], first_product("p", 7, 0, "spare"))
+        sums = second_product(h_q, wide_banks("vector"))
+        cast_y(CW, CW, finish_chunk(1, sums), nc.scalar.copy)
+        h_q = quantize_h(2 * CW)
+        banks["early"] = early
+        turns["early"] = []
+        sums = second_product(h_q, wide_banks("early"))
 
         open_h(768, JT)
         open_h(896, JT)
         nc.gpsimd.tensor_tensor(h_part(7, 0), p_last[:], prod_part(7, 0), ALU.add)
-        for jt, g in ((6, 0), (6, 1), (7, 1)):
-            add_on_vector(jt, g)
+        for g in range(G):
+            add_on_vector(6, g)
+        nc.vector.tensor_tensor(h_part(7, 1), last_parent, prod_part(7, 1), ALU.add)
         y = finish_chunk(2, sums)
-        bank = next_bank("scalar")
+        bank = next_bank("vector")
         sums = second_product(quantize_h(768), [bank[:, t, :] for t in range(4)])
-        pairs = [next_bank("scalar"), next_bank("vector")]
+        pairs = [next_bank("vector"), next_bank("vector")]
         last_sums = second_product(quantize_h(896), [pairs[t // 2][:, t % 2, :] for t in range(4)])
-        cast_y(512, CW, y, nc.vector.tensor_copy)
         y_w = placed([P, 768], U32, "y_w_first", H_AT[896] - KB)
         planes(y_w, 0, 0, 512)
-        planes(y_w, 0, 512, 768)
+        cast_y(512, CW, y, nc.vector.tensor_copy)
         y = ring.tile([P, 4, 2 * JT], F32, name="y")
         add_bias_into(y[:, :, 0:JT], sums)
         add_bias_into(y[:, :, JT:2 * JT], last_sums, (2, 3))
         nc.sync.dma_start(y_rows[:, :, 768:S], y[:])
+        planes(y_w, 0, 512, 768)
         cast_y(768, JT, y[:, :, 0:JT], nc.scalar.copy)
         cast_y(896, JT, y[:, :, JT:2 * JT], nc.vector.tensor_copy)
         y_w = placed([P, 256], U32, "y_w_last")

@@ -26,7 +26,7 @@ KB = 1024
 WP_PIECES = ((0, 512), (512, 768), (768, 1024))
 WP_STAGE_AT = 0
 W2_BF_AT = 24 * KB
-RELU_A_AT = {(1, 1): 32 * KB, (2, 1): 60 * KB, (3, 1): 64 * KB}
+RELU_A_AT = {(1, 1): 70 * KB, (2, 1): 60 * KB, (3, 1): WP_STAGE_AT + 8 * KB}
 RELU_B_AT = {(1, 0): 36 * KB, (2, 0): 44 * KB, (3, 0): 48 * KB}
 H_AT = {0: W2_BF_AT - 4 * KB, 256: W2_BF_AT + 2 * KB, 512: 52 * KB, 896: 54 * KB}
 PROD_AT = {(0, 0): WP_STAGE_AT, (0, 1): WP_STAGE_AT + 4 * KB, (1, 0): WP_STAGE_AT + 8 * KB, (2, 0): W2_BF_AT - 2 * KB, (3, 0): H_AT[256]}
@@ -62,7 +62,7 @@ def tile_list_syntax_node_latency_kernel(tc, tab_words, tab_scales, offs, offs2,
         lists = {side: keep.tile([P, S // 16], U16, name="list_" + side) for side in "lrp"}
         tab_w = placed([P, T], I32, "tab_w")
         wl_raw = placed([P, H // 2], I32, "wl_raw")
-        wr_raw = placed([P, H], I32, "wr_raw", RELU_A_AT[1, 1])
+        wr_raw = placed([P, H], I32, "wr_raw")
         wp_stage = placed([P, 6144], F32, "wp_stage", WP_STAGE_AT)
         wp_bf = wp_stage[:, 4096:6144].bitcast(BF16)
         w2_raw = [placed([P, 4, N], F32, "w2_raw%d" % g) for g in range(G)]
@@ -79,9 +79,8 @@ def tile_list_syntax_node_latency_kernel(tc, tab_words, tab_scales, offs, offs2,
         load_scale_rows(wl_sc_raw[:], wl_scales[0])
         for piece, (r0, r1) in enumerate(WP_PIECES):
             if piece == 1:
-                load_scale_rows(wr_sc_raw[:], wr_scales[0])
-            if piece == 2:
                 nc.sync.dma_start(wr_raw[:], wr_words[0].rearrange("p n t -> p (n t)").bitcast(I32))
+                load_scale_rows(wr_sc_raw[:], wr_scales[0])
             nc.sync.dma_start(wp_stage[:, 4 * r0:4 * r1].rearrange("p (i r) -> p i r", i=4), wp_rows[:, :, r0:r1])
         nc.sync.dma_start(lists["p"][:], offs)
         for g in range(G):
@@ -151,12 +150,16 @@ def tile_list_syntax_node_latency_kernel(tc, tab_words, tab_scales, offs, offs2,
         prods = {}
         h_tiles = {}
 
-        def rectify(side, c, g, halves=(0, 1)):
-            if 0 in halves:
-                at = (RELU_A_AT if side == "l" else RELU_B_AT).get((c, g))
-                relus[side, c, g] = placed([P, CW, 4], F32, "relu_%s%d%d" % (side, c, g), at)
-            for i in halves:
-                nc.scalar.activation(relus[side, c, g][:, i * JT:(i + 1) * JT, :], first_product(side, 2 * c + i, g, "scalar"), ACT.Relu)
+        def rectify(side, c, g):
+            name = "relu_%s%d%d" % (side, c, g)
+            if side == "l" and (c, g) in RELU_A_AT:
+                parts = [placed([P, JT, 4], F32, name + "a", RELU_A_AT[c, g])[:], placed([P, JT, 4], F32, name + "b", RELU_A_AT[c, g] + 2 * KB)[:]]
+                relus[side, c, g] = parts
+            else:
+                relus[side, c, g] = placed([P, CW, 4], F32, name, RELU_B_AT.get((c, g)) if side == "r" else None)
+                parts = [relus[side, c, g][:, i * JT:(i + 1) * JT, :] for i in range(2)]
+            for i in range(2):
+                nc.scalar.activation(parts[i], first_product(side, 2 * c + i, g, "scalar"), ACT.Relu)
 
         def multiply_on_gpsimd(c, g):
             prods[c, g] = placed([P, CW, 4], F32, "prod%d%d" % (c, g), PROD_AT[c, g])
@@ -164,11 +167,11 @@ def tile_list_syntax_node_latency_kernel(tc, tab_words, tab_scales, offs, offs2,
 
         def multiply_on_vector(c, g, halves=(0, 1)):
             if 0 in halves:
-                prods[c, g] = placed([P, CW, 4], F32, "prod%d%d" % (c, g))
+                prods[c, g] = placed([P, CW, 4], F32, "prod%d%d" % (c, g), PROD_AT.get((c, g)))
             for i in halves:
                 part = slice(i * JT, (i + 1) * JT)
                 nc.vector.scalar_tensor_tensor(prods[c, g][:, part, :], first_product("r", 2 * c + i, g, "vector"), 0.0,
-                                               relus["l", c, g][:, part, :], ALU.max, ALU.mult)
+                                               relus["l", c, g][i], ALU.max, ALU.mult)
 
         def open_h(j0, width):
             h_tiles[j0] = placed([P, G, width, 4], BF16, "h_bf%d" % j0, H_AT.get(j0))
@@ -236,7 +239,7 @@ def tile_list_syntax_node_latency_kernel(tc, tab_words, tab_scales, offs, offs2,
         gather("scales", "r", 0, S)
         gather("words", "r", 0, 256, W2_BF_AT)
         gather("words", "r", 256, 256)
-        gather("scales", "p", 0, 256)
+        gather("scales", "p", 0, 512)
         gather("words", "p", 0, 256)
 
         deal(nc.gpsimd.tensor_copy, wl_w[:], wl_raw[:], 2)
@@ -247,14 +250,14 @@ def tile_list_syntax_node_latency_kernel(tc, tab_words, tab_scales, offs, offs2,
                                     wp_stage[:, 4 * r0:4 * r1].rearrange("p (i m t e) -> p m t e i", i=4, t=4, e=4), 1.0, 0.0, ALU.mult, ALU.add)
         quantised["p"] = quantize(wp_bf, "wp")
         gather("words", "r", 512, 512, WP_STAGE_AT + 12 * KB)
-        gather("scales", "p", 256, 768, WP_STAGE_AT + 14 * KB)
+        gather("scales", "p", 512, 512, WP_STAGE_AT + 14 * KB)
         gather("words", "p", 256, 768, WP_STAGE_AT + 15 * KB)
 
         for c, g in ((0, 0), (0, 1)):
             rectify("l", c, g)
+        deal(nc.scalar.copy, wr_w[:].bitcast(U32), wr_raw[:].bitcast(U32), 4)
         deal_scales(nc.scalar.copy, wr_sc[:].bitcast(U32), wr_sc_raw[:].bitcast(U32))
         rectify("l", 1, 0)
-        deal(nc.scalar.copy, wr_w[:].bitcast(U32), wr_raw[:].bitcast(U32), 4)
         rectify("l", 1, 1)
         for c, g in ((0, 0), (0, 1), (1, 0)):
             rectify("r", c, g)
@@ -271,7 +274,7 @@ def tile_list_syntax_node_latency_kernel(tc, tab_words, tab_scales, offs, offs2,
         multiply_on_vector(1, 1)
         for side, c, g in (("r", 2, 0), ("l", 2, 1), ("l", 3, 0), ("r", 3, 0), ("l", 3, 1)):
             rectify(side, c, g)
-        quantised["w2"] = quantize(w2_bf[:].rearrange("p g c -> p (g c)"), "w2", RELU_A_AT[1, 1], RELU_B_AT[1, 0])
+        quantised["w2"] = quantize(w2_bf[:].rearrange("p g c -> p (g c)"), "w2", RELU_A_AT[1, 1] - 2 * KB, RELU_B_AT[1, 0])
         h_q = quantize_h(0)
 
         multiply_on_gpsimd(2, 0)

@@ -28,10 +28,10 @@ WP_STAGE_AT = 0
 W2_BF_AT = 24 * KB
 RELU_A_AT = {(1, 1): 70 * KB, (2, 1): 60 * KB, (3, 1): WP_STAGE_AT + 8 * KB}
 RELU_B_AT = {(1, 0): 36 * KB, (2, 0): 44 * KB, (3, 0): 48 * KB}
-H_AT = {0: W2_BF_AT - 4 * KB, 256: W2_BF_AT + 2 * KB, 512: 52 * KB, 896: 54 * KB}
+H_AT = {0: W2_BF_AT - 4 * KB, 256: W2_BF_AT - 6 * KB, 512: 52 * KB, 896: 54 * KB}
 PROD_AT = {(0, 0): WP_STAGE_AT, (0, 1): WP_STAGE_AT + 4 * KB, (1, 0): WP_STAGE_AT + 8 * KB, (2, 0): W2_BF_AT - 2 * KB, (3, 0): H_AT[256]}
 H_CODES_AT = {0: RELU_B_AT[1, 0] + KB, 256: RELU_B_AT[2, 0], 512: RELU_B_AT[3, 0]}
-H_PLANE_AT = {256: RELU_A_AT[2, 1], 512: RELU_A_AT[3, 1]}
+H_PLANE_AT = {0: RELU_A_AT[1, 1] + KB, 256: RELU_A_AT[2, 1], 512: RELU_A_AT[3, 1]}
 
 
 def tile_list_syntax_node_latency_kernel(tc, tab_words, tab_scales, offs, offs2, offs3, wp, wl_words, wl_scales,
@@ -230,6 +230,8 @@ def tile_list_syntax_node_latency_kernel(tc, tab_words, tab_scales, offs, offs2,
 
         def planes(y_w, at, j0, j1):
             nc.vector.quantize_mx(out=y_w[:, j0 - at:j1 - at].bitcast(E4M3), scales=y_sc[:, j0:j1], in_=y_bf[:, 4 * j0:4 * j1])
+
+        def store_words(y_w, at, j0, j1):
             nc.sync.dma_start(y_words[:, j0:j1], y_w[:, j0 - at:j1 - at].bitcast(I32))
 
         gather("scales", "l", 0, 256)
@@ -239,7 +241,7 @@ def tile_list_syntax_node_latency_kernel(tc, tab_words, tab_scales, offs, offs2,
         gather("scales", "r", 0, S)
         gather("words", "r", 0, 256, W2_BF_AT)
         gather("words", "r", 256, 256)
-        gather("scales", "p", 0, 512)
+        gather("scales", "p", 0, 768)
         gather("words", "p", 0, 256)
 
         deal(nc.gpsimd.tensor_copy, wl_w[:], wl_raw[:], 2)
@@ -250,7 +252,7 @@ def tile_list_syntax_node_latency_kernel(tc, tab_words, tab_scales, offs, offs2,
                                     wp_stage[:, 4 * r0:4 * r1].rearrange("p (i m t e) -> p m t e i", i=4, t=4, e=4), 1.0, 0.0, ALU.mult, ALU.add)
         quantised["p"] = quantize(wp_bf, "wp")
         gather("words", "r", 512, 512, WP_STAGE_AT + 12 * KB)
-        gather("scales", "p", 512, 512, WP_STAGE_AT + 14 * KB)
+        gather("scales", "p", 768, 256, WP_STAGE_AT + 14 * KB)
         gather("words", "p", 256, 768, WP_STAGE_AT + 15 * KB)
 
         for c, g in ((0, 0), (0, 1)):
@@ -274,8 +276,8 @@ def tile_list_syntax_node_latency_kernel(tc, tab_words, tab_scales, offs, offs2,
         multiply_on_vector(1, 1)
         for side, c, g in (("r", 2, 0), ("l", 2, 1), ("l", 3, 0), ("r", 3, 0), ("l", 3, 1)):
             rectify(side, c, g)
-        quantised["w2"] = quantize(w2_bf[:].rearrange("p g c -> p (g c)"), "w2", RELU_A_AT[1, 1] - 2 * KB, RELU_B_AT[1, 0])
         h_q = quantize_h(0)
+        quantised["w2"] = quantize(w2_bf[:].rearrange("p g c -> p (g c)"), "w2", RELU_A_AT[1, 1] - 3 * KB, RELU_B_AT[1, 0])
 
         multiply_on_gpsimd(2, 0)
         open_h(CW, CW)
@@ -322,16 +324,20 @@ def tile_list_syntax_node_latency_kernel(tc, tab_words, tab_scales, offs, offs2,
         last_sums = second_product(quantize_h(896), [pairs[t // 2][:, t % 2, :] for t in range(4)])
         y_w = placed([P, 768], U32, "y_w_first", H_AT[896] - KB)
         planes(y_w, 0, 0, 512)
+        store_words(y_w, 0, 0, 512)
         cast_y(512, CW, y, nc.vector.tensor_copy)
         y = ring.tile([P, 4, 2 * JT], F32, name="y")
         add_bias_into(y[:, :, 0:JT], sums)
         add_bias_into(y[:, :, JT:2 * JT], last_sums, (2, 3))
         nc.sync.dma_start(y_rows[:, :, 768:S], y[:])
         planes(y_w, 0, 512, 768)
+        store_words(y_w, 0, 512, 768)
         cast_y(768, JT, y[:, :, 0:JT], nc.scalar.copy)
         cast_y(896, JT, y[:, :, JT:2 * JT], nc.vector.tensor_copy)
         y_w = placed([P, 256], U32, "y_w_last")
-        planes(y_w, 768, 768, S)
+        planes(y_w, 768, 768, 896)
+        planes(y_w, 768, 896, S)
+        store_words(y_w, 768, 768, S)
         for q in range(4):
             queue = nc.sync if q % 2 == 0 else nc.scalar
             queue.dma_start(out_2[0][4 * q:4 * q + 4, :].bitcast(I32), y_sc[32 * q:32 * q + 4, :].bitcast(I32))

from contextlib import ExitStack

import concourse.mybir as mybir

K, H, N, T, S = 512, 1024, 512, 2048, 1024
FLOPS = 2 * S * (3 * K * H + H * N)

F32 = mybir.dt.float32
BF16 = mybir.dt.bfloat16
I32 = mybir.dt.int32
U32 = mybir.dt.uint32
U16 = mybir.dt.uint16
U8 = mybir.dt.uint8
E4M3 = mybir.dt.float8_e4m3fn_x4
E2M1 = mybir.dt.float4_e2m1fn_x4
ALU = mybir.AluOpType
ACT = mybir.ActivationFunctionType

P = 128
G = H // 512
JT = 128
CW = 256
CHUNKS = S // CW
KB = 1024

WP_PIECES = ((0, 512), (512, 768), (768, 1024))
WP_STAGE_AT = 0
W2_BF_AT = 24 * KB
RELU_A_AT = {(1, 1): 70 * KB, (2, 1): 60 * KB, (3, 1): WP_STAGE_AT + 8 * KB}
RELU_B_AT = {(1, 0): 36 * KB, (2, 0): 44 * KB, (3, 0): 48 * KB}
H_AT = {0: W2_BF_AT - 4 * KB, 256: W2_BF_AT - 6 * KB, 512: 52 * KB, 896: 54 * KB}
PROD_AT = {(0, 0): WP_STAGE_AT, (0, 1): WP_STAGE_AT + 4 * KB, (1, 0): WP_STAGE_AT + 8 * KB, (2, 0): W2_BF_AT - 2 * KB, (3, 0): H_AT[256]}
H_CODES_AT = {0: RELU_B_AT[1, 0] + KB, 256: RELU_B_AT[2, 0], 512: RELU_B_AT[3, 0]}
H_PLANE_AT = {0: RELU_A_AT[1, 1] + KB, 256: RELU_A_AT[2, 1], 512: RELU_A_AT[3, 1]}


def tile_list_syntax_node_latency_kernel(tc, tab_words, tab_scales, offs, offs2, offs3, wp, wl_words, wl_scales,
                                                   wr_words, wr_scales, w2, b2, out_0, out_1, out_2):
    nc = tc.nc
    with ExitStack() as ctx:
        keep = ctx.enter_context(tc.tile_pool(name="keep", bufs=1))
        shared = ctx.enter_context(tc.tile_pool(name="shared", bufs=1))
        ring = ctx.enter_context(tc.tile_pool(name="ring", bufs=3))
        psum = ctx.enter_context(tc.psum_pool(name="psum", bufs=1))

        def placed(shape, dtype, name, at=None):
            if at is None:
                return keep.tile(shape, dtype, name=name, align_bytes=64)
            return shared.tile(shape, dtype, name=name, align_bytes=64, offset=at)

        tab_sc = placed([P, T], U8, "tab_sc")
        wl_sc_raw = placed([P, H // 4], I32, "wl_sc_raw")
        wr_sc_raw = placed([P, H // 4], I32, "wr_sc_raw")
        nc.gpsimd.memset(tab_sc[:].bitcast(I32), 0)
        nc.gpsimd.memset(wl_sc_raw[:], 0)
        nc.gpsimd.memset(wr_sc_raw[:], 0)

        def load_scale_rows(plane, rows):
            for q in range(4):
                nc.sync.dma_start(plane[32 * q:32 * q + 4, :], rows[4 * q:4 * q + 4, :].bitcast(I32))

        lists = {side: keep.tile([P, S // 16], U16, name="list_" + side) for side in "lrp"}
        tab_w = placed([P, T], I32, "tab_w")
        wl_raw = placed([P, H // 2], I32, "wl_raw")
        wr_raw = placed([P, H], I32, "wr_raw")
        wp_stage = placed([P, 6144], F32, "wp_stage", WP_STAGE_AT)
        wp_bf = wp_stage[:, 4096:6144].bitcast(BF16)
        w2_raw = [placed([P, 4, N], F32, "w2_raw%d" % g) for g in range(G)]
        bias = placed([P, 4], F32, "bias")
        wp_rows = wp.rearrange("(p i) r -> p i r", i=4)
        w2_rows = w2.rearrange("(g m t e) n -> g t m (e n)", g=G, t=4, e=4)

        nc.sync.dma_start(lists["l"][:], offs2)
        nc.sync.dma_start(wl_raw[:], wl_words[0].bitcast(I32))
        nc.sync.dma_start(bias[:], b2.rearrange("(p t) -> p t", t=4))
        load_scale_rows(tab_sc[:].bitcast(I32), tab_scales[0])
        nc.sync.dma_start(tab_w[:], tab_words[0].rearrange("p n t -> p (n t)").bitcast(I32))
        nc.sync.dma_start(lists["r"][:], offs3)
        load_scale_rows(wl_sc_raw[:], wl_scales[0])
        for piece, (r0, r1) in enumerate(WP_PIECES):
            if piece == 1:
                nc.sync.dma_start(wr_raw[:], wr_words[0].rearrange("p n t -> p (n t)").bitcast(I32))
                load_scale_rows(wr_sc_raw[:], wr_scales[0])
            nc.sync.dma_start(wp_stage[:, 4 * r0:4 * r1].rearrange("p (i r) -> p i r", i=4), wp_rows[:, :, r0:r1])
        nc.sync.dma_start(lists["p"][:], offs)
        for g in range(G):
            for t in range(4):
                nc.sync.dma_start(w2_raw[g][:, t, :], w2_rows[g, t])

        got = {(kind, side): [] for kind in ("words", "scales") for side in "lrp"}

        def gather(kind, side, j0, width, at=None):
            dtype = U32 if kind == "words" else U8
            window = tab_w[:].bitcast(U32) if kind == "words" else tab_sc[:]
            piece = placed([P, width], dtype, "got_%s_%s%d" % (kind, side, j0), at)
            nc.vector.tensor_copy(piece[:], window.indirect(lists[side][:, j0 // 16:(j0 + width) // 16]))
            got[kind, side].append((j0, width, piece))

        def picked(kind, side, j):
            j0, width, piece = [one for one in got[kind, side] if one[0] <= j < one[0] + one[1]][0]
            return piece[:, j - j0:j - j0 + JT]

        def deal(copy, dealt, raw, run):
            copy(dealt.rearrange("p (g t m e) -> p g t m e", g=G, t=4, e=run),
                 raw.rearrange("p (g m t e) -> p g t m e", g=G, t=4, e=run))

        def deal_scales(copy, dealt, raw):
            copy(dealt.rearrange("p (g t c i) -> p g c t i", g=G, t=4, i=4),
                 raw.rearrange("p (g c i t) -> p g c t i", g=G, t=4, i=4))

        def quantize(grouped, name, codes_at=None, plane_at=None):
            width = grouped.shape[1] // 4
            codes = placed([P, width], U32, name + "_codes", codes_at)
            plane = placed([P, width], U8, name + "_plane", plane_at)
            nc.vector.quantize_mx(out=codes[:].bitcast(E4M3), scales=plane[:], in_=grouped)
            return codes, plane

        banks = {reader: [psum.tile([P, 4, JT], F32, name="bank_%s%d" % (reader, b)) for b in range(count)]
                 for reader, count in (("vector", 4), ("scalar", 4))}
        turns = {reader: [] for reader in banks}

        def next_bank(reader):
            turns[reader].append(reader)
            return banks[reader][len(turns[reader]) % len(banks[reader])]

        wl_w = placed([P, H // 2], I32, "wl_w")
        wl_sc = placed([P, H], U8, "wl_sc")
        wr_w = placed([P, H], I32, "wr_w")
        wr_sc = placed([P, H], U8, "wr_sc")
        quantised = {}

        def stationary(side, c):
            if side == "l":
                return wl_w[:, c // 2:(c + P) // 2].bitcast(U8).bitcast(E2M1), wl_sc[:, c:c + P]
            if side == "r":
                return wr_w[:, c:c + P].bitcast(E4M3), wr_sc[:, c:c + P]
            codes, plane = quantised[side]
            return codes[:, c:c + P].bitcast(E4M3), plane[:, c:c + P]

        def first_product(side, jt, g, reader):
            bank = next_bank(reader)
            for t in range(4):
                w_codes, w_plane = stationary(side, 512 * g + P * t)
                nc.tensor.matmul_mx(out=bank[:, t, :], lhsT=w_codes, lhsT_scale=w_plane,
                                    rhs=picked("words", side, jt * JT).bitcast(E4M3), rhs_scale=picked("scales", side, jt * JT),
                                    start=True, stop=True)
            return bank[:].rearrange("p t j -> p j t")

        relus = {}
        prods = {}
        h_tiles = {}

        def rectify(side, c, g):
            name = "relu_%s%d%d" % (side, c, g)
            if side == "l" and (c, g) in RELU_A_AT:
                parts = [placed([P, JT, 4], F32, name + "a", RELU_A_AT[c, g])[:], placed([P, JT, 4], F32, name + "b", RELU_A_AT[c, g] + 2 * KB)[:]]
                relus[side, c, g] = parts
            else:
                relus[side, c, g] = placed([P, CW, 4], F32, name, RELU_B_AT.get((c, g)) if side == "r" else None)
                parts = [relus[side, c, g][:, i * JT:(i + 1) * JT, :] for i in range(2)]
            for i in range(2):
                nc.scalar.activation(parts[i], first_product(side, 2 * c + i, g, "scalar"), ACT.Relu)

        def multiply_on_gpsimd(c, g):
            prods[c, g] = placed([P, CW, 4], F32, "prod%d%d" % (c, g), PROD_AT[c, g])
            nc.gpsimd.tensor_tensor(prods[c, g][:], relus["l", c, g][:], relus["r", c, g][:], ALU.mult)

        def multiply_on_vector(c, g, halves=(0, 1)):
            if 0 in halves:
                prods[c, g] = placed([P, CW, 4], F32, "prod%d%d" % (c, g), PROD_AT.get((c, g)))
            for i in halves:
                part = slice(i * JT, (i + 1) * JT)
                nc.vector.scalar_tensor_tensor(prods[c, g][:, part, :], first_product("r", 2 * c + i, g, "vector"), 0.0,
                                               relus["l", c, g][i], ALU.max, ALU.mult)

        def open_h(j0, width):
            h_tiles[j0] = placed([P, G, width, 4], BF16, "h_bf%d" % j0, H_AT.get(j0))

        def h_part(jt, g):
            j0 = max(j for j in h_tiles if j <= jt * JT)
            return h_tiles[j0][:, g, jt * JT - j0:(jt + 1) * JT - j0, :]

        def prod_part(jt, g):
            return prods[jt // 2, g][:, jt % 2 * JT:(jt % 2 + 1) * JT, :]

        def add_on_vector(jt, g, parent=None):
            if parent is None:
                parent = first_product("p", jt, g, "vector")
            nc.vector.tensor_tensor(h_part(jt, g), parent, prod_part(jt, g), ALU.add)

        def quantize_h(j0):
            return quantize(h_tiles[j0][:].rearrange("p g j t -> p (g j t)"), "h%d" % j0, H_CODES_AT.get(j0), H_PLANE_AT.get(j0))

        def second_product(h_q, sums):
            h_codes, h_plane = h_q
            width = h_codes.shape[1] // G
            for t in range(4):
                for g in range(G):
                    w_codes, w_plane = stationary("w2", 512 * g + P * t)
                    nc.tensor.matmul_mx(out=sums[t], lhsT=w_codes, lhsT_scale=w_plane,
                                        rhs=h_codes[:, g * width:(g + 1) * width].bitcast(E4M3),
                                        rhs_scale=h_plane[:, g * width:(g + 1) * width], start=(g == 0), stop=(g == G - 1))
            return sums

        def wide_banks(reader):
            pairs = [next_bank(reader)[:].rearrange("p (a b) j -> p a (b j)", a=2) for pair in range(2)]
            return [pairs[t // 2][:, t % 2, :] for t in range(4)]

        y_sc = placed([P, S], U8, "y_sc")
        y_bf = placed([P, 4 * S], BF16, "y_bf")
        y_rows = out_0.rearrange("(p t) j -> p t j", t=4)
        y_words = out_1[0].rearrange("p m t -> p (m t)").bitcast(I32)

        def add_bias_into(y, sums, on_vector=()):
            for t in range(4):
                if t in on_vector:
                    nc.vector.tensor_scalar(y[:, t, :], sums[t], bias[:, t:t + 1], None, ALU.add)
                else:
                    nc.scalar.activation(y[:, t, :], sums[t], ACT.Identity, bias=bias[:, t:t + 1])

        def cast_y(j0, width, y, copy):
            copy(y_bf[:, 4 * j0:4 * (j0 + width)].rearrange("p (c i t) -> p c t i", i=4, t=4),
                 y.rearrange("p t (c i) -> p c t i", i=4))

        def finish_chunk(c, sums):
            y = ring.tile([P, 4, CW], F32, name="y")
            add_bias_into(y[:], sums)
            nc.sync.dma_start(y_rows[:, :, c * CW:(c + 1) * CW], y[:])
            return y[:]

        def planes(y_w, at, j0, j1):
            nc.vector.quantize_mx(out=y_w[:, j0 - at:j1 - at].bitcast(E4M3), scales=y_sc[:, j0:j1], in_=y_bf[:, 4 * j0:4 * j1])

        def store_words(y_w, at, j0, j1):
            nc.sync.dma_start(y_words[:, j0:j1], y_w[:, j0 - at:j1 - at].bitcast(I32))

        gather("scales", "l", 0, 256)
        gather("scales", "l", 256, 768)
        gather("words", "l", 0, 256)
        gather("words", "l", 256, 768)
        gather("scales", "r", 0, S)
        gather("words", "r", 0, 256, W2_BF_AT)
        gather("words", "r", 256, 256)
        gather("scales", "p", 0, 768)
        gather("words", "p", 0, 256)

        deal(nc.gpsimd.tensor_copy, wl_w[:], wl_raw[:], 2)
        deal_scales(nc.gpsimd.tensor_copy, wl_sc[:].bitcast(I32), wl_sc_raw[:])
        for r0, r1 in WP_PIECES:
            g, m0, m1 = r0 // 512, r0 % 512 // 16, (r1 - 1) % 512 // 16 + 1
            nc.gpsimd.tensor_scalar(wp_bf[:, 2048 * g:2048 * (g + 1)].rearrange("p (t m e i) -> p m t e i", t=4, e=4, i=4)[:, m0:m1],
                                    wp_stage[:, 4 * r0:4 * r1].rearrange("p (i m t e) -> p m t e i", i=4, t=4, e=4), 1.0, 0.0, ALU.mult, ALU.add)
        quantised["p"] = quantize(wp_bf, "wp")
        gather("words", "r", 512, 512, WP_STAGE_AT + 12 * KB)
        gather("scales", "p", 768, 256, WP_STAGE_AT + 14 * KB)
        gather("words", "p", 256, 768, WP_STAGE_AT + 15 * KB)

        for c, g in ((0, 0), (0, 1)):
            rectify("l", c, g)
        deal(nc.scalar.copy, wr_w[:].bitcast(U32), wr_raw[:].bitcast(U32), 4)
        deal_scales(nc.scalar.copy, wr_sc[:].bitcast(U32), wr_sc_raw[:].bitcast(U32))
        rectify("l", 1, 0)
        rectify("l", 1, 1)
        for c, g in ((0, 0), (0, 1), (1, 0)):
            rectify("r", c, g)
            multiply_on_gpsimd(c, g)
        rectify("l", 2, 0)
        w2_bf = placed([P, G, 2048], BF16, "w2_bf", W2_BF_AT)
        for g in range(G):
            nc.scalar.copy(w2_bf[:, g, :].rearrange("p (u c t) -> p c t u", u=4, t=4), w2_raw[g][:].rearrange("p t (c u) -> p c t u", u=4))

        open_h(0, CW)
        for g in range(G):
            for jt in range(2):
                add_on_vector(jt, g)
        multiply_on_vector(1, 1)
        for side, c, g in (("r", 2, 0), ("l", 2, 1), ("l", 3, 0), ("r", 3, 0), ("l", 3, 1)):
            rectify(side, c, g)
        h_q = quantize_h(0)
        quantised["w2"] = quantize(w2_bf[:].rearrange("p g c -> p (g c)"), "w2", RELU_A_AT[1, 1] - 3 * KB, RELU_B_AT[1, 0])

        multiply_on_gpsimd(2, 0)
        open_h(CW, CW)
        for g in range(G):
            for jt in (2, 3):
                add_on_vector(jt, g)
        multiply_on_vector(2, 1)
        sums = second_product(h_q, wide_banks("vector"))
        cast_y(0, CW, finish_chunk(0, sums), nc.scalar.copy)
        h_q = quantize_h(CW)

        early, late = banks["scalar"][3::-3], banks["scalar"][1:3]
        first, second = banks["vector"][3::-3], banks["vector"][1:3]
        banks["vector"] = [late[1], first[0], first[1], late[0]]
        turns["vector"] = []
        multiply_on_gpsimd(3, 0)
        open_h(2 * CW, CW)
        for g in range(G):
            for jt in (4, 5):
                add_on_vector(jt, g)
        multiply_on_vector(3, 1)
        banks["spare"] = [second[1], second[0]]
        turns["spare"] = []
        p_last = placed([P, JT, 4], F32, "p_last")
        last_parent = first_product("p", 7, 1, "spare")
        nc.scalar.copy(p_last[:], first_product("p", 7, 0, "spare"))
        sums = second_product(h_q, wide_banks("vector"))
        cast_y(CW, CW, finish_chunk(1, sums), nc.scalar.copy)
        h_q = quantize_h(2 * CW)
        banks["early"] = early
        turns["early"] = []
        sums = second_product(h_q, wide_banks("early"))

        open_h(768, JT)
        open_h(896, JT)
        nc.gpsimd.tensor_tensor(h_part(7, 0), p_last[:], prod_part(7, 0), ALU.add)
        for g in range(G):
            add_on_vector(6, g)
        nc.vector.tensor_tensor(h_part(7, 1), last_parent, prod_part(7, 1), ALU.add)
        y = finish_chunk(2, sums)
        bank = next_bank("vector")
        sums = second_product(quantize_h(768), [bank[:, t, :] for t in range(4)])
        pairs = [next_bank("vector"), next_bank("vector")]
        last_sums = second_product(quantize_h(896), [pairs[t // 2][:, t % 2, :] for t in range(4)])
        y_w = placed([P, 768], U32, "y_w_first", H_AT[896] - KB)
        planes(y_w, 0, 0, 512)
        store_words(y_w, 0, 0, 512)
        cast_y(512, CW, y, nc.vector.tensor_copy)
        y = ring.tile([P, 4, 2 * JT], F32, name="y")
        add_bias_into(y[:, :, 0:JT], sums)
        add_bias_into(y[:, :, JT:2 * JT], last_sums, (2, 3))
        nc.sync.dma_start(y_rows[:, :, 768:S], y[:])
        planes(y_w, 0, 512, 768)
        store_words(y_w, 0, 512, 768)
        cast_y(768, JT, y[:, :, 0:JT], nc.scalar.copy)
        cast_y(896, JT, y[:, :, JT:2 * JT], nc.vector.tensor_copy)
        y_w = placed([P, 256], U32, "y_w_last")
        planes(y_w, 768, 768, 896)
        planes(y_w, 768, 896, S)
        store_words(y_w, 768, 768, S)
        for q in range(4):
            queue = nc.sync if q % 2 == 0 else nc.scalar
            queue.dma_start(out_2[0][4 * q:4 * q + 4, :].bitcast(I32), y_sc[32 * q:32 * q + 4, :].bitcast(I32))
